import numpy as np, ml_dtypes
CORES = [13,21,141,149]
N = 4
BF = ml_dtypes.bfloat16
V, H, M, CAP, R = 1280, 80, 2, 32, 4
L = M * H
def lanes(t, r):
    c = (M * (N * t + r) + np.arange(M)) & 15
    return (16 * np.arange(H)[None, :] + c[:, None]).reshape(-1)
def pack(b, x, lm):
    return {"nb": np.ascontiguousarray(b.reshape(N, 128, V)).astype(np.float32), "xs": np.ascontiguousarray(x.reshape(N, 128, V)).astype(np.float32).astype(BF),
            "lim": np.ascontiguousarray(lm.reshape(N, 128, 1)).astype(np.int32)}
def parts(rng):
    dens = rng.choice(np.array([0.08, 0.25, 0.5, 0.8]), (N, 8, 1, V)); u = rng.random((N, 8, 16, V))
    h = np.minimum((V * u * u).astype(np.int64), V - 1)
    pool = rng.integers(V // 4, V, (8, 12)); known = pool[np.arange(8)[None, :, None, None], rng.integers(0, 12, (N, 8, 16, V))]
    h = np.where(rng.random((N, 8, 16, V)) < 0.35, known, h)
    b = np.where(rng.random((N, 8, 16, V)) < dens, h, V)
    top = np.where(rng.random((N, 8, 1, V)) < 0.02, 256, rng.choice(np.array([4, 16, 40, 64]), (N, 8, 1, V)))
    x = (top * rng.random((N, 8, 16, V))).astype(np.int64)
    lm = rng.permutation(np.array([6, 16, 28, 45, 70, 110, 180, 300]))[None, :, None] + rng.integers(0, 8, (N, 8, 16))
    return b, x, lm
def late(rng, b, x, lm, g):
    E = np.stack([np.append(rng.permutation(lanes(0, r)[:-1]), lanes(0, r)[-1])[-26:] for r in range(N)])
    C = np.stack([np.append(rng.permutation(lanes(1, r)[:-1]), lanes(1, r)[-1])[-14:] for r in range(N)])
    D = np.stack([rng.permutation(np.setdiff1d(lanes(2, r), E[r]))[:4] for r in range(N)])
    low = E[:, :12]; own = E[:, 12:18]; top = E[:, 18:]; lows = low.reshape(-1)
    pool = np.setdiff1d(np.arange(V), np.concatenate([E.reshape(-1), C.reshape(-1), D.reshape(-1)]))
    b[:, g] = rng.choice(pool, (N, 16, V)); x[:, g] = rng.integers(128, 256, (N, 16, V)); lm[:, g] = rng.integers(600, 1600, (N, 16))
    for r in range(N):
        b[r, g][:, E[r]] = V; b[r, g][:, C[r, :3]] = V
    for r in range(N):
        z = rng.permutation(pool)[:12]; x[r, g][:, z] = 255; x[r, g][rng.integers(0, 16, 12), z] = 254
        b[r, g][rng.integers(0, 16, 12), low[r]] = z
        p = rng.integers(0, 16, 8); b[r, g][p, top[r]] = rng.choice(pool, 8); b[r, g][(p + rng.integers(1, 16, 8)) & 15, top[r]] = rng.choice(pool, 8)
        q = (r + 1) % N; s = C[r, :6]; k = rng.integers(0, 16, 6); j = (k + rng.integers(1, 16, 6)) & 15
        b[q, g][k, own[q]] = s; b[r, g][k, s] = s; b[r, g][j, s] = own[q]
        for i in range(8):
            n = rng.permutation(lows)[:16]; n[12 + (i & 3)] = top[q, i] if i < 4 else top[0, i]
            b[r, g][:, C[r, 6 + i]] = n
        if r < N - 1:
            for i in range(4):
                n = rng.permutation(lows)[:16]; n[int(rng.integers(0, 16))] = top[0, 4 + i]
                b[r, g][:, D[r, i]] = n
def setup_inputs(rng):
    return pack(*parts(rng))
def setup_inputs_spread(rng):
    d = rng.random((N, 8, 1, V))
    b = np.where(rng.random((N, 8, 16, V)) < d * d * d, rng.integers(0, V, (N, 8, 16, V)), V)
    x = np.minimum((np.exp2(8 * rng.random((N, 8, 1, V))) * rng.random((N, 8, 16, V))).astype(np.int64), 255)
    lm = np.minimum((np.exp2(3 + 9 * rng.random((N, 8, 1))) * (0.5 + 0.5 * rng.random((N, 8, 16)))).astype(np.int64), 4079)
    return pack(b, x, lm)
def setup_inputs_ends(rng):
    x = 255 * np.where(rng.random((N, 8, 1, V)) < 0.5, rng.integers(0, 2, (N, 8, 1, V)), rng.integers(0, 2, (N, 8, 16, V)))
    x[:, 1::2, :, :16] = 255; x[:, 1::2, :, V - 1] = 255
    mode = rng.choice(np.array([0, 0, 1, 2, 2, 2, 3, 4]), (N, 8, 1, V)); coin = rng.integers(0, 2, (N, 8, 16, V))
    v = np.arange(V)[None, :]; p = np.arange(16)[:, None]
    b = np.where(mode == 0, 0, np.where(mode == 1, V, np.where(mode == 2, coin * V, np.where(mode == 3, np.where(coin == 1, p, V - 1), rng.integers(0, V + 1, (N, 8, 16, V))))))
    b[:, 0:6:2, :, 0:16:2] = V
    b[:, 3:6:2, :, 0:16] = V; b[:, 3:6:2, 5, 0:16] = 0
    b[N - 1, 7] = np.where((v >= V - 192) & (p == ((v >> 4) & 15)), V, 0)
    big = np.array([9, 16, 8, 16, 0, 9, 12, 16])[None, :, None]
    lm = np.where(np.argsort(rng.random((N, 8, 16)), axis=2) < big, 4079, 0)
    return pack(b, x, lm)
def setup_inputs_corners(rng):
    x = rng.integers(16, 32, (N, 8, 16, V)); x[..., V - 80:V - 16] = 255; x[..., V - 16:] = 0
    pos = np.argsort(rng.random((N, 8, 16, V)), axis=2)
    many = np.where((rng.random((N, 8, 16, V)) < 0.4) | (pos < 4), rng.integers(0, V - 16, (N, 8, 16, V)), V)
    one = np.where(pos == 0, rng.integers(0, V - 80, (N, 8, 16, V)), V)
    kind = rng.choice(np.array([0, 1, 2, 2]), (N, 8, 1, V)); counts = (CAP, CAP + 1, L, CAP - 1, 1, 0, CAP, 2)
    for q in range(N):
        v = lanes(0, q)
        for g in range(8):
            n = counts[(g + 3 * q) % 8]; o = rng.permutation(L)
            kind[q, g, 0, v[o[:n]]] = 0 if g % 4 == 2 else rng.integers(0, 2, n)
            kind[q, g, 0, v[o[n:]]] = rng.integers(1, 3, L - n) if g % 4 == 2 else 2
    b = np.where(kind == 0, V, np.where(kind == 1, one, many))
    lm = 40 + rng.integers(0, 8, (N, 8, 16)); o = np.argsort(rng.random((N, 8, 16)), axis=2)
    lm[:, 1::2] = np.where(o[:, 1::2] < 9, lm[:, 1::2], 0); lm[:, 2::4] = np.where(o[:, 2::4] < 8, lm[:, 2::4], 0)
    return pack(b, x, lm)
def setup_inputs_crowd(rng):
    b, x, lm = parts(rng)
    b[:, :4] = np.where(rng.random((N, 4, 16, V)) < 0.1, rng.integers(V - 128, V, (N, 4, 16, V)), V); b[:, :4, 0, :] = 0
    v = np.arange(V)
    for t in range(16 // (N * M)):
        c = (M * (N * t + N - 1)) & 15
        b[:, 1:4:2, 0, np.flatnonzero(((v & 15) == c) & ((v >> 4) % CAP == CAP - 1))] = V
    lm[:, :4] = 4079; x[:, :2] = 255
    b[:, 4:] = np.where(b[:, 4:] < V, rng.choice(np.array([0, 1, 18, 40, V - 1]), (N, 4, 16, V)), V); b[:, 4:, :, :48] = V
    return pack(b, x, lm)
def setup_inputs_alike(rng):
    b, x, lm = parts(rng)
    u = rng.random((N, 8, 3, V)); few = np.minimum((V * u * u).astype(np.int64), V - 1)
    few[:, :, 0] = np.where(rng.random((N, 8, V)) < 0.15, np.arange(V), few[:, :, 0])
    pool = rng.integers(V // 2, V, (8, 4)); few[:, :, 2] = pool[np.arange(8)[None, :, None], rng.integers(0, 4, (N, 8, V))]
    which = np.minimum(rng.integers(0, 3, (N, 8, 16, V)), rng.integers(0, 3, (N, 8, 1, V)))
    b = np.where(rng.random((N, 8, 16, V)) < rng.choice(np.array([0.4, 0.8, 1.0]), (N, 8, 1, V)), np.take_along_axis(few, which, 2), V)
    lm = np.minimum(4 * lm, 4079)
    late(rng, b, x, lm, int(rng.integers(0, 8)))
    return pack(b, x, lm)
def check_inputs(d):
    bad = []
    for k, lo, hi in (("nb", 0, V), ("xs", 0, 255), ("lim", 0, 4079)):
        a = np.asarray(d[k]).astype(np.float64)
        if not np.all((a >= lo) & (a <= hi)): bad.append("range of " + k)
        elif not np.all(a == np.floor(a)): bad.append("whole numbers in " + k)
    return bad
def reference(nb, xs, lim):
    b = nb.astype(np.int32).reshape(N, 8, 16, V); x = xs.astype(np.float32).astype(np.int32).reshape(N, 8, 16, V)
    lm = lim.astype(np.int64).reshape(N, 8, 16, 1)
    J = np.tile(np.arange(V), (8, 1)); gone = np.zeros((8, V), bool)
    A = [0] * N; g8 = np.arange(8)[:, None, None]
    for t in range(R):
        new = []
        for r in range(N):
            v = lanes(t, r); q = b[r][:, :, v]
            has = q < V; u = np.where(has, q, 0)
            n = J[g8, u]; elem = has & gone[g8, u]; var = has & ~elem
            at = n.reshape(8, 1, 16 * L)
            Q = np.take_along_axis(b[r], at, 2).reshape(8, 16, 16, L); X = np.take_along_axis(x[r], at, 2).reshape(8, 16, 16, L)
            ek = elem[:, None]
            cov = var & np.any((Q == q[:, :, None, :]) & ek, axis=2)
            unc = var & ~cov
            deg = np.sum(np.where(unc[:, None], X, 0), axis=2) + np.max(np.where(ek, X, 0), axis=2)
            live = ~gone[:, v]
            hit = live & (np.sum(deg <= lm[r] + (A[r] & 7), axis=1) >= 9)
            piv = hit & (np.add.accumulate(hit.astype(np.int64), axis=1) <= CAP)
            col = np.minimum(np.where(unc & (q != v), q, V), np.min(np.where(ek & (Q != v), Q, V), axis=2))
            S = np.where(elem, np.sum(X, axis=1), -1); k = np.argmax(S, axis=1)
            e = np.take_along_axis(n, k[:, None, :], 1)[:, 0, :]
            b[r][:, :, v] = np.where(cov & (live & ~piv)[:, None, :], V, q)
            new.append((v, piv, col, np.minimum(deg, 255), e, piv & np.any(elem, axis=1)))
        for g in range(8):
            es = []; vs = []
            for v, piv, col, sz, e, cl in new:
                w = np.flatnonzero(piv[g]); b[:, g][:, :, v[w]] = col[g][:, w]; x[:, g][:, :, v[w]] = sz[g][:, w]; gone[g, v[w]] = True
                w = np.flatnonzero(cl[g]); es.append(e[g][w]); vs.append(v[w])
            ue, ui = np.unique(np.concatenate(es), return_index=True)
            J[g, ue] = np.concatenate(vs)[ui]
            J[g] = J[g][J[g]]
        A = [int(np.sum(a[1])) for a in new]
    return {"yn": b.reshape(N, 128, V).astype(np.float32), "yx": x.reshape(N, 128, V).astype(np.float32).astype(BF), "yj": np.stack([J] * N).astype(np.float32)}

@@ -1,0 +1,686 @@
+from concourse.bass import DstId, RemoteDMATransfer
+from concourse.mybir import AluOpType as Op, ActivationFunctionType as Fn
+
+V, H, CAP, ROUNDS = 1280, 80, 32, 4
+N = 4
+L = 2 * H
+LX = L + CAP
+VT = 1792
+G0 = 1288
+BL = 36
+IDW = 640
+SHIFT = 512 * 32618
+FP, BF, I32, U16 = "float32", "bfloat16", "int32", "uint16"
+CH0 = [(0, 64), (64, 160)]
+CH = [(0, 64), (64, 128), (128, 160)]
+
+_S = {
+    "nm": (VT, FP), "en": (VT, FP), "rs": (VT, FP), "vn": (G0, FP), "jt": (VT, FP), "xm": (VT, BF), "xo": (VT, BF),
+    "la": (576, FP), "ln": (576, FP), "ksl": (576, FP), "ksn": (128, FP), "w": (IDW, FP), "vid": (IDW, FP), "vb": (128, FP),
+    "idc": (512, FP), "jwa": (32, U16), "jwb": (32, U16), "jwc": (32, U16), "evu": (32, U16), "vc": (64, U16), "cwu": (32, U16),
+    "jwf": (32, FP),
+    "qf0": (LX, FP), "qf1": (LX, FP), "qu0": (L, U16), "qu1": (L, U16), "qr0": (16 * L, FP), "qr1": (16 * L, FP),
+    "lv0": (LX, FP), "lv1": (LX, FP), "ns0": (LX, FP), "ns1": (LX, FP), "dead0": (L, BF), "dead1": (L, BF),
+    "xg": (16 * L, BF), "eq": (16 * L, BF), "xv": (16 * L, BF), "msc": (16 * L, BF), "lmx": (L, FP), "deg": (LX, FP),
+    "ocx": (LX, FP), "e1": (LX, FP), "esg": (L, FP), "q2": (L, FP), "q3": (L, FP), "qn": (L, U16), "ok": (L, BF), "hit": (LX, BF),
+    "cum": (LX, BF), "c255": (LX, BF), "sg": (2 * LX, BF), "pla": (2, FP), "plw": (2, U16), "vx": (2, FP), "vy": (2, FP),
+    "piv": (L, BF),
+    "qp": (32, U16), "vp": (32, U16), "e1p": (32, FP), "ocp": (32, FP), "ocq": (32, FP),
+    "xn": (512, FP), "vr": (512, FP), "cc": (512, FP), "nsc": (512, FP), "key": (512, FP), "ksc": (512, FP),
+    "mi": (32, I32), "mj": (32, I32), "kd": (32, FP),
+    "kw": (32, FP), "ke": (64, FP), "kf": (64, FP), "kg": (64, FP), "jd": (256, FP), "js": (256, FP), "jr": (256, FP), "xr": (256, FP),
+    "er": (256, FP), "jf": (384, FP), "xt": (128, BF), "nt": (128, FP), "a1": (1, BF), "ai": (1, I32), "aj": (1, I32),
+    "limi": (1, I32), "limf": (1, FP), "lima": (1, FP), "limb": (1, FP), "kon": (16, FP),
+    "one": (128, BF), "idn": (128, BF), "i1280": (128, BF), "idead": (128, BF), "ipen": (128, BF), "bd": (128, BF), "bd8": (128, BF),
+    "dk": (2048, BF), "o16": (128, BF), "pii": (1, I32), "pij": (2, I32), "sh": (2, FP), "sc": (2, FP),
+    "dmp": (2, FP), "col": (512, I32), "cki": (512, I32), "gi": (128, I32), "dg": (256, FP), "seg": (1024, BF),
+    "c32": (64, I32), "seg32": (64, BF), "kb": (512, FP), "kp": (512, FP), "tri": (64, FP), "lrep": (L, U16),
+}
+PSUM = ["b0", "b1", "b2", "bdeg", "bhit", "bkey", "bself"]
+SCRATCH = {n: ("sbuf", [128, c], d) for n, (c, d) in _S.items()}
+SCRATCH.update({n: ("psum", [128, 512], FP) for n in PSUM})
+SEMAPHORES = (["qv", "qs", "qt", "qg", "dn", "dx", "do", "dl", "on", "ox", "oj", "loc"]
+              + ["a%d" % b for b in range(16)] + ["n%d" % b for b in range(16)])
+KON = {n: i for i, n in enumerate(["neg1", "half", "c33", "kv0", "kv1", "c32c", "c1280", "mbig", "p15", "pg"])}
+
+
+def plan(core, T, topo):
+    direct = [d for d in T.cores if d != core and topo.may_write(core, d)]
+    rest = [d for d in T.cores if d != core and not topo.may_write(core, d)]
+    relays = []
+    for d in rest:
+        ok = [x for x in topo.cores_of(core) if x not in T.cores and x not in relays and topo.may_write(x, d)]
+        ok.sort(key=lambda x: (topo.die(x) != topo.die(core), x))
+        relays.append(ok[0])
+    return direct, list(zip(relays, rest))
+
+
+def bits(engines):
+    return sum(1 << e for e in engines)
+
+
+def groups(t):
+    a, n = ("la", "a"), ("ln", "n")
+    return [[a, n]] if t == 0 else [[a], [n]]
+
+
+def share(engines, n, i):
+    k = len(engines) // n
+    return engines[i * k:(i + 1) * k]
+
+
+def legs(core, T, topo, m):
+    direct, via = plan(core, T, topo)
+    relays = [x for x, d in via]
+    return [[(d, j, share(topo.engines(core, d), len(ds) * m, i * m + j)) for i, d in enumerate(ds) for j in range(m)]
+            for ds in (relays, direct)]
+
+
+def onward(x, dst, topo, m):
+    return [(j, share(topo.engines(x, dst), m, j)) for j in range(m)]
+
+
+def relay_program(g, core, T, topo):
+    for r, src in enumerate(T.cores):
+        for x, dst in plan(src, T, topo)[1]:
+            if x != core:
+                continue
+            rid, pid = topo.addr(dst, core)
+            n = 0
+            for t in range(ROUNDS):
+                b = 4 * t + r
+                for grp in groups(t):
+                    for call in legs(src, T, topo, len(grp)):
+                        for d, j, eng in call:
+                            if d == core:
+                                g.wait_ge(T.sem["%s%d" % (grp[j][1], b)], len(eng))
+                    tr = []
+                    for j, eng in onward(core, dst, topo, len(grp)):
+                        piece = T[grp[j][0]][:, BL * b:BL * (b + 1)]
+                        tr.append(RemoteDMATransfer(dst_ids=[DstId(rid=rid, pnc=pid)], dma_engine_mask=bits(eng),
+                                                    remote_sem=T.sem["%s%d" % (grp[j][1], b)], srcs=[piece], dsts=[piece]))
+                        n += len(eng)
+                    g.remote_dma_fused(tr, local_sem=T.sem.loc)
+            g.wait_ge(T.sem.loc, n)
+
+
+def rank_program(g, core, T, topo):
+    rank = T.rank_of(core)
+    if rank is None:
+        relay_program(g, core, T, topo)
+        return
+    r = rank
+    Q = {"v": g.vector, "s": g.scalar, "t": g.tensor, "g": g, "y": g.sync}
+    cnt = {q: 0 for q in "vstg"}
+    known = {q: {} for q in "vstgy"}
+    hist = {}
+    totals = {}
+
+    def is_psum(n):
+        return n in PSUM
+
+    def deps(q, reads, writes):
+        toks = []
+        for kind, regs in (("r", reads), ("w", writes)):
+            for n, lo, hi in regs:
+                for e in hist.get(n, ()):
+                    if not is_psum(n) and (e[1] <= lo or hi <= e[0]):
+                        continue
+                    if kind == "r" and e[2] == "r" and not is_psum(n):
+                        continue
+                    if is_psum(n) and e[3] == q and (q == "t" or kind == "r" and e[2] == "r"):
+                        continue
+                    toks.append((e[4], e[5], e[6]))
+        return toks
+
+    def wait_for(q, toks):
+        need = {}
+        k = known[q]
+        for s, v, snap in toks:
+            if need.get(s, (0, None))[0] < v:
+                need[s] = (v, snap)
+        for s in list(need):
+            v = need[s][0]
+            if k.get(s, 0) >= v or any(o != s and sn.get(s, 0) >= v and k.get(o, 0) < ov for o, (ov, sn) in need.items()):
+                continue
+            Q[q].wait_ge(T.sem[s], v)
+        for s, (v, snap) in need.items():
+            k[s] = max(k.get(s, 0), v)
+            for o, ov in snap.items():
+                k[o] = max(k.get(o, 0), ov)
+
+    def note(q, reads, writes, sem, val, snap):
+        for n, lo, hi in writes:
+            h = hist.setdefault(n, [])
+            h[:] = [e for e in h if not (lo <= e[0] and e[1] <= hi)]
+            h.append((lo, hi, "w", q, sem, val, snap))
+        for n, lo, hi in reads:
+            h = hist.setdefault(n, [])
+            h[:] = [e for e in h if not (e[2] == "r" and e[3] == q and q in cnt and lo <= e[0] and e[1] <= hi)]
+            h.append((lo, hi, "r", q, sem, val, snap))
+
+    def real(x):
+        return ("kon", KON[x[0]], KON[x[0]] + 1) if x[0] in KON else x
+
+    def flat(x):
+        if not isinstance(x, tuple):
+            return []
+        if x[0] == "I":
+            return flat(x[1]) + flat(x[2])
+        x = real(x)
+        return [(x[0], x[1], x[2])]
+
+    def ap(x):
+        if not isinstance(x, tuple):
+            return x
+        if x[0] == "I":
+            return ap(x[1]).indirect(ap(x[2]))
+        x = real(x)
+        if len(x) > 3:
+            return T[x[0]][:, x[1]:x[2]:x[3]]
+        return T[x[0]][:, x[1]:x[2]]
+
+    def emit(q, fn, outs, ins):
+        reads, writes = [], []
+        for x in ins:
+            reads += flat(x)
+        for x in outs:
+            if isinstance(x, tuple) and x[0] == "I":
+                writes += flat(x[1])
+                reads += flat(x[2])
+            else:
+                writes += flat(x)
+        wait_for(q, deps(q, reads, writes))
+        inst = fn()
+        sem = "q" + q
+        cnt[q] += 1
+        inst.then_inc(T.sem[sem], 1)
+        totals[sem] = cnt[q]
+        snap = dict(known[q])
+        snap[sem] = cnt[q]
+        note(q, reads, writes, sem, cnt[q], snap)
+
+    def tc(out, in_):
+        emit("v", lambda: g.vector.tensor_copy(out=ap(out), in_=ap(in_)), [out], [in_])
+
+    def tt(out, a, b, op):
+        emit("v", lambda: g.vector.tensor_tensor(out=ap(out), in0=ap(a), in1=ap(b), op=op), [out], [a, b])
+
+    def ts(out, a, s1, op0, s2=None, op1=None):
+        if op1 is None:
+            emit("v", lambda: g.vector.tensor_scalar(out=ap(out), in0=ap(a), scalar1=ap(s1), scalar2=None, op0=op0), [out], [a, s1])
+        else:
+            emit("v", lambda: g.vector.tensor_scalar(out=ap(out), in0=ap(a), scalar1=ap(s1), scalar2=ap(s2), op0=op0, op1=op1),
+                 [out], [a, s1, s2])
+
+    def scan(out, d0, d1, op0, op1):
+        emit("v", lambda: g.vector.tensor_tensor_scan(out=ap(out), data0=ap(d0), data1=ap(d1), initial=0.0, op0=op0, op1=op1),
+             [out], [d0, d1])
+
+    def fill(out, c):
+        emit("v", lambda: g.vector.memset(ap(out), c), [out], [])
+
+    def act(out, in_, func=Fn.Copy, bias=0.0, scale=1.0, accum=None):
+        if accum is None:
+            emit("s", lambda: g.scalar.activation(out=ap(out), in_=ap(in_), func=func, bias=ap(bias), scale=ap(scale)),
+                 [out], [in_, bias, scale])
+        else:
+            emit("s", lambda: g.scalar.activation(out=ap(out), in_=ap(in_), func=func, bias=ap(bias), scale=scale,
+                                                  accum_out=ap(accum)), [out, accum], [in_, bias])
+
+    def mm(out, w, x, start, stop):
+        emit("t", lambda: g.tensor.matmul(out=ap(out), lhsT=ap(w), rhs=ap(x), start=start, stop=stop), [out], [w, x])
+
+    def iota(out, pattern, base, mul, flag=False):
+        if flag:
+            emit("g", lambda: g.iota(ap(out), pattern, base, mul, allow_small_or_imprecise_dtypes=True), [out], [])
+        else:
+            emit("g", lambda: g.iota(ap(out), pattern, base, mul), [out], [])
+
+    def dma(q, out, in_, sem, reads, writes):
+        wait_for(q, deps("dma", reads, writes))
+        Q[q].dma_start(out=out, in_=in_).then_inc(T.sem[sem], 16)
+        totals[sem] = totals.get(sem, 0) + 16
+        note("dma", reads, writes, sem, totals[sem], dict(known[q]))
+
+    near = [T.rank_of(d) for d in plan(core, T, topo)[0]]
+    order = [r] + near + [q for q in range(N) if q != r and q not in near]
+    first, last = order[:1 + len(near)], order[1 + len(near):]
+
+    def send(b, grp):
+        wait_for("g", deps("g", [(buf, BL * b, BL * (b + 1)) for buf, s in grp], []))
+        for call in legs(core, T, topo, len(grp)):
+            tr = []
+            for d, j, eng in call:
+                rid, pid = topo.addr(d, core)
+                piece = T[grp[j][0]][:, BL * b:BL * (b + 1)]
+                tr.append(RemoteDMATransfer(dst_ids=[DstId(rid=rid, pnc=pid)], dma_engine_mask=bits(eng),
+                                            remote_sem=T.sem["%s%d" % (grp[j][1], b)], srcs=[piece], dsts=[piece]))
+                totals["loc"] = totals.get("loc", 0) + len(eng)
+            g.remote_dma_fused(tr, local_sem=T.sem.loc)
+
+    for t in range(ROUNDS):
+        for q, src in enumerate(T.cores):
+            for grp in groups(t):
+                got = [(j, eng) for call in legs(src, T, topo, len(grp)) for d, j, eng in call if d == core]
+                got += [y for x, d in plan(src, T, topo)[1] if d == core for y in onward(x, core, topo, len(grp))]
+                for j, eng in got:
+                    buf, s = grp[j]
+                    b = 4 * t + q
+                    note("net", [], [(buf, BL * b, BL * (b + 1))], "%s%d" % (s, b), len(eng), {})
+                    totals["%s%d" % (s, b)] = len(eng)
+
+    c0s = [(8 * t + 2 * r) % 16 for t in range(2)]
+
+    def classes(n, st):
+        return [(n, c0s[st] + m, 16 * (H - 1) + c0s[st] + m + 1, 16) for m in range(2)]
+
+    def consts_v():
+        fill(("o16", 0, 128), -0.0625)
+        fill(("c32c", 0, 1), float(CAP))
+        ts(("cki", 0, 512), ("col", 0, 512), 15, Op.bitwise_and)
+        ts(("dg", 0, 256), ("cki", 0, 256), ("p15", 0, 1), Op.is_equal)
+        for lo, hi in ((0, 512), (512, 1024)):
+            ts(("seg", lo, hi), ("cki", 0, 512), 0.0, Op.is_gt)
+        fill(("neg1", 0, 1), -1.0)
+        fill(("half", 0, 1), 0.5)
+        fill(("mbig", 0, 1), -3.0e7)
+
+    def consts_v2():
+        for t in range(1, ROUNDS):
+            fill(("ln", BL * (4 * t + r), BL * (4 * t + r) + 4), 0.0)
+        for n in ("e1", "ns1"):
+            fill((n, L, LX), 0.0)
+        for i in range(2):
+            fill(("lv%d" % i, L, LX), float(V))
+        fill(("qf0", L, LX), float(V))
+        ts(("kp", 0, 512), ("cki", 0, 512), -512.0, Op.mult, 7680.0, Op.add)
+        ts(("c32", 0, 64), ("col", 0, 64), 31, Op.bitwise_and)
+        ts(("seg32", 0, 64), ("c32", 0, 64), 0.0, Op.is_gt)
+        for c in range(2):
+            ts(("dmp", c, c + 1), ("sc", c, c + 1), 576.0, Op.add)
+            ts(("tri", 32 * c, 32 * c + 32), ("col", 0, 32), ("sc", c, c + 1), Op.is_lt, ("dmp", c, c + 1), Op.mult)
+        for n in ("jwa", "jwb", "jwc"):
+            ts((n, 0, 32), ("jwf", 0, 32), ("p15", 0, 1), Op.add)
+
+    def consts_g():
+        iota(("jwf", 0, 32), [[BL, 16], [16, 2]], 4, 0, True)
+        iota(("en", 0, G0), [[0, G0]], 0, 0, True)
+        iota(("rs", 0, G0), [[0, G0]], -SHIFT - 16384, 0, True)
+        iota(("idc", 0, 512), [[BL, 16], [1, 32]], 4 - SHIFT, 0, True)
+        iota(("w", 0, IDW), [[1, IDW]], -SHIFT, 0, True)
+        iota(("vn", 0, G0), [[-1, G0]], V, 0, True)
+        iota(("jt", 0, VT), [[1, VT]], 0, 0, True)
+        iota(("vid", 0, IDW), [[0, IDW]], 0, 0, True)
+
+    def names_again(st, lo, hi):
+        act(("qr%d" % st, 16 * lo, 16 * hi), ("I", ("qf%d" % st, 0, LX), ("lrep", lo, hi)), Fn.Identity, ("c1280", 0, 1), -1.0)
+
+    def consts_s():
+        names_again(1, H, L)
+        act(("i1280", 0, 128), ("idn", 0, 128), Fn.Copy, 0.0, 1280.0)
+        act(("bd8", 0, 128), ("bd", 0, 128), Fn.Copy, 0.0, 8192.0)
+        act(("kb", 0, 512), ("seg", 0, 512), Fn.Identity, ("mbig", 0, 1), 6.0e7)
+        for k in range(16):
+            act(("dk", 128 * k, 128 * k + 128), ("idn", 0, 128), Fn.Copy, 0.0, ("dg", k, k + 1))
+        act(("idead", 0, 128), ("idn", 0, 128), Fn.Copy, 0.0, -32768.0)
+        act(("ipen", 0, 128), ("idn", 0, 128), Fn.Copy, 0.0, -64.0)
+
+    def sums(buf, lo, hi):
+        for k in range(16):
+            mm(("bdeg", lo, hi), ("idn", 0, 128), (buf, 16 * lo + k, 16 * (hi - 1) + k + 1, 16), k == 0, k == 15)
+
+    def hits(t):
+        st, old = t % 2, 4 * (t - 1)
+        if t > 0:
+            put("rs", old, old + 4, ("ksn", 0, 128))
+        if t == 0:
+            ts(("ok", 0, L), ("bdeg", 0, L), ("limf", 0, 1), Op.is_le)
+        else:
+            tt(("ok", 0, L), ("bdeg", 0, L), ("lmx", 0, L), Op.is_le)
+        if t >= 2:
+            mm(("bhit", 0, L), ("ipen", 0, 128), ("dead%d" % st, 0, L), True, False)
+        mm(("bhit", 0, L), ("bd", 0, 128), ("ok", 0, L), t < 2, True)
+        ts(("hit", 0, L), ("bhit", 0, L), 9.0, Op.is_ge)
+        scan(("cum", 0, LX), ("hit", 0, LX), ("c255", 0, LX), Op.add, Op.min)
+        for c in range(2):
+            act(("sg", c * LX, (c + 1) * LX), ("cum", 0, LX), Fn.Sign, ("sh", c, c + 1), -1.0, ("pla", c, c + 1))
+        if t == 0:
+            ts(("deg", 0, L), ("bdeg", 0, L), -1.0, Op.mult, ("limf", 0, 1), Op.add)
+        else:
+            tt(("deg", 0, L), ("lmx", 0, L), ("bdeg", 0, L), Op.subtract)
+        if t > 1:
+            put("rs", 0, old, ("jr", 0, 32 * old))
+        ts(("plw", 0, 2), ("pla", 0, 2), 0.5, Op.mult, float(LX // 2), Op.add)
+
+    def variables(t):
+        st, b = t % 2, 4 * t + r
+        act(("vy", 0, 2), ("pla", 0, 2), Fn.Sign, ("c33", 0, 1))
+        act(("vx", 0, 2), ("vy", 0, 2), Fn.Identity, ("kv%d" % st, 0, 1), (1 - V) / 2.0)
+        for c in range(2):
+            act(("la", BL * b + c, BL * b + c + 1), ("pla", c, c + 1), Fn.Identity, ("vx", c, c + 1), 8.0)
+
+    def sizes(t):
+        b = 4 * t + r
+        ts(("la", BL * b + 4, BL * (b + 1)), ("I", ("deg", 0, LX), ("plw", 0, 2)), ("limb", 0, 1), Op.subtract, -256.0, Op.max)
+
+    def dead_of(t):
+        ts(("piv", 0, L), ("cum", 0, L), float(CAP), Op.is_le)
+        tt(("dead%d" % t, 0, L), ("piv", 0, L), ("hit", 0, L), Op.mult)
+
+    def count(t):
+        act(("a1", 0, 1), ("cum", L - 1, L), Fn.Relu, ("c32c", 0, 1), -1.0)
+        mm(("bhit", 0, 1), ("o16", 0, 128), ("a1", 0, 1), True, True)
+
+    def limits(t):
+        tc(("ai", 0, 1), ("bhit", 0, 1))
+        ts(("aj", 0, 1), ("ai", 0, 1), 7, Op.bitwise_and)
+        tt(("lima", 0, 1), ("limf", 0, 1), ("aj", 0, 1), Op.add)
+        ts(("limb", 0, 1), ("lima", 0, 1), 1.0, Op.add)
+
+    def list_v(b):
+        tc(("evu", 2 * b, 2 * b + 2), ("la", BL * b, BL * b + 2))
+
+    def list_c(b):
+        tc(("cwu", 2 * b, 2 * b + 2), ("la", BL * b + 2, BL * b + 4))
+
+    def put(table, lo, hi, src):
+        tc(("I", (table, 0, VT), ("evu", 2 * lo, 2 * hi)), src)
+
+    def put_names(b):
+        o, i = ("I", ("nm", 0, VT), ("evu", 2 * b, 2 * b + 2)), ("ln", BL * b + 4, BL * (b + 1))
+        ts(o, i, -1.0, Op.mult, float(V), Op.add)
+
+    def size_of(b):
+        i = 32 * (b % 4)
+        act(("xt", i, i + 32), ("la", BL * b + 4, BL * (b + 1)), Fn.Identity, ("neg1", 0, 1), -1.0)
+
+    def outputs(t):
+        for q in range(N):
+            b = 4 * t + q
+            i = 32 * q
+            act(("nt", i, i + 32), ("ln", BL * b + 4, BL * (b + 1)), Fn.Identity, ("c1280", 0, 1), -1.0)
+            act(("vid", BL * b + 4, BL * (b + 1)), ("I", ("jt", 0, VT), ("evu", 2 * b, 2 * b + 2)))
+        put("nm", 4 * t, 4 * t + 4, ("nt", 0, 128))
+        put("xo", 4 * t, 4 * t + 4, ("xt", 0, 128))
+
+    def picks(t):
+        st = t % 2
+        for lo, hi in CH:
+            act(("xg", 16 * lo, 16 * hi), ("I", ("xm", 0, G0), ("qu%d" % st, lo, hi)))
+
+    def self_picks():
+        for k in range(16):
+            mm(("bself", 0, L), ("dk", 128 * k, 128 * k + 128), ("xg", k, 16 * (L - 1) + k + 1, 16), k == 0, k == 15)
+
+    def main(t):
+        st, old = t % 2, 4 * (t - 1)
+
+        def cover(c):
+            lo, hi = CH[c]
+            tt(("eq", 16 * lo, 16 * hi), ("I", ("en", 0, G0), ("qu%d" % st, lo, hi)), ("qr%d" % st, 16 * lo, 16 * hi), Op.is_equal)
+            if t >= 2:
+                mm((PSUM[c], 0, hi - lo), ("idead", 0, 128), ("dead%d" % st, lo, hi), True, False)
+            for k in range(16):
+                mm((PSUM[c], 0, hi - lo), ("i1280", 0, 128), ("eq", 16 * lo + k, 16 * (hi - 1) + k + 1, 16), t < 2 and k == 0, k == 15)
+
+        def uncovered(c):
+            lo, hi = CH[c]
+            tt(("q2", lo, hi), ("qf%d" % st, lo, hi), (PSUM[c], 0, hi - lo), Op.max)
+            ts(("qn", lo, hi), ("q2", lo, hi), float(V), Op.min)
+
+        def pick(c, on):
+            lo, hi = CH[c]
+            o, i = ("xv", 16 * lo, 16 * hi), ("I", ("xm", 0, G0), ("qn", lo, hi))
+            if on == "s":
+                act(o, i, Fn.Relu)
+            else:
+                ts(o, i, 0.0, Op.max)
+
+        def largest(c):
+            lo, hi = CH[c]
+            scan(("msc", 16 * lo, 16 * hi), ("seg", 0, 16 * (hi - lo)), ("xg", 16 * lo, 16 * hi), Op.mult, Op.min)
+
+        cover(0)
+        tt(("ksn", 0, 128), ("idc", 32 * old, 32 * old + 128), ("bkey", 0, 128), Op.add)
+        cover(1)
+        uncovered(0)
+        pick(0, "s")
+        cover(2)
+        uncovered(1)
+        pick(1, "s")
+        sums("xv", *CH[0])
+        largest(0)
+        uncovered(2)
+        pick(2, "v")
+        largest(1)
+        largest(2)
+        ts(("lmx", 0, L), ("msc", 15, 16 * L, 16), ("limb", 0, 1), Op.add, ("lima", 0, 1), Op.min)
+        for q in range(N):
+            act(("ksl", BL * (old + q) + 4, BL * (old + q + 1)), ("ksn", 32 * q, 32 * q + 32))
+        if t > 1:
+            act(("jr", 0, 32 * old), ("I", ("ksl", 0, BL * (old + 4)), (("jwb", "jwc")[t - 2], 0, 2 * old)))
+        for c in range(2):
+            tc(("evu", 2 * old + c, 2 * old + 7 + c, 2), ("la", BL * old + c, BL * (old + 3) + c + 1, BL))
+        sums("xv", *CH[2])
+        sums("xv", *CH[1])
+
+    def pivots(t):
+        st, b = t % 2, 4 * t + r
+
+        def keys():
+            tt(("key", 0, 512), ("I", ("rs", 0, G0), ("qp", 0, 32)), ("kp", 0, 512), Op.add)
+            scan(("ksc", 0, 512), ("kb", 0, 512), ("key", 0, 512), Op.min, Op.max)
+
+        def own_gathers():
+            self_picks()
+            act(("esg", 0, L), ("bself", 0, L), Fn.Sign, ("half", 0, 1))
+            act(("e1", 0, L), ("esg", 0, L), Fn.Relu, 0.0, float(V))
+            act(("ocx", 0, L), ("q2", 0, L), Fn.Identity, ("c1280", 0, 1), -1.0)
+            act(("e1p", 0, 32), ("I", ("e1", 0, LX), ("plw", 0, 2)))
+
+        def names():
+            tt(("b0", 0, 512), ("xn", 0, 512), ("b1", 0, 512), Op.not_equal)
+            tt(("cc", 0, 512), ("xn", 0, 512), ("b0", 0, 512), Op.mult)
+            scan(("nsc", 0, 512), ("seg", 0, 512), ("cc", 0, 512), Op.mult, Op.max)
+            tt(("ocp", 0, 32), ("I", ("ocx", 0, LX), ("plw", 0, 2)), ("e1p", 0, 32), Op.min)
+            tt(("ocq", 0, 32), ("I", ("ns%d" % st, 0, LX), ("plw", 0, 2)), ("ocp", 0, 32), Op.mult)
+            tt(("ln", BL * b + 4, BL * (b + 1)), ("ocq", 0, 32), ("nsc", 15, 512, 16), Op.max)
+            send(b, [("ln", "n")])
+
+        def claims():
+            tc(("mi", 0, 32), ("ksc", 15, 512, 16))
+            ts(("mj", 0, 32), ("mi", 0, 32), 511, Op.bitwise_and)
+            tt(("kd", 0, 32), ("mj", 0, 32), ("dg", 0, 32), Op.mult)
+            scan(("kw", 0, 32), ("seg", 0, 32), ("kd", 0, 32), Op.mult, Op.add)
+            for c in range(2):
+                ts(("ke", 32 * c, 32 * c + 32), ("mj", 0, 32), ("kw", 16 * c + 15, 16 * c + 16), Op.is_equal)
+            tt(("kf", 0, 64), ("ke", 0, 64), ("tri", 0, 64), Op.mult)
+            scan(("kg", 0, 64), ("seg32", 0, 64), ("kf", 0, 64), Op.mult, Op.max)
+            tt(("la", BL * b + 2, BL * b + 4), ("kw", 15, 32, 16), ("kg", 31, 64, 32), Op.max)
+            send(b, [("la", "a")])
+
+        tc(("qp", 0, 32), ("I", ("qf%d" % st, 0, LX), ("plw", 0, 2)))
+        act(("xn", 0, 512), ("I", ("en", 0, G0), ("qp", 0, 32)))
+        keys()
+        tc(("vp", 0, 32), ("I", ("lv%d" % st, 0, LX), ("plw", 0, 2)))
+        variables(t)
+        if t < ROUNDS - 1:
+            count(t)
+        act(("vr", 0, 512), ("I", ("vn", 0, G0), ("vp", 0, 32)))
+        act(("b1", 0, 512), ("vr", 0, 512))
+        own_gathers()
+        sizes(t)
+        claims()
+        if t < ROUNDS - 1:
+            limits(t)
+        if t < 2:
+            dead_of(t)
+        names()
+
+    def kept_rows(t):
+        st = t % 2
+        tt(("b1", 0, L), ("qf%d" % st, 0, L), ("e1", 0, L), Op.max)
+        if t == 1:
+            tt(("qf1", 0, L), ("q2", 0, L), ("b1", 0, L), Op.min)
+            tc(("qu1", 0, L), ("qf1", 0, L))
+        else:
+            tt(("q3", 0, L), ("q2", 0, L), ("b1", 0, L), Op.min)
+            for m, x in enumerate(classes("nm", st)):
+                act(x, ("q3", m * H, (m + 1) * H))
+
+    def update(t):
+        jo, jn = (None, "jwa", "jwb")[t], (None, "jwb", "jwc")[t]
+        old = 4 * t
+        n = 32 * old
+
+        def place(table, b, src):
+            tc(("I", (table, 0, VT), ("vc", 4 * b, 4 * b + 2)), src)
+
+        def land(qs, lists, sz, nms):
+            for q in qs:
+                b = 4 * t + q
+                if lists:
+                    tc(("vc", 4 * b, 4 * b + 4), ("la", BL * b, BL * b + 4))
+                    size_of(b)
+                if sz:
+                    place("xm", b, ("la", BL * b + 4, BL * (b + 1)))
+                if nms:
+                    place("en", b, ("ln", BL * b + 4, BL * (b + 1)))
+
+        land(first, True, True, False)
+        land(first, False, False, True)
+        land(last, True, t == 0, False)
+        mm(("bkey", 0, 128), ("bd8", 0, 128), ("xt", 0, 128), True, True)
+        if t > 0:
+            for q in (3, 2, 1, 0):
+                b = 4 * t + q
+                tc(("I", ("w", 0, IDW), ("vc", 4 * b + 2, 4 * b + 4)), ("idc", 32 * b, 32 * b + 32))
+            tt(("jd", 0, n), ("I", ("w", 0, IDW), (jo, 0, 2 * old)), ("dg", 0, n), Op.mult)
+            scan(("js", 0, n), ("seg", 0, n), ("jd", 0, n), Op.mult, Op.add)
+            ts((jn, 0, 2 * old), ("js", 15, n, 16), float(SHIFT), Op.add)
+            act(("xr", 0, n), ("I", ("la", 0, BL * (old + 4)), (jn, 0, 2 * old)))
+            land(last, False, True, False)
+            put("xm", 0, old, ("xr", 0, n))
+        picks(t + 1)
+        land(last, False, False, True)
+        if t > 0:
+            tc(("er", 0, n), ("I", ("ln", 0, BL * (old + 4)), (jn, 0, 2 * old)))
+            put("en", 0, old, ("er", 0, n))
+
+    dma("y", T["nm"][:, 0:V], T.nb[:, :], "dn", [], [("nm", 0, V)])
+    dma("s", T["xm"][:, 0:V], T.xs[:, :], "dx", [], [("xm", 0, V)])
+    dma("s", T["limi"][:, 0:1], T.lim[:, 0:1], "dl", [], [("limi", 0, 1)])
+    wait_for("y", [("dn", 16, {})])
+    dma("y", T["xo"][:, 0:V], T.xs[:, :], "do", [], [("xo", 0, V)])
+    iota(("pii", 0, 1), [[1, 1]], 0, 1)
+    iota(("col", 0, 512), [[1, 512]], 0, 0)
+    fill(("one", 0, 128), 1.0)
+    emit("g", lambda: g.affine_select(T["idn"][:, :], T["one"][:, :], [[-1, 128]], Op.is_equal, 0.0, 0, 1),
+         [("idn", 0, 128)], [("one", 0, 128)])
+    for i in range(2):
+        iota(("lv%d" % i, 0, L), [[1, 2], [16, H]], c0s[i], 0, True)
+    fill(("xm", V, V + 16), 0.0)
+    fill(("hit", L, LX), 1.0)
+    fill(("c255", 0, LX), 255.0)
+    for n in ("deg", "ocx", "ns0"):
+        fill((n, L, LX), 0.0)
+    fill(("qf1", L, LX), float(V))
+    fill(("c1280", 0, 1), float(V))
+    fill(("ksl", 0, 576), 0.0)
+    fill(("c33", 0, 1), float(LX - 2 * H + 1))
+    for i in range(2):
+        fill(("kv%d" % i, 0, 1), 8.0 * LX + c0s[i] + (1 - V) / 2.0)
+    ts(("pij", 0, 1), ("pii", 0, 1), 15, Op.bitwise_and)
+    ts(("pij", 1, 2), ("pii", 0, 1), 4, Op.arith_shift_right)
+    tc(("p15", 0, 1), ("pij", 0, 1))
+    tc(("pg", 0, 1), ("pij", 1, 2))
+    for c in range(2):
+        ts(("sc", c, c + 1), ("p15", 0, 1), 16.0 * c, Op.add)
+        ts(("sh", c, c + 1), ("p15", 0, 1), 16.0 * c + 0.5, Op.add)
+    ts(("gi", 0, 128), ("col", 0, 128), 4, Op.arith_shift_right)
+    ts(("bd", 0, 128), ("gi", 0, 128), ("pg", 0, 1), Op.is_equal)
+    for buf in ("la", "ln"):
+        fill((buf, BL * r, BL * r + 4), 0.0)
+    tc(("lrep", 0, L), ("col", 0, L))
+    tc(("limf", 0, 1), ("limi", 0, 1))
+    ts(("limb", 0, 1), ("limf", 0, 1), 1.0, Op.add)
+
+    for m, x in enumerate(classes("nm", 0)):
+        tc(("qu0", m * H, (m + 1) * H), x)
+    for lo, hi in CH0:
+        mid = (lo + hi) // 2
+        for f, a, z in ((tc, lo, mid), (act, mid, hi)):
+            f(("xv", 16 * a, 16 * z), ("I", ("xm", 0, G0), ("qu0", a, z)))
+        sums("xv", lo, hi)
+    for st in (1, 0):
+        for m, x in enumerate(classes("nm", st)):
+            tc(("qf%d" % st, m * H, (m + 1) * H), x)
+    act(("ocx", 0, L), ("qf0", 0, L), Fn.Identity, ("c1280", 0, 1), -1.0)
+    names_again(1, 0, H)
+    tc(("qu1", 0, L), ("qf1", 0, L))
+    tt(("ns0", 0, L), ("qf0", 0, L), ("lv0", 0, L), Op.not_equal)
+    hits(0)
+    sizes(0)
+    variables(0)
+    tc(("ocp", 0, 32), ("I", ("ocx", 0, LX), ("plw", 0, 2)))
+    tt(("ln", BL * r + 4, BL * (r + 1)), ("I", ("ns0", 0, LX), ("plw", 0, 2)), ("ocp", 0, 32), Op.mult)
+    send(r, [("la", "a"), ("ln", "n")])
+    consts_g()
+    consts_v()
+    count(0)
+    limits(0)
+    consts_s()
+    dead_of(0)
+    tt(("ns1", 0, L), ("qf1", 0, L), ("lv1", 0, L), Op.not_equal)
+    consts_v2()
+    update(0)
+
+    for t in range(1, ROUNDS):
+        main(t)
+        hits(t)
+        pivots(t)
+        outputs(t - 1)
+        if t == 1:
+            for lo, hi in CH:
+                names_again(0, lo, hi)
+        kept_rows(t)
+        if t > 1:
+            put_names(4 * (t - 2) + r)
+        if t < ROUNDS - 1:
+            update(t)
+
+    t, old = 3, 12
+
+    def lands(qs):
+        for q in qs:
+            b = 4 * t + q
+            list_v(b)
+            act(("vb", 32 * q, 32 * q + 32), ("I", ("jt", 0, VT), ("evu", 2 * b, 2 * b + 2)))
+            size_of(b)
+            list_c(b)
+
+    def sizes_out(qs):
+        for q in qs:
+            put("xo", 12 + q, 13 + q, ("xt", 32 * q, 32 * q + 32))
+
+    lands(first)
+    sizes_out(first)
+    for q in first:
+        put_names(12 + q)
+    lands(last)
+    for q in (3, 2, 1, 0):
+        tc(("I", ("vid", 0, IDW), ("cwu", 24 + 2 * q, 26 + 2 * q)), ("vb", 32 * q, 32 * q + 32))
+    for lo, hi in ((0, 8), (8, old)):
+        act(("jf", 32 * lo, 32 * hi), ("I", ("vid", 0, IDW), ("jwc", 2 * lo, 2 * hi)))
+    sizes_out(last)
+    dma("s", T.yx[:, :], T["xo"][:, 0:V], "ox", [("xo", 0, V)], [])
+    for q in last:
+        put_names(12 + q)
+    dma("y", T.yn[:, :], T["nm"][:, 0:V], "on", [("nm", 0, V)], [])
+    put("jt", 0, 8, ("jf", 0, 256))
+    put("jt", 8, old, ("jf", 256, 384))
+    dma("y", T.yj[:, :], T["jt"][0:128:16, 0:V], "oj", [("jt", 0, V)], [])
+    for s, v in totals.items():
+        if known["g"].get(s, 0) < v:
+            g.wait_ge(T.sem[s], v)

@@ -4,44 +4,66 @@ from concourse.mybir import AluOpType as Op, ActivationFunctionType as Fn
 V, H, CAP, ROUNDS = 1280, 80, 32, 4
 N = 4
 L = 2 * H
-LX = L + CAP
-VT = 1792
+LX = L + 2 * CAP
+VT = 2304
 G0 = 1288
-BL = 36
-IDW = 640
+WIDE = [36, 44, 52, 92]
+START = [752, 576, 368, 0]
+SIZES, VARS, CLAIMS, FREE = [0, 0, 20, 0], [32, 32, 0, 32], [None, 34, 2, 34], 60
+CW = 896
+ID0, VAL = 384, 1024
 SHIFT = 512 * 32618
 FP, BF, I32, U16 = "float32", "bfloat16", "int32", "uint16"
 CH0 = [(0, 64), (64, 160)]
-CH = [(0, 64), (64, 128), (128, 160)]
+CH = [(0, 48), (48, 112), (112, 160)]
+PART = [0, 0, 24, 0, 0, 0]
+LISTS = {1: ("qu1", "qn"), 2: ("qu0", "qm"), 3: ("qn", "qu1")}
+CYCLE, GATHER, SCATTER, PE, WAKE, ACROSS, HOP = 0.001, 1.4, 2.5, 0.5, 0.08, 0.13, 2.2
+FIXED = {"v": 0.06, "s": 0.12, "t": 0.0, "g": 0.15}
+PASSES = 2
+SAME = True
+KEYS = 0
+DBG = []
 
 _S = {
-    "nm": (VT, FP), "en": (VT, FP), "rs": (VT, FP), "vn": (G0, FP), "jt": (VT, FP), "xm": (VT, BF), "xo": (VT, BF),
-    "la": (576, FP), "ln": (576, FP), "ksl": (576, FP), "ksn": (128, FP), "w": (IDW, FP), "vid": (IDW, FP), "vb": (128, FP),
-    "idc": (512, FP), "jwa": (32, U16), "jwb": (32, U16), "jwc": (32, U16), "evu": (32, U16), "vc": (64, U16), "cwu": (32, U16),
-    "jwf": (32, FP),
-    "qf0": (LX, FP), "qf1": (LX, FP), "qu0": (L, U16), "qu1": (L, U16), "qr0": (16 * L, FP), "qr1": (16 * L, FP),
-    "lv0": (LX, FP), "lv1": (LX, FP), "ns0": (LX, FP), "ns1": (LX, FP), "dead0": (L, BF), "dead1": (L, BF),
-    "xg": (16 * L, BF), "eq": (16 * L, BF), "xv": (16 * L, BF), "msc": (16 * L, BF), "lmx": (L, FP), "deg": (LX, FP),
-    "ocx": (LX, FP), "e1": (LX, FP), "esg": (L, FP), "q2": (L, FP), "q3": (L, FP), "qn": (L, U16), "ok": (L, BF), "hit": (LX, BF),
-    "cum": (LX, BF), "c255": (LX, BF), "sg": (2 * LX, BF), "pla": (2, FP), "plw": (2, U16), "vx": (2, FP), "vy": (2, FP),
-    "piv": (L, BF),
-    "qp": (32, U16), "vp": (32, U16), "e1p": (32, FP), "ocp": (32, FP), "ocq": (32, FP),
-    "xn": (512, FP), "vr": (512, FP), "cc": (512, FP), "nsc": (512, FP), "key": (512, FP), "ksc": (512, FP),
-    "mi": (32, I32), "mj": (32, I32), "kd": (32, FP),
-    "kw": (32, FP), "ke": (64, FP), "kf": (64, FP), "kg": (64, FP), "jd": (256, FP), "js": (256, FP), "jr": (256, FP), "xr": (256, FP),
-    "er": (256, FP), "jf": (384, FP), "xt": (128, BF), "nt": (128, FP), "a1": (1, BF), "ai": (1, I32), "aj": (1, I32),
-    "limi": (1, I32), "limf": (1, FP), "lima": (1, FP), "limb": (1, FP), "kon": (16, FP),
-    "one": (128, BF), "idn": (128, BF), "i1280": (128, BF), "idead": (128, BF), "ipen": (128, BF), "bd": (128, BF), "bd8": (128, BF),
-    "dk": (2048, BF), "o16": (128, BF), "pii": (1, I32), "pij": (2, I32), "sh": (2, FP), "sc": (2, FP),
-    "dmp": (2, FP), "col": (512, I32), "cki": (512, I32), "gi": (128, I32), "dg": (256, FP), "seg": (1024, BF),
-    "c32": (64, I32), "seg32": (64, BF), "kb": (512, FP), "kp": (512, FP), "tri": (64, FP), "lrep": (L, U16),
+    "nm": (VT, FP), "en": (VT, FP), "rs": (VT, FP), "jt": (VT, FP), "xm": (VT, BF), "xo": (VT, BF),
+    "la": (CW, FP), "ln": (CW, FP), "l3": (128, FP), "idt": (CW, FP),
+    "jf0": (8, FP), "jf1": (16, FP), "jf2": (24, FP), "jf3": (24, FP), "ju0": (8, U16), "ju1": (16, U16), "ju2": (24, U16),
+    "ju3": (24, U16), "j3": (8, U16), "jb": (32, FP), "m0": (24, FP), "m1": (24, FP), "evu": (32, U16),
+    "er0": (128, FP), "er1": (256, FP), "er2": (384, FP), "xr0": (128, BF), "xr1": (256, BF), "xr2": (384, BF),
+    "idr": (384, FP), "bk": (384, FP), "jv": (384, FP), "xt": (512, BF), "nt": (384, FP),
+    "qf0": (LX, FP), "qf1": (LX, FP), "of0": (LX, FP), "of1": (LX, FP), "ocx": (L, FP), "nl0": (LX, FP), "nl1": (LX, FP), "lid": (LX, FP),
+    "qu0": (L, U16), "qu1": (L, U16), "qn": (L, U16), "qm": (L, U16), "qr0": (16 * L, FP), "qr1": (16 * L, FP),
+    "dead0": (L, BF), "dead1": (L, BF), "piv": (L, BF), "pih": (L, BF),
+    "eq": (16 * L, BF), "xv": (16 * L, BF), "msc": (16 * L, BF), "deg": (LX, I32), "si": (L, I32),
+    "z": (LX, FP), "q2": (L, FP), "ok": (L, BF), "hit": (LX, BF), "cum": (LX, BF), "c255": (LX, BF),
+    "sg": (2 * LX, BF), "sn": (2 * LX, BF), "sgl": (2 * LX, BF), "plw": (2, U16), "vx": (2, FP), "vy": (2, FP),
+    "qp": (32, U16), "vp": (32, U16), "zp": (32, FP), "xn": (544, FP), "vr": (544, FP), "cc": (544, FP), "nsc": (512, FP),
+    "key": (512, FP), "ksc": (512, FP), "mi": (32, I32), "mj": (32, I32), "rho": (768, FP), "ne": (768, BF), "fc": (768, FP),
+    "c1": (768, FP), "rev": (48, U16), "rep": (48, U16), "revf": (48, FP), "repi": (48, I32),
+    "a1": (1, BF), "ai": (1, I32), "aj": (1, I32), "limi": (1, I32), "limf": (1, FP), "lima": (1, FP),
+    "one": (128, BF), "idn": (128, BF), "idead": (128, BF), "ipen": (128, BF), "imx": (128, BF), "bdh": (128, BF), "bd": (128, BF),
+    "bd8": (128, BF), "dk": (2048, BF), "o16": (128, BF), "pii": (2, I32), "pij": (2, I32), "c16": (2, I32), "sc": (2, FP),
+    "ck": (16, FP), "qsc": (16, FP), "qbi": (16, FP), "wsc": (16, FP), "seg": (1024, BF), "kb": (512, FP),
 }
-PSUM = ["b0", "b1", "b2", "bdeg", "bhit", "bkey", "bself"]
+PSUM = {"b0": 1024, "b1": 1024, "b2": 512, "d0": 512, "bhit": 512, "bkey": 512}
 SCRATCH = {n: ("sbuf", [128, c], d) for n, (c, d) in _S.items()}
-SCRATCH.update({n: ("psum", [128, 512], FP) for n in PSUM})
+SCRATCH.update({n: ("psum", [128, c], FP) for n, c in PSUM.items()})
 SEMAPHORES = (["qv", "qs", "qt", "qg", "dn", "dx", "do", "dl", "on", "ox", "oj", "loc"]
-              + ["a%d" % b for b in range(16)] + ["n%d" % b for b in range(16)])
-KON = {n: i for i, n in enumerate(["neg1", "half", "c33", "kv0", "kv1", "c32c", "c1280", "mbig", "p15", "pg"])}
+              + [x + str(b) for x in ("a", "n", "la", "ln") for b in range(16)])
+
+
+def block(t, q, part=0, n=None):
+    lo = START[t] + WIDE[t] * q + part
+    return ("la", lo, lo + (WIDE[t] if n is None else n))
+
+
+def names_of(t, q):
+    return ("l3", 32 * q, 32 * q + 32) if t == ROUNDS - 1 else ("ln",) + block(t, q, SIZES[t], 32)[1:]
+
+
+def messages(t, q):
+    return [(block(t, q), "a%d" % (4 * t + q)), (names_of(t, q), "n%d" % (4 * t + q))]
 
 
 def plan(core, T, topo):
@@ -59,25 +81,20 @@ def bits(engines):
     return sum(1 << e for e in engines)
 
 
-def groups(t):
-    a, n = ("la", "a"), ("ln", "n")
-    return [[a, n]] if t == 0 else [[a], [n]]
-
-
-def share(engines, n, i):
-    k = len(engines) // n
-    return engines[i * k:(i + 1) * k]
-
-
-def legs(core, T, topo, m):
+def legs(core, T, topo):
     direct, via = plan(core, T, topo)
-    relays = [x for x, d in via]
-    return [[(d, j, share(topo.engines(core, d), len(ds) * m, i * m + j)) for i, d in enumerate(ds) for j in range(m)]
-            for ds in (relays, direct)]
+    out = []
+    for ds in ([x for x, d in via], direct):
+        k = [len(topo.engines(core, d)) // len(ds) for d in ds]
+        out.append([(d, topo.engines(core, d)[i * k[i]:(i + 1) * k[i]]) for i, d in enumerate(ds)])
+    return out
 
 
-def onward(x, dst, topo, m):
-    return [(j, share(topo.engines(x, dst), m, j)) for j in range(m)]
+def transfer(T, topo, src, dst, engines, cols, sem):
+    rid, pid = topo.addr(dst, src)
+    piece = T[cols[0]][:, cols[1]:cols[2]]
+    return RemoteDMATransfer(dst_ids=[DstId(rid=rid, pnc=pid)], dma_engine_mask=bits(engines), remote_sem=T.sem[sem],
+                             srcs=[piece], dsts=[piece])
 
 
 def relay_program(g, core, T, topo):
@@ -85,23 +102,13 @@ def relay_program(g, core, T, topo):
         for x, dst in plan(src, T, topo)[1]:
             if x != core:
                 continue
-            rid, pid = topo.addr(dst, core)
-            n = 0
+            into = [eng for call in legs(src, T, topo) for d, eng in call if d == core][0]
+            out = topo.engines(core, dst)
             for t in range(ROUNDS):
-                b = 4 * t + r
-                for grp in groups(t):
-                    for call in legs(src, T, topo, len(grp)):
-                        for d, j, eng in call:
-                            if d == core:
-                                g.wait_ge(T.sem["%s%d" % (grp[j][1], b)], len(eng))
-                    tr = []
-                    for j, eng in onward(core, dst, topo, len(grp)):
-                        piece = T[grp[j][0]][:, BL * b:BL * (b + 1)]
-                        tr.append(RemoteDMATransfer(dst_ids=[DstId(rid=rid, pnc=pid)], dma_engine_mask=bits(eng),
-                                                    remote_sem=T.sem["%s%d" % (grp[j][1], b)], srcs=[piece], dsts=[piece]))
-                        n += len(eng)
-                    g.remote_dma_fused(tr, local_sem=T.sem.loc)
-            g.wait_ge(T.sem.loc, n)
+                for cols, sem in messages(t, r):
+                    g.wait_ge(T.sem[sem], len(into))
+                    g.remote_dma_fused([transfer(T, topo, core, dst, out, cols, sem)], local_sem=T.sem.loc)
+            g.wait_ge(T.sem.loc, 2 * ROUNDS * len(out))
 
 
 def rank_program(g, core, T, topo):
@@ -115,20 +122,30 @@ def rank_program(g, core, T, topo):
     known = {q: {} for q in "vstgy"}
     hist = {}
     totals = {}
+    row, aside = [], set()
+    calls = []
 
-    def is_psum(n):
-        return n in PSUM
+    def meet(a, b):
+        return a[0] < b[1] and b[0] < a[1] and (a[2] != b[2] or (a[0] - b[0]) % a[2] == 0)
+
+    def holds(a, b):
+        return a[0] <= b[0] and b[1] <= a[1] and (a[2] == 1 or a[2] == b[2] and (a[0] - b[0]) % a[2] == 0)
+
+    def parts(regs):
+        return [(x[0], (x[1:] + (1,))[:3]) for x in regs]
 
     def deps(q, reads, writes):
         toks = []
         for kind, regs in (("r", reads), ("w", writes)):
-            for n, lo, hi in regs:
+            for n, c in parts(regs):
                 for e in hist.get(n, ()):
-                    if not is_psum(n) and (e[1] <= lo or hi <= e[0]):
+                    if n not in PSUM and not meet(c, e[0]):
                         continue
-                    if kind == "r" and e[2] == "r" and not is_psum(n):
+                    if kind == "r" and e[2] == "r" and n not in PSUM:
                         continue
-                    if is_psum(n) and e[3] == q and (q == "t" or kind == "r" and e[2] == "r"):
+                    if n in PSUM and e[3] == q and (q == "t" or kind == "r" and e[2] == "r"):
+                        continue
+                    if not SAME and kind == "w" and e[3] == q and q in "vs":
                         continue
                     toks.append((e[4], e[5], e[6]))
         return toks
@@ -150,61 +167,136 @@ def rank_program(g, core, T, topo):
                 k[o] = max(k.get(o, 0), ov)
 
     def note(q, reads, writes, sem, val, snap):
-        for n, lo, hi in writes:
+        for n, c in parts(writes):
             h = hist.setdefault(n, [])
-            h[:] = [e for e in h if not (lo <= e[0] and e[1] <= hi)]
-            h.append((lo, hi, "w", q, sem, val, snap))
-        for n, lo, hi in reads:
+            h[:] = [e for e in h if not holds(c, e[0])]
+            h.append((c, n, "w", q, sem, val, snap))
+        for n, c in parts(reads):
             h = hist.setdefault(n, [])
-            h[:] = [e for e in h if not (e[2] == "r" and e[3] == q and q in cnt and lo <= e[0] and e[1] <= hi)]
-            h.append((lo, hi, "r", q, sem, val, snap))
-
-    def real(x):
-        return ("kon", KON[x[0]], KON[x[0]] + 1) if x[0] in KON else x
+            h[:] = [e for e in h if not (e[2] == "r" and e[3] == q and q in cnt and holds(c, e[0]))]
+            h.append((c, n, "r", q, sem, val, snap))
 
     def flat(x):
         if not isinstance(x, tuple):
             return []
-        if x[0] == "I":
-            return flat(x[1]) + flat(x[2])
-        x = real(x)
-        return [(x[0], x[1], x[2])]
+        return [x[1], x[2]] if x[0] == "I" else [x]
 
     def ap(x):
         if not isinstance(x, tuple):
             return x
         if x[0] == "I":
             return ap(x[1]).indirect(ap(x[2]))
-        x = real(x)
         if len(x) > 3:
             return T[x[0]][:, x[1]:x[2]:x[3]]
         return T[x[0]][:, x[1]:x[2]]
 
-    def emit(q, fn, outs, ins):
+    def width(x):
+        return 16 * width(x[2]) if x[0] == "I" else len(range(*x[1:]))
+
+    def cost(q, outs, ins, pace):
+        full = [x for x in ins + outs if isinstance(x, tuple)]
+        n = max(width(x) for x in full) if q != "t" else width(outs[0])
+        if any(x[0] == "I" for x in full):
+            return 0.06 + CYCLE * n * (SCATTER if outs[0][0] == "I" else GATHER)
+        if pace is None:
+            narrow = all(x[0] not in PSUM and _S[x[0]][1] in (BF, U16) for x in full if width(x) == n)
+            pace = {"v": 0.5 if narrow else 1, "s": 1, "g": 2, "t": PE}[q]
+        return FIXED[q] + CYCLE * (max(64, n * pace) if q == "v" else max(64, n) * pace if q == "t" else n * pace)
+
+    def emit(q, fn, outs, ins, pace=None):
         reads, writes = [], []
         for x in ins:
             reads += flat(x)
         for x in outs:
-            if isinstance(x, tuple) and x[0] == "I":
-                writes += flat(x[1])
-                reads += flat(x[2])
-            else:
-                writes += flat(x)
-        wait_for(q, deps(q, reads, writes))
-        inst = fn()
-        sem = "q" + q
-        cnt[q] += 1
-        inst.then_inc(T.sem[sem], 1)
-        totals[sem] = cnt[q]
-        snap = dict(known[q])
-        snap[sem] = cnt[q]
-        note(q, reads, writes, sem, cnt[q], snap)
+            writes += flat(x)[:1]
+            reads += flat(x)[1:]
+
+        def issue():
+            wait_for(q, deps(q, reads, writes))
+            inst = fn()
+            sem = "q" + q
+            cnt[q] += 1
+            inst.then_inc(T.sem[sem], 1)
+            totals[sem] = cnt[q]
+            snap = dict(known[q])
+            snap[sem] = cnt[q]
+            note(q, reads, writes, sem, cnt[q], snap)
+        c = cost(q, outs, ins, pace)
+        calls.append((q, issue, reads, writes + row, c, c))
+        del row[:]
+
+    def next_of(name):
+        row.append((name, 0, 1))
+
+    def later(f, *args):
+        n = len(calls)
+        f(*args)
+        aside.update(range(n, len(calls)))
+
+    def in_order():
+        seen, pre = {}, []
+        for i, (q, issue, reads, writes, c, lat) in enumerate(calls):
+            p = set()
+            for kind, regs in (("r", reads), ("w", writes)):
+                for n, c in parts(regs):
+                    p.update(e[2] for e in seen.get(n, ()) if n in PSUM or (meet(c, e[0]) and "w" in (kind, e[1])))
+            for n, c in parts(writes):
+                seen[n] = [e for e in seen.get(n, ()) if not holds(c, e[0])] + [(c, "w", i)]
+            for n, c in parts(reads):
+                seen.setdefault(n, []).append((c, "r", i))
+            pre.append(p - {i})
+        post = [[] for _ in calls]
+        for i, p in enumerate(pre):
+            for j in p:
+                post[j].append(i)
+
+        def gap(j, i):
+            return calls[j][5] + (ACROSS if calls[j][0] != calls[i][0] else 0.0 if calls[j][0] == "t" else WAKE)
+
+        def lay(order, back):
+            at, used = {}, {}
+            for i in order:
+                d = calls[i][4]
+                if back:
+                    t0 = max([calls[i][5] - d] + [at[k] + calls[k][4] + gap(i, k) - d for k in post[i]])
+                else:
+                    t0 = max([0.0] + [at[j] + gap(j, i) for j in pre[i]])
+                u = used.setdefault(calls[i][0], [])
+                n = 0
+                while n < len(u) and u[n][0] < t0 + d:
+                    t0 = max(t0, u[n][1])
+                    n += 1
+                u.insert(n, (t0, t0 + d))
+                at[i] = t0
+            return at
+        order, done = [], set()
+        for i in [i for i in range(len(calls)) if i not in aside] + sorted(aside):
+            stack, need = [i], set()
+            while stack:
+                j = stack.pop()
+                if j not in done and j not in need:
+                    need.add(j)
+                    stack += pre[j]
+            order += sorted(need)
+            done |= need
+        best = None
+        for _ in range(PASSES):
+            at = lay(order, False)
+            end = max(at[i] + calls[i][5] for i in at)
+            if best is None or end < best[0]:
+                best = (end, at)
+            late = lay(sorted(at, key=lambda i: (-at[i] - calls[i][5], -i)), True)
+            order = sorted(late, key=lambda i: (-late[i] - calls[i][4], i))
+            DBG.append(end)
+        for i in sorted(best[1], key=lambda i: (best[1][i], i)):
+            calls[i][1]()
 
     def tc(out, in_):
         emit("v", lambda: g.vector.tensor_copy(out=ap(out), in_=ap(in_)), [out], [in_])
 
     def tt(out, a, b, op):
-        emit("v", lambda: g.vector.tensor_tensor(out=ap(out), in0=ap(a), in1=ap(b), op=op), [out], [a, b])
+        emit("v", lambda: g.vector.tensor_tensor(out=ap(out), in0=ap(a), in1=ap(b), op=op), [out], [a, b],
+             1 if a[0] in PSUM or b[0] in PSUM else 2)
 
     def ts(out, a, s1, op0, s2=None, op1=None):
         if op1 is None:
@@ -213,474 +305,375 @@ def rank_program(g, core, T, topo):
             emit("v", lambda: g.vector.tensor_scalar(out=ap(out), in0=ap(a), scalar1=ap(s1), scalar2=ap(s2), op0=op0, op1=op1),
                  [out], [a, s1, s2])
 
-    def scan(out, d0, d1, op0, op1):
-        emit("v", lambda: g.vector.tensor_tensor_scan(out=ap(out), data0=ap(d0), data1=ap(d1), initial=0.0, op0=op0, op1=op1),
+    def scan(out, d0, d1, op0, op1, first=0.0):
+        emit("v", lambda: g.vector.tensor_tensor_scan(out=ap(out), data0=ap(d0), data1=ap(d1), initial=first, op0=op0, op1=op1),
              [out], [d0, d1])
 
     def fill(out, c):
         emit("v", lambda: g.vector.memset(ap(out), c), [out], [])
 
-    def act(out, in_, func=Fn.Copy, bias=0.0, scale=1.0, accum=None):
-        if accum is None:
-            emit("s", lambda: g.scalar.activation(out=ap(out), in_=ap(in_), func=func, bias=ap(bias), scale=ap(scale)),
-                 [out], [in_, bias, scale])
-        else:
-            emit("s", lambda: g.scalar.activation(out=ap(out), in_=ap(in_), func=func, bias=ap(bias), scale=scale,
-                                                  accum_out=ap(accum)), [out, accum], [in_, bias])
+    def act(out, in_, scale=1.0, bias=0.0, func=None):
+        f = func or (Fn.Identity if isinstance(bias, tuple) else Fn.Copy)
+        emit("s", lambda: g.scalar.activation(out=ap(out), in_=ap(in_), func=f, bias=ap(bias), scale=ap(scale)), [out], [in_, bias, scale])
 
     def mm(out, w, x, start, stop):
         emit("t", lambda: g.tensor.matmul(out=ap(out), lhsT=ap(w), rhs=ap(x), start=start, stop=stop), [out], [w, x])
 
-    def iota(out, pattern, base, mul, flag=False):
-        if flag:
-            emit("g", lambda: g.iota(ap(out), pattern, base, mul, allow_small_or_imprecise_dtypes=True), [out], [])
-        else:
+    def iota(out, pattern, base, mul=0):
+        if _S[out[0]][1] == I32:
             emit("g", lambda: g.iota(ap(out), pattern, base, mul), [out], [])
+        else:
+            emit("g", lambda: g.iota(ap(out), pattern, base, mul, allow_small_or_imprecise_dtypes=True), [out], [])
 
-    def dma(q, out, in_, sem, reads, writes):
-        wait_for(q, deps("dma", reads, writes))
-        Q[q].dma_start(out=out, in_=in_).then_inc(T.sem[sem], 16)
-        totals[sem] = totals.get(sem, 0) + 16
-        note("dma", reads, writes, sem, totals[sem], dict(known[q]))
+    def const(out, c):
+        iota(out, [[0, width(out)]], c)
+
+    def select(out, in_, pattern, op, base, mul):
+        emit("g", lambda: g.affine_select(ap(out), ap(in_), pattern, op, 0.0, base, mul), [out], [in_])
+
+    def dma(q, out, in_, sem, reads, writes, lat):
+        def issue():
+            wait_for(q, deps("dma", reads, writes))
+            Q[q].dma_start(out=out, in_=in_).then_inc(T.sem[sem], 16)
+            totals[sem] = totals.get(sem, 0) + 16
+            note("dma", reads, writes, sem, totals[sem], dict(known[q]))
+        calls.append((q, issue, reads, writes, 0.05, lat))
+
+    def pick(win, offs):
+        return ("I", win, offs)
 
     near = [T.rank_of(d) for d in plan(core, T, topo)[0]]
-    order = [r] + near + [q for q in range(N) if q != r and q not in near]
-    first, last = order[:1 + len(near)], order[1 + len(near):]
+    far = [q for q in range(N) if q != r and q not in near]
 
-    def send(b, grp):
-        wait_for("g", deps("g", [(buf, BL * b, BL * (b + 1)) for buf, s in grp], []))
-        for call in legs(core, T, topo, len(grp)):
-            tr = []
-            for d, j, eng in call:
-                rid, pid = topo.addr(d, core)
-                piece = T[grp[j][0]][:, BL * b:BL * (b + 1)]
-                tr.append(RemoteDMATransfer(dst_ids=[DstId(rid=rid, pnc=pid)], dma_engine_mask=bits(eng),
-                                            remote_sem=T.sem["%s%d" % (grp[j][1], b)], srcs=[piece], dsts=[piece]))
-                totals["loc"] = totals.get("loc", 0) + len(eng)
-            g.remote_dma_fused(tr, local_sem=T.sem.loc)
+    def send(t, j):
+        cols, sem = messages(t, r)[j]
 
-    for t in range(ROUNDS):
-        for q, src in enumerate(T.cores):
-            for grp in groups(t):
-                got = [(j, eng) for call in legs(src, T, topo, len(grp)) for d, j, eng in call if d == core]
-                got += [y for x, d in plan(src, T, topo)[1] if d == core for y in onward(x, core, topo, len(grp))]
-                for j, eng in got:
-                    buf, s = grp[j]
-                    b = 4 * t + q
-                    note("net", [], [(buf, BL * b, BL * (b + 1))], "%s%d" % (s, b), len(eng), {})
-                    totals["%s%d" % (s, b)] = len(eng)
+        def issue():
+            wait_for("g", deps("g", [cols], []))
+            left = "l" + sem
+            for call in legs(core, T, topo):
+                g.remote_dma_fused([transfer(T, topo, core, d, eng, cols, sem) for d, eng in call], local_sem=T.sem[left])
+                totals[left] = totals.get(left, 0) + sum(len(eng) for d, eng in call)
+            note("net", [cols], [], left, totals[left], {})
+        sent = [("sent", len(calls), len(calls) + 1)]
+        calls.append(("g", issue, [cols], [("sends", 0, 1)] + sent, 0.5, 0.5))
+        for q in near + far:
+            src = T.cores[q]
+            got = [len(eng) for call in legs(src, T, topo) for d, eng in call if d == core]
+            got += [len(topo.engines(x, core)) for x, d in plan(src, T, topo)[1] if d == core]
+            land, s = messages(t, q)[j]
+            totals[s] = got[0]
+            calls.append(("net", lambda a=([land], s, got[0]): note("net", [], a[0], a[1], a[2], {}), sent, [land],
+                          0.0, HOP * (1 if q in near else 2) * (1.8 if t == 0 else 1)))
 
     c0s = [(8 * t + 2 * r) % 16 for t in range(2)]
 
-    def classes(n, st):
-        return [(n, c0s[st] + m, 16 * (H - 1) + c0s[st] + m + 1, 16) for m in range(2)]
+    def classes(st):
+        return [((m * H, (m + 1) * H), ("nm", c0s[st] + m, 16 * (H - 1) + c0s[st] + m + 1, 16)) for m in range(2)]
 
-    def consts_v():
-        fill(("o16", 0, 128), -0.0625)
-        fill(("c32c", 0, 1), float(CAP))
-        ts(("cki", 0, 512), ("col", 0, 512), 15, Op.bitwise_and)
-        ts(("dg", 0, 256), ("cki", 0, 256), ("p15", 0, 1), Op.is_equal)
-        for lo, hi in ((0, 512), (512, 1024)):
-            ts(("seg", lo, hi), ("cki", 0, 512), 0.0, Op.is_gt)
-        fill(("neg1", 0, 1), -1.0)
-        fill(("half", 0, 1), 0.5)
-        fill(("mbig", 0, 1), -3.0e7)
+    def lx(t):
+        return L + CAP * (1 + t // 2)
 
-    def consts_v2():
-        for t in range(1, ROUNDS):
-            fill(("ln", BL * (4 * t + r), BL * (4 * t + r) + 4), 0.0)
-        for n in ("e1", "ns1"):
-            fill((n, L, LX), 0.0)
-        for i in range(2):
-            fill(("lv%d" % i, L, LX), float(V))
-        fill(("qf0", L, LX), float(V))
-        ts(("kp", 0, 512), ("cki", 0, 512), -512.0, Op.mult, 7680.0, Op.add)
-        ts(("c32", 0, 64), ("col", 0, 64), 31, Op.bitwise_and)
-        ts(("seg32", 0, 64), ("c32", 0, 64), 0.0, Op.is_gt)
-        for c in range(2):
-            ts(("dmp", c, c + 1), ("sc", c, c + 1), 576.0, Op.add)
-            ts(("tri", 32 * c, 32 * c + 32), ("col", 0, 32), ("sc", c, c + 1), Op.is_lt, ("dmp", c, c + 1), Op.mult)
-        for n in ("jwa", "jwb", "jwc"):
-            ts((n, 0, 32), ("jwf", 0, 32), ("p15", 0, 1), Op.add)
+    P15 = ("sc", 0, 1)
+    PLW = ("plw", 0, 2)
 
-    def consts_g():
-        iota(("jwf", 0, 32), [[BL, 16], [16, 2]], 4, 0, True)
-        iota(("en", 0, G0), [[0, G0]], 0, 0, True)
-        iota(("rs", 0, G0), [[0, G0]], -SHIFT - 16384, 0, True)
-        iota(("idc", 0, 512), [[BL, 16], [1, 32]], 4 - SHIFT, 0, True)
-        iota(("w", 0, IDW), [[1, IDW]], -SHIFT, 0, True)
-        iota(("vn", 0, G0), [[-1, G0]], V, 0, True)
-        iota(("jt", 0, VT), [[1, VT]], 0, 0, True)
-        iota(("vid", 0, IDW), [[0, IDW]], 0, 0, True)
-
-    def names_again(st, lo, hi):
-        act(("qr%d" % st, 16 * lo, 16 * hi), ("I", ("qf%d" % st, 0, LX), ("lrep", lo, hi)), Fn.Identity, ("c1280", 0, 1), -1.0)
-
-    def consts_s():
-        names_again(1, H, L)
-        act(("i1280", 0, 128), ("idn", 0, 128), Fn.Copy, 0.0, 1280.0)
-        act(("bd8", 0, 128), ("bd", 0, 128), Fn.Copy, 0.0, 8192.0)
-        act(("kb", 0, 512), ("seg", 0, 512), Fn.Identity, ("mbig", 0, 1), 6.0e7)
+    def constants():
+        iota(("pii", 0, 2), [[0, 2]], 0, 1)
+        iota(("c16", 0, 2), [[16, 2]], 0)
+        ts(("pij", 0, 2), ("pii", 0, 2), 15, Op.bitwise_and)
+        tt(("sc", 0, 2), ("pij", 0, 2), ("c16", 0, 2), Op.add)
+        fill(("one", 0, 128), 1.0)
+        select(("idn", 0, 128), ("one", 0, 128), [[-1, 128]], Op.is_equal, 0, 1)
+        select(("bdh", 0, 128), ("one", 0, 128), [[-16, 8], [0, 16]], Op.is_ge, 0, 1)
+        select(("bd", 0, 128), ("bdh", 0, 128), [[16, 8], [0, 16]], Op.is_ge, 15, -1)
+        for st in range(2):
+            iota(("nl%d" % st, 0, L), [[-1, 2], [-16, H]], V - c0s[st])
+            for n, c in (("nl", 0.0), ("of", 0.0), ("qf", float(V))):
+                fill((n + str(st), L, LX), c)
+        iota(("lid", 0, LX), [[1, LX]], 0)
+        fill(("xm", V, V + 16), 0.0)
+        fill(("hit", L, L + CAP), 1.0)
+        fill(("c255", 0, LX), 255.0)
+        fill(("deg", L, LX), 0)
+        fill(("z", L, LX), 0.0)
+        fill(("sgl", 0, 2 * LX), 1.0)
+        fill(("sgl", lx(0), lx(0) + 1), 0.0)
+        for t in range(ROUNDS):
+            const(block(t, r, VARS[t] + 2 + 8 * t, 2), 0)
+        for t in range(ROUNDS - 1):
+            for q in range(N):
+                lo = block(t, q, 0 if SIZES[t] else 32)[1]
+                const(("ln", lo, lo + WIDE[t] - 32), 0)
+        tc(("limf", 0, 1), ("limi", 0, 1))
+        tc(("lima", 0, 1), ("limi", 0, 1))
+        const(("en", 0, G0), -1)
+        const(("rs", 0, G0), -SHIFT - 16384)
+        iota(("idt", 0, CW), [[1, CW]], -ID0 - SHIFT)
+        iota(("jt", 0, VT), [[1, VT]], 0)
+        iota(("ck", 0, 16), [[1, 16]], 0)
+        ts(("qsc", 0, 16), ("ck", 0, 16), P15, Op.not_equal, -1.0, Op.mult)
+        ts(("qbi", 0, 16), ("qsc", 0, 16), -1281.0, Op.mult, -1.0, Op.add)
+        ts(("wsc", 0, 16), ("qsc", 0, 16), 19200.0, Op.mult, 20480.0, Op.add)
         for k in range(16):
-            act(("dk", 128 * k, 128 * k + 128), ("idn", 0, 128), Fn.Copy, 0.0, ("dg", k, k + 1))
-        act(("idead", 0, 128), ("idn", 0, 128), Fn.Copy, 0.0, -32768.0)
-        act(("ipen", 0, 128), ("idn", 0, 128), Fn.Copy, 0.0, -64.0)
+            o = ("dk", 128 * k, 128 * k + 128)
+            if k % 2:
+                ts(o, ("idn", 0, 128), ("wsc", k, k + 1), Op.mult)
+            else:
+                act(o, ("idn", 0, 128), ("wsc", k, k + 1))
+        for n, c in (("idead", -20480.0), ("imx", -1.0 / 4096), ("ipen", -32.0)):
+            act((n, 0, 128), ("idn", 0, 128), c)
+        act(("bd8", 0, 128), ("bd", 0, 128), -2.0)
+        act(("o16", 0, 128), ("one", 0, 128), -0.0625)
+        const(("dead1", 0, L), 1)
+        fill(("seg", 0, 1024), 1.0)
+        fill(("seg", 0, 1024, 16), 0.0)
+        const(("kb", 0, 512), 512)
+        fill(("kb", 0, 512, 16), -6.0e7)
+        const(("c1", 0, 768), 1)
+        iota(("revf", 0, 48), [[0, 24], [-16, 2]], 31)
+        ts(("rev", 0, 48), ("revf", 0, 48), P15, Op.subtract)
+        iota(("repi", 0, 48), [[1, 24], [0, 2]], 0)
+        tc(("rep", 0, 48), ("repi", 0, 48))
+        for t in range(ROUNDS):
+            iota(("jb", 8 * t, 8 * t + 8), [[WIDE[t], 4], [16, 2]], START[t] + SIZES[t] + (VAL if t < 3 else 0))
+            ts(("jf%d" % t, 8 * t, 8 * t + 8) if t < 3 else ("j3", 0, 8), ("jb", 8 * t, 8 * t + 8), P15, Op.add)
 
-    def sums(buf, lo, hi):
+    def lanes_of(st):
+        for (lo, hi), x in classes(st):
+            tc(("qu%d" % st, lo, hi), x)
+        n = len(calls)
+        for (lo, hi), x in classes(st):
+            act(("of%d" % st, lo, hi), x, -1.0, float(V))
+        for (lo, hi), x in classes(st):
+            act(("qf%d" % st, lo, hi), x)
         for k in range(16):
-            mm(("bdeg", lo, hi), ("idn", 0, 128), (buf, 16 * lo + k, 16 * (hi - 1) + k + 1, 16), k == 0, k == 15)
+            o, i = ("qr%d" % st, k, 16 * (L - 1) + k + 1, 16), ("qf%d" % st, 0, L)
+            if k % 3 < st:
+                ts(o, i, ("qsc", k, k + 1), Op.mult, ("qbi", k, k + 1), Op.add)
+            else:
+                act(o, i, ("qsc", k, k + 1), ("qbi", k, k + 1))
+        aside.update(range(n, len(calls)))
+
+    def sums(lo, hi, stop):
+        for k in range(16):
+            mm(("d0", lo, hi), ("idn", 0, 128), ("xv", 16 * lo + k, 16 * (hi - 1) + k + 1, 16), k == 0, stop and k == 15)
 
     def hits(t):
-        st, old = t % 2, 4 * (t - 1)
-        if t > 0:
-            put("rs", old, old + 4, ("ksn", 0, 128))
+        st, n = t % 2, lx(t)
         if t == 0:
-            ts(("ok", 0, L), ("bdeg", 0, L), ("limf", 0, 1), Op.is_le)
+            ts(("ok", 0, L), ("d0", 0, L), ("lima", 0, 1), Op.is_le)
+            later(tc, ("deg", 0, L), ("d0", 0, L))
         else:
-            tt(("ok", 0, L), ("bdeg", 0, L), ("lmx", 0, L), Op.is_le)
+            tc(("si", 0, L), ("d0", 0, L))
+            ts(("deg", 0, L), ("si", 0, L), 4095, Op.bitwise_and)
+            ts(("ok", 0, L), ("deg", 0, L), ("lima", 0, 1), Op.is_le)
         if t >= 2:
             mm(("bhit", 0, L), ("ipen", 0, 128), ("dead%d" % st, 0, L), True, False)
         mm(("bhit", 0, L), ("bd", 0, 128), ("ok", 0, L), t < 2, True)
-        ts(("hit", 0, L), ("bhit", 0, L), 9.0, Op.is_ge)
-        scan(("cum", 0, LX), ("hit", 0, LX), ("c255", 0, LX), Op.add, Op.min)
+        ts(("hit", 0, L), ("bhit", 0, L), 9.0 if t < 2 else -23.0, Op.is_ge)
+        scan(("cum", 0, n), ("hit", 0, n), ("c255", 0, n), Op.add, Op.min)
         for c in range(2):
-            act(("sg", c * LX, (c + 1) * LX), ("cum", 0, LX), Fn.Sign, ("sh", c, c + 1), -1.0, ("pla", c, c + 1))
-        if t == 0:
-            ts(("deg", 0, L), ("bdeg", 0, L), -1.0, Op.mult, ("limf", 0, 1), Op.add)
-        else:
-            tt(("deg", 0, L), ("lmx", 0, L), ("bdeg", 0, L), Op.subtract)
-        if t > 1:
-            put("rs", 0, old, ("jr", 0, 32 * old))
-        ts(("plw", 0, 2), ("pla", 0, 2), 0.5, Op.mult, float(LX // 2), Op.add)
+            ts(("sg", c * n, (c + 1) * n), ("cum", 0, n), ("sc", c, c + 1), Op.is_le)
+        scan(("sn", 0, 2 * n), ("sgl", 0, 2 * n), ("sg", 0, 2 * n), Op.mult, Op.add)
+        tc(PLW, ("sn", n - 1, 2 * n, n))
 
     def variables(t):
-        st, b = t % 2, 4 * t + r
-        act(("vy", 0, 2), ("pla", 0, 2), Fn.Sign, ("c33", 0, 1))
-        act(("vx", 0, 2), ("vy", 0, 2), Fn.Identity, ("kv%d" % st, 0, 1), (1 - V) / 2.0)
-        for c in range(2):
-            act(("la", BL * b + c, BL * b + c + 1), ("pla", c, c + 1), Fn.Identity, ("vx", c, c + 1), 8.0)
+        n = lx(t)
+        ts(("vy", 0, 2), ("sn", n - 1, 2 * n, n), float(H), Op.is_ge, 1.0 - V, Op.mult)
+        ts(("vx", 0, 2), ("sn", n - 1, 2 * n, n), 16.0, Op.mult, float(c0s[t % 2]), Op.add)
+        ts(block(t, r, SIZES[t], 32), pick(("deg", 0, LX), PLW), -1.0, Op.mult, -255.0, Op.max)
+        tt(block(t, r, VARS[t], 2), ("vx", 0, 2), ("vy", 0, 2), Op.add)
 
-    def sizes(t):
-        b = 4 * t + r
-        ts(("la", BL * b + 4, BL * (b + 1)), ("I", ("deg", 0, LX), ("plw", 0, 2)), ("limb", 0, 1), Op.subtract, -256.0, Op.max)
+    def after(t):
+        if t < ROUNDS - 1:
+            act(("a1", 0, 1), ("cum", L - 1, L), -1.0, float(CAP), Fn.Relu)
+            mm(("bhit", 0, 1), ("o16", 0, 128), ("a1", 0, 1), True, True)
+            tc(("ai", 0, 1), ("bhit", 0, 1))
+            ts(("aj", 0, 1), ("ai", 0, 1), 7, Op.bitwise_and)
+            tt(("lima", 0, 1), ("limf", 0, 1), ("aj", 0, 1), Op.add)
+        if t < 2:
+            ts(("piv", 0, L), ("cum", 0, L), float(CAP), Op.is_le, 2.0, Op.mult)
+            tt(("pih", 0, L), ("piv", 0, L), ("hit", 0, L), Op.mult)
+            act(("dead%d" % t, 0, L), ("pih", 0, L), 1.0, 1.0)
+        if t == 1:
+            const(("hit", L, L + CAP), 0)
+            const(("hit", L + CAP, LX), 1)
+            const(("sgl", lx(0), lx(0) + 1), 1)
+            const(("sgl", LX, LX + 1), 0)
 
-    def dead_of(t):
-        ts(("piv", 0, L), ("cum", 0, L), float(CAP), Op.is_le)
-        tt(("dead%d" % t, 0, L), ("piv", 0, L), ("hit", 0, L), Op.mult)
-
-    def count(t):
-        act(("a1", 0, 1), ("cum", L - 1, L), Fn.Relu, ("c32c", 0, 1), -1.0)
-        mm(("bhit", 0, 1), ("o16", 0, 128), ("a1", 0, 1), True, True)
-
-    def limits(t):
-        tc(("ai", 0, 1), ("bhit", 0, 1))
-        ts(("aj", 0, 1), ("ai", 0, 1), 7, Op.bitwise_and)
-        tt(("lima", 0, 1), ("limf", 0, 1), ("aj", 0, 1), Op.add)
-        ts(("limb", 0, 1), ("lima", 0, 1), 1.0, Op.add)
-
-    def list_v(b):
-        tc(("evu", 2 * b, 2 * b + 2), ("la", BL * b, BL * b + 2))
-
-    def list_c(b):
-        tc(("cwu", 2 * b, 2 * b + 2), ("la", BL * b + 2, BL * b + 4))
-
-    def put(table, lo, hi, src):
-        tc(("I", (table, 0, VT), ("evu", 2 * lo, 2 * hi)), src)
-
-    def put_names(b):
-        o, i = ("I", ("nm", 0, VT), ("evu", 2 * b, 2 * b + 2)), ("ln", BL * b + 4, BL * (b + 1))
-        ts(o, i, -1.0, Op.mult, float(V), Op.add)
-
-    def size_of(b):
-        i = 32 * (b % 4)
-        act(("xt", i, i + 32), ("la", BL * b + 4, BL * (b + 1)), Fn.Identity, ("neg1", 0, 1), -1.0)
-
-    def outputs(t):
-        for q in range(N):
-            b = 4 * t + q
-            i = 32 * q
-            act(("nt", i, i + 32), ("ln", BL * b + 4, BL * (b + 1)), Fn.Identity, ("c1280", 0, 1), -1.0)
-            act(("vid", BL * b + 4, BL * (b + 1)), ("I", ("jt", 0, VT), ("evu", 2 * b, 2 * b + 2)))
-        put("nm", 4 * t, 4 * t + 4, ("nt", 0, 128))
-        put("xo", 4 * t, 4 * t + 4, ("xt", 0, 128))
-
-    def picks(t):
-        st = t % 2
-        for lo, hi in CH:
-            act(("xg", 16 * lo, 16 * hi), ("I", ("xm", 0, G0), ("qu%d" % st, lo, hi)))
-
-    def self_picks():
-        for k in range(16):
-            mm(("bself", 0, L), ("dk", 128 * k, 128 * k + 128), ("xg", k, 16 * (L - 1) + k + 1, 16), k == 0, k == 15)
+    def put(table, n, src, lo=0):
+        tc(pick((table, 0, VT), ("evu", lo // 16, (lo + n) // 16)), src)
 
     def main(t):
-        st, old = t % 2, 4 * (t - 1)
+        st = t % 2
+        qu, qn = LISTS[t]
 
         def cover(c):
             lo, hi = CH[c]
-            tt(("eq", 16 * lo, 16 * hi), ("I", ("en", 0, G0), ("qu%d" % st, lo, hi)), ("qr%d" % st, 16 * lo, 16 * hi), Op.is_equal)
-            if t >= 2:
-                mm((PSUM[c], 0, hi - lo), ("idead", 0, 128), ("dead%d" % st, lo, hi), True, False)
+            bank = ("b%d" % (c % 3), 0, hi - lo)
+            next_of("covers")
+            tt(("eq", 16 * lo, 16 * hi), pick(("en", 0, G0), (qu, lo, hi)), ("qr%d" % st, 16 * lo, 16 * hi), Op.is_equal)
+            mm(bank, ("idead", 0, 128), ("dead%d" % st, lo, hi), True, False)
             for k in range(16):
-                mm((PSUM[c], 0, hi - lo), ("i1280", 0, 128), ("eq", 16 * lo + k, 16 * (hi - 1) + k + 1, 16), t < 2 and k == 0, k == 15)
+                if k == 15 and hi == L:
+                    next_of("sums")
+                mm(bank, ("dk", 128 * k, 128 * k + 128), ("eq", 16 * lo + k, 16 * (hi - 1) + k + 1, 16), False, k == 15)
 
         def uncovered(c):
             lo, hi = CH[c]
-            tt(("q2", lo, hi), ("qf%d" % st, lo, hi), (PSUM[c], 0, hi - lo), Op.max)
-            ts(("qn", lo, hi), ("q2", lo, hi), float(V), Op.min)
+            bank = ("b%d" % (c % 3), 0, hi - lo)
+            tt(("q2", lo, hi), ("qf%d" % st, lo, hi), bank, Op.max)
+            ts((qn, lo, hi), ("q2", lo, hi), float(V), Op.min)
+            later(act, ("z", lo, hi), bank, 1.0, 0.0, Fn.Abs)
+            for f, a, z in ((act, lo, hi - PART[c]), (tc, hi - PART[c], hi)):
+                if a < z:
+                    if f is act:
+                        next_of("picks")
+                    f(("xv", 16 * a, 16 * z), pick(("xm", 0, G0), (qn, a, z)))
 
-        def pick(c, on):
+        def degrees(c):
             lo, hi = CH[c]
-            o, i = ("xv", 16 * lo, 16 * hi), ("I", ("xm", 0, G0), ("qn", lo, hi))
-            if on == "s":
-                act(o, i, Fn.Relu)
-            else:
-                ts(o, i, 0.0, Op.max)
-
-        def largest(c):
-            lo, hi = CH[c]
-            scan(("msc", 16 * lo, 16 * hi), ("seg", 0, 16 * (hi - lo)), ("xg", 16 * lo, 16 * hi), Op.mult, Op.min)
+            scan(("msc", 16 * lo, 16 * hi), ("seg", 0, 16 * (hi - lo)), ("xv", 16 * lo, 16 * hi), Op.mult, Op.min)
+            next_of("sums")
+            sums(lo, hi, False)
+            mm(("d0", lo, hi), ("imx", 0, 128), ("msc", 16 * lo + 15, 16 * hi, 16), False, True)
 
         cover(0)
-        tt(("ksn", 0, 128), ("idc", 32 * old, 32 * old + 128), ("bkey", 0, 128), Op.add)
-        cover(1)
-        uncovered(0)
-        pick(0, "s")
-        cover(2)
-        uncovered(1)
-        pick(1, "s")
-        sums("xv", *CH[0])
-        largest(0)
-        uncovered(2)
-        pick(2, "v")
-        largest(1)
-        largest(2)
-        ts(("lmx", 0, L), ("msc", 15, 16 * L, 16), ("limb", 0, 1), Op.add, ("lima", 0, 1), Op.min)
-        for q in range(N):
-            act(("ksl", BL * (old + q) + 4, BL * (old + q + 1)), ("ksn", 32 * q, 32 * q + 32))
-        if t > 1:
-            act(("jr", 0, 32 * old), ("I", ("ksl", 0, BL * (old + 4)), (("jwb", "jwc")[t - 2], 0, 2 * old)))
-        for c in range(2):
-            tc(("evu", 2 * old + c, 2 * old + 7 + c, 2), ("la", BL * old + c, BL * (old + 3) + c + 1, BL))
-        sums("xv", *CH[2])
-        sums("xv", *CH[1])
+        for c in range(len(CH)):
+            if c + 1 < len(CH):
+                cover(c + 1)
+            elif KEYS == 0:
+                keys(t)
+            uncovered(c)
+        for c in range(len(CH)):
+            degrees(c)
+        if KEYS == 1:
+            keys(t)
+        if KEYS == 2:
+            later(keys, t)
 
     def pivots(t):
-        st, b = t % 2, 4 * t + r
-
-        def keys():
-            tt(("key", 0, 512), ("I", ("rs", 0, G0), ("qp", 0, 32)), ("kp", 0, 512), Op.add)
-            scan(("ksc", 0, 512), ("kb", 0, 512), ("key", 0, 512), Op.min, Op.max)
-
-        def own_gathers():
-            self_picks()
-            act(("esg", 0, L), ("bself", 0, L), Fn.Sign, ("half", 0, 1))
-            act(("e1", 0, L), ("esg", 0, L), Fn.Relu, 0.0, float(V))
-            act(("ocx", 0, L), ("q2", 0, L), Fn.Identity, ("c1280", 0, 1), -1.0)
-            act(("e1p", 0, 32), ("I", ("e1", 0, LX), ("plw", 0, 2)))
-
-        def names():
-            tt(("b0", 0, 512), ("xn", 0, 512), ("b1", 0, 512), Op.not_equal)
-            tt(("cc", 0, 512), ("xn", 0, 512), ("b0", 0, 512), Op.mult)
-            scan(("nsc", 0, 512), ("seg", 0, 512), ("cc", 0, 512), Op.mult, Op.max)
-            tt(("ocp", 0, 32), ("I", ("ocx", 0, LX), ("plw", 0, 2)), ("e1p", 0, 32), Op.min)
-            tt(("ocq", 0, 32), ("I", ("ns%d" % st, 0, LX), ("plw", 0, 2)), ("ocp", 0, 32), Op.mult)
-            tt(("ln", BL * b + 4, BL * (b + 1)), ("ocq", 0, 32), ("nsc", 15, 512, 16), Op.max)
-            send(b, [("ln", "n")])
-
-        def claims():
-            tc(("mi", 0, 32), ("ksc", 15, 512, 16))
-            ts(("mj", 0, 32), ("mi", 0, 32), 511, Op.bitwise_and)
-            tt(("kd", 0, 32), ("mj", 0, 32), ("dg", 0, 32), Op.mult)
-            scan(("kw", 0, 32), ("seg", 0, 32), ("kd", 0, 32), Op.mult, Op.add)
-            for c in range(2):
-                ts(("ke", 32 * c, 32 * c + 32), ("mj", 0, 32), ("kw", 16 * c + 15, 16 * c + 16), Op.is_equal)
-            tt(("kf", 0, 64), ("ke", 0, 64), ("tri", 0, 64), Op.mult)
-            scan(("kg", 0, 64), ("seg32", 0, 64), ("kf", 0, 64), Op.mult, Op.max)
-            tt(("la", BL * b + 2, BL * b + 4), ("kw", 15, 32, 16), ("kg", 31, 64, 32), Op.max)
-            send(b, [("la", "a")])
-
-        tc(("qp", 0, 32), ("I", ("qf%d" % st, 0, LX), ("plw", 0, 2)))
-        act(("xn", 0, 512), ("I", ("en", 0, G0), ("qp", 0, 32)))
-        keys()
-        tc(("vp", 0, 32), ("I", ("lv%d" % st, 0, LX), ("plw", 0, 2)))
+        st, n = t % 2, 256 * t
+        nl = ("nl%d" % st, 0, LX)
+        tc(("qp", 0, 32), pick(("qf%d" % st, 0, LX), PLW))
+        act(("key", 0, 512), pick(("rs", 0, G0), ("qp", 0, 32)))
+        tc(("vp", 0, 32), pick(("lid", 0, LX), PLW))
         variables(t)
-        if t < ROUNDS - 1:
-            count(t)
-        act(("vr", 0, 512), ("I", ("vn", 0, G0), ("vp", 0, 32)))
-        act(("b1", 0, 512), ("vr", 0, 512))
-        own_gathers()
-        sizes(t)
-        claims()
-        if t < ROUNDS - 1:
-            limits(t)
-        if t < 2:
-            dead_of(t)
-        names()
+        act(("vr", 0, 512), pick(nl, ("vp", 0, 32)))
+        act(("vr", 512, 544), pick(nl, PLW))
+        act(("b1", 0, 544), ("vr", 0, 544))
+        act(("xn", 0, 512), pick(("en", 0, G0), ("qp", 0, 32)))
+        act(("zp", 0, 32), pick(("z", 0, LX), PLW), -1.0)
+        if t == ROUNDS - 1:
+            later(act, block(t, r, FREE, 32), ("vr", 512, 544), -1.0, float(V))
+        scan(("ksc", 0, 512), ("kb", 0, 512), ("key", 0, 512), Op.add, Op.max)
+        tc(("mi", 0, 32), ("ksc", 15, 512, 16))
+        ts(("mj", 0, 32), ("mi", 0, 32), 511, Op.bitwise_and)
+        later(act, ("rho", 0, n), pick(("jf%d" % (t - 1), 0, 8 * t), ("rep", 0, 16 * t)), 1.0, float(-VAL - ID0))
+        later(fill, ("c1", 31, n, 32), float(VAL + block(t, r, FREE if t == ROUNDS - 1 else SIZES[t])[1]))
+        tt(("ne", 0, n), pick(("mj", 0, 32), ("rev", 0, 16 * t)), ("rho", 0, n), Op.not_equal)
+        scan(("fc", 0, n), ("ne", 0, n), ("c1", 0, n), Op.mult, Op.add, float(VAL))
+        tt(block(t, r, CLAIMS[t], 8 * t), ("fc", 31, n, 32), ("jf%d" % (t - 1), 0, 8 * t), Op.min)
+        send(t, 0)
+        tt(("xn", 512, 544), pick(("of%d" % st, 0, LX), PLW), ("zp", 0, 32), Op.add)
+        tt(("b0", 0, 544), ("xn", 0, 544), ("b1", 0, 544), Op.not_equal)
+        tt(("cc", 0, 544), ("xn", 0, 544), ("b0", 0, 544), Op.mult)
+        scan(("nsc", 0, 512), ("seg", 0, 512), ("cc", 0, 512), Op.mult, Op.max)
+        tt(names_of(t, r), ("cc", 512, 544), ("nsc", 15, 512, 16), Op.max)
+        send(t, 1)
 
     def kept_rows(t):
-        st = t % 2
-        tt(("b1", 0, L), ("qf%d" % st, 0, L), ("e1", 0, L), Op.max)
+        o = ("of1" if t == 1 else "ocx", 0, L)
+        act(o, ("q2", 0, L), -1.0, float(V), Fn.Relu)
         if t == 1:
-            tt(("qf1", 0, L), ("q2", 0, L), ("b1", 0, L), Op.min)
-            tc(("qu1", 0, L), ("qf1", 0, L))
+            act(("qf1", 0, L), o, -1.0, float(V))
         else:
-            tt(("q3", 0, L), ("q2", 0, L), ("b1", 0, L), Op.min)
-            for m, x in enumerate(classes("nm", st)):
-                act(x, ("q3", m * H, (m + 1) * H))
+            for (lo, hi), x in classes(t % 2):
+                act(x, ("ocx", lo, hi), -1.0, float(V))
+
+    def roots(t):
+        if t > 0:
+            lists = [block(t, q, CLAIMS[t], 8 * t) for q in [r] + near + far]
+            tt(("m0", 0, 8 * t), lists[0], lists[1], Op.min)
+            tt(("m1", 0, 8 * t), lists[2], lists[3], Op.min)
+            tt(("jf%d" % t, 0, 8 * t), ("m0", 0, 8 * t), ("m1", 0, 8 * t), Op.min)
+        k = min(8 * t + 8, 24)
+        ts(("ju%d" % t, 0, k), ("jf%d" % t, 0, k), float(-VAL - START[t]), Op.add)
+        for c in range(2):
+            lo = START[t] + VARS[t] + c
+            tc(("evu", 8 * t + c, 8 * t + 7 + c, 2), ("la", lo, lo + 3 * WIDE[t] + 1, WIDE[t]))
 
     def update(t):
-        jo, jn = (None, "jwa", "jwb")[t], (None, "jwb", "jwc")[t]
-        old = 4 * t
-        n = 32 * old
+        n = 128 * (t + 1)
+        ju = ("ju%d" % t, 0, n // 16)
+        xr, er = ("xr%d" % t, 0, n), ("er%d" % t, 0, n)
+        roots(t)
+        act(xr, pick(("la", START[t], CW), ju), 4096.0)
+        next_of("roots")
+        act(er, pick(("ln", START[t], CW), ju))
+        put("xm", n, xr)
+        put("en", n, er)
+        mm(("bkey", 0, n), ("bd8", 0, 128), xr, True, True)
+        next_of("roots")
+        act(("bk", 0, n), ("bkey", 0, n))
+        next_of("roots")
+        act(("idr", 0, n), pick(("idt", START[t], CW), ju))
+        later(act, ("xt", n - 128, n), (xr[0], n - 128, n), -1.0 / 4096)
+        later(act, ("nt", n - 128, n), (er[0], n - 128, n), -1.0, float(V))
 
-        def place(table, b, src):
-            tc(("I", (table, 0, VT), ("vc", 4 * b, 4 * b + 2)), src)
+    def keys(t):
+        n = 128 * t
+        tt(pick(("rs", 0, VT), ("evu", 0, n // 16)), ("idr", 0, n), ("bk", 0, n), Op.add)
 
-        def land(qs, lists, sz, nms):
-            for q in qs:
-                b = 4 * t + q
-                if lists:
-                    tc(("vc", 4 * b, 4 * b + 4), ("la", BL * b, BL * b + 4))
-                    size_of(b)
-                if sz:
-                    place("xm", b, ("la", BL * b + 4, BL * (b + 1)))
-                if nms:
-                    place("en", b, ("ln", BL * b + 4, BL * (b + 1)))
+    dma("y", T["nm"][:, 0:V], T.nb[:, :], "dn", [], [("nm", 0, V)], 3.8)
+    dma("s", T["xm"][:, 0:V], T.xs[:, :], "dx", [], [("xm", 0, V)], 3.8)
+    dma("s", T["limi"][:, 0:1], T.lim[:, 0:1], "dl", [], [("limi", 0, 1)], 3.8)
+    dma("y", T["xo"][:, 0:V], T.xs[:, :], "do", [("limi", 0, 1)], [("xo", 0, V)], 3.0)
+    later(constants)
 
-        land(first, True, True, False)
-        land(first, False, False, True)
-        land(last, True, t == 0, False)
-        mm(("bkey", 0, 128), ("bd8", 0, 128), ("xt", 0, 128), True, True)
-        if t > 0:
-            for q in (3, 2, 1, 0):
-                b = 4 * t + q
-                tc(("I", ("w", 0, IDW), ("vc", 4 * b + 2, 4 * b + 4)), ("idc", 32 * b, 32 * b + 32))
-            tt(("jd", 0, n), ("I", ("w", 0, IDW), (jo, 0, 2 * old)), ("dg", 0, n), Op.mult)
-            scan(("js", 0, n), ("seg", 0, n), ("jd", 0, n), Op.mult, Op.add)
-            ts((jn, 0, 2 * old), ("js", 15, n, 16), float(SHIFT), Op.add)
-            act(("xr", 0, n), ("I", ("la", 0, BL * (old + 4)), (jn, 0, 2 * old)))
-            land(last, False, True, False)
-            put("xm", 0, old, ("xr", 0, n))
-        picks(t + 1)
-        land(last, False, False, True)
-        if t > 0:
-            tc(("er", 0, n), ("I", ("ln", 0, BL * (old + 4)), (jn, 0, 2 * old)))
-            put("en", 0, old, ("er", 0, n))
-
-    dma("y", T["nm"][:, 0:V], T.nb[:, :], "dn", [], [("nm", 0, V)])
-    dma("s", T["xm"][:, 0:V], T.xs[:, :], "dx", [], [("xm", 0, V)])
-    dma("s", T["limi"][:, 0:1], T.lim[:, 0:1], "dl", [], [("limi", 0, 1)])
-    wait_for("y", [("dn", 16, {})])
-    dma("y", T["xo"][:, 0:V], T.xs[:, :], "do", [], [("xo", 0, V)])
-    iota(("pii", 0, 1), [[1, 1]], 0, 1)
-    iota(("col", 0, 512), [[1, 512]], 0, 0)
-    fill(("one", 0, 128), 1.0)
-    emit("g", lambda: g.affine_select(T["idn"][:, :], T["one"][:, :], [[-1, 128]], Op.is_equal, 0.0, 0, 1),
-         [("idn", 0, 128)], [("one", 0, 128)])
-    for i in range(2):
-        iota(("lv%d" % i, 0, L), [[1, 2], [16, H]], c0s[i], 0, True)
-    fill(("xm", V, V + 16), 0.0)
-    fill(("hit", L, LX), 1.0)
-    fill(("c255", 0, LX), 255.0)
-    for n in ("deg", "ocx", "ns0"):
-        fill((n, L, LX), 0.0)
-    fill(("qf1", L, LX), float(V))
-    fill(("c1280", 0, 1), float(V))
-    fill(("ksl", 0, 576), 0.0)
-    fill(("c33", 0, 1), float(LX - 2 * H + 1))
-    for i in range(2):
-        fill(("kv%d" % i, 0, 1), 8.0 * LX + c0s[i] + (1 - V) / 2.0)
-    ts(("pij", 0, 1), ("pii", 0, 1), 15, Op.bitwise_and)
-    ts(("pij", 1, 2), ("pii", 0, 1), 4, Op.arith_shift_right)
-    tc(("p15", 0, 1), ("pij", 0, 1))
-    tc(("pg", 0, 1), ("pij", 1, 2))
-    for c in range(2):
-        ts(("sc", c, c + 1), ("p15", 0, 1), 16.0 * c, Op.add)
-        ts(("sh", c, c + 1), ("p15", 0, 1), 16.0 * c + 0.5, Op.add)
-    ts(("gi", 0, 128), ("col", 0, 128), 4, Op.arith_shift_right)
-    ts(("bd", 0, 128), ("gi", 0, 128), ("pg", 0, 1), Op.is_equal)
-    for buf in ("la", "ln"):
-        fill((buf, BL * r, BL * r + 4), 0.0)
-    tc(("lrep", 0, L), ("col", 0, L))
-    tc(("limf", 0, 1), ("limi", 0, 1))
-    ts(("limb", 0, 1), ("limf", 0, 1), 1.0, Op.add)
-
-    for m, x in enumerate(classes("nm", 0)):
-        tc(("qu0", m * H, (m + 1) * H), x)
+    lanes_of(0)
     for lo, hi in CH0:
         mid = (lo + hi) // 2
         for f, a, z in ((tc, lo, mid), (act, mid, hi)):
-            f(("xv", 16 * a, 16 * z), ("I", ("xm", 0, G0), ("qu0", a, z)))
-        sums("xv", lo, hi)
-    for st in (1, 0):
-        for m, x in enumerate(classes("nm", st)):
-            tc(("qf%d" % st, m * H, (m + 1) * H), x)
-    act(("ocx", 0, L), ("qf0", 0, L), Fn.Identity, ("c1280", 0, 1), -1.0)
-    names_again(1, 0, H)
-    tc(("qu1", 0, L), ("qf1", 0, L))
-    tt(("ns0", 0, L), ("qf0", 0, L), ("lv0", 0, L), Op.not_equal)
+            f(("xv", 16 * a, 16 * z), pick(("xm", 0, G0), ("qu0", a, z)))
+        sums(lo, hi, True)
     hits(0)
-    sizes(0)
     variables(0)
-    tc(("ocp", 0, 32), ("I", ("ocx", 0, LX), ("plw", 0, 2)))
-    tt(("ln", BL * r + 4, BL * (r + 1)), ("I", ("ns0", 0, LX), ("plw", 0, 2)), ("ocp", 0, 32), Op.mult)
-    send(r, [("la", "a"), ("ln", "n")])
-    consts_g()
-    consts_v()
-    count(0)
-    limits(0)
-    consts_s()
-    dead_of(0)
-    tt(("ns1", 0, L), ("qf1", 0, L), ("lv1", 0, L), Op.not_equal)
-    consts_v2()
+    send(0, 0)
+    act(("zp", 0, 32), pick(("nl0", 0, LX), PLW))
+    tt(("vr", 0, 32), pick(("of0", 0, LX), PLW), ("zp", 0, 32), Op.not_equal)
+    tt(names_of(0, r), pick(("of0", 0, LX), PLW), ("vr", 0, 32), Op.mult)
+    send(0, 1)
+    later(after, 0)
+    later(lanes_of, 1)
     update(0)
 
     for t in range(1, ROUNDS):
         main(t)
         hits(t)
         pivots(t)
-        outputs(t - 1)
-        if t == 1:
-            for lo, hi in CH:
-                names_again(0, lo, hi)
-        kept_rows(t)
-        if t > 1:
-            put_names(4 * (t - 2) + r)
+        later(after, t)
+        later(kept_rows, t)
         if t < ROUNDS - 1:
             update(t)
 
-    t, old = 3, 12
-
-    def lands(qs):
-        for q in qs:
-            b = 4 * t + q
-            list_v(b)
-            act(("vb", 32 * q, 32 * q + 32), ("I", ("jt", 0, VT), ("evu", 2 * b, 2 * b + 2)))
-            size_of(b)
-            list_c(b)
-
-    def sizes_out(qs):
-        for q in qs:
-            put("xo", 12 + q, 13 + q, ("xt", 32 * q, 32 * q + 32))
-
-    lands(first)
-    sizes_out(first)
-    for q in first:
-        put_names(12 + q)
-    lands(last)
-    for q in (3, 2, 1, 0):
-        tc(("I", ("vid", 0, IDW), ("cwu", 24 + 2 * q, 26 + 2 * q)), ("vb", 32 * q, 32 * q + 32))
-    for lo, hi in ((0, 8), (8, old)):
-        act(("jf", 32 * lo, 32 * hi), ("I", ("vid", 0, IDW), ("jwc", 2 * lo, 2 * hi)))
-    sizes_out(last)
-    dma("s", T.yx[:, :], T["xo"][:, 0:V], "ox", [("xo", 0, V)], [])
-    for q in last:
-        put_names(12 + q)
-    dma("y", T.yn[:, :], T["nm"][:, 0:V], "on", [("nm", 0, V)], [])
-    put("jt", 0, 8, ("jf", 0, 256))
-    put("jt", 8, old, ("jf", 256, 384))
-    dma("y", T.yj[:, :], T["jt"][0:128:16, 0:V], "oj", [("jt", 0, V)], [])
+    def older():
+        put("nm", 384, ("nt", 0, 384))
+        put("xo", 384, ("xt", 0, 384))
+        for t in range(ROUNDS - 1):
+            for q in range(N):
+                act(block(t, q, SIZES[t], 32), pick(("jt", 0, VT), ("evu", 8 * t + 2 * q, 8 * t + 2 * q + 2)))
+    later(older)
+    roots(3)
+    act(("jv", 0, 384), pick(("la", 0, CW), ("ju3", 0, 24)))
+    act(("xt", 384, 512), pick(("la", 0, START[2]), ("j3", 0, 8)), -1.0)
+    put("jt", 384, ("jv", 0, 384))
+    dma("s", T.yj[:, :], T["jt"][0:128:16, 0:V], "oj", [("jt", 0, V)], [], 2.0)
+    ts(pick(("nm", 0, VT), ("evu", 24, 32)), ("l3", 0, 128), -1.0, Op.mult, float(V), Op.add)
+    dma("y", T.yn[:, :], T["nm"][:, 0:V], "on", [("nm", 0, V)], [], 3.2)
+    put("xo", 128, ("xt", 384, 512), 384)
+    dma("s", T.yx[:, :], T["xo"][:, 0:V], "ox", [("xo", 0, V)], [], 2.5)
+    in_order()
     for s, v in totals.items():
         if known["g"].get(s, 0) < v:
             g.wait_ge(T.sem[s], v)

@@ -7,32 +7,31 @@ L = 2 * H
 LX = L + 2 * CAP
 VT = 2304
 G0 = 1288
-WIDE = [36, 44, 52, 92]
-START = [752, 576, 368, 0]
-SIZES, VARS, CLAIMS, FREE = [0, 0, 20, 0], [32, 32, 0, 32], [None, 34, 2, 34], 60
-CW = 896
-ID0, VAL = 384, 1024
+START = [384, 256, 128, 0]
+ID0, VAL = 124, 1024
 SHIFT = 512 * 32618
-FP, BF, I32, U16 = "float32", "bfloat16", "int32", "uint16"
-CH0 = [(0, 64), (64, 160)]
+WIDE, SLOTS = [72, 80, 88, 128], [0, 288, 608, 960]
+VARS, COUNT, CLAIMS, FREE, NAMES = 32, 34, 36, 60, [36, 44, 52, 96]
+FP, BF, F16, I32, U16 = "float32", "bfloat16", "float16", "int32", "uint16"
+CH0 = [(0, 54, 96), (96, 128, 160)]
 CH = [(0, 48), (48, 112), (112, 160)]
-PART = [0, 0, 24, 0, 0, 0]
+PART = [0, 0, 0]
 LISTS = {1: ("qu1", "qn"), 2: ("qu0", "qm"), 3: ("qn", "qu1")}
-CYCLE, GATHER, SCATTER, PE, WAKE, ACROSS, HOP = 0.001, 1.4, 2.5, 0.5, 0.08, 0.13, 2.2
+CYCLE, GATHER, SCATTER, PE, WAKE, ACROSS, HOP = 0.001, 1.4, 3.0, 0.5, 0.08, 0.13, 1.7
 FIXED = {"v": 0.06, "s": 0.12, "t": 0.0, "g": 0.15}
-PASSES = 2
-SAME = True
-KEYS = 0
+SENDS = ["x", "r1", "a0", "r0", "a1", "k2", "a2", "k3", "a3", "n3"]
+PASSES = 1
 DBG = []
 
 _S = {
     "nm": (VT, FP), "en": (VT, FP), "rs": (VT, FP), "jt": (VT, FP), "xm": (VT, BF), "xo": (VT, BF),
-    "la": (CW, FP), "ln": (CW, FP), "l3": (128, FP), "idt": (CW, FP),
-    "jf0": (8, FP), "jf1": (16, FP), "jf2": (24, FP), "jf3": (24, FP), "ju0": (8, U16), "ju1": (16, U16), "ju2": (24, U16),
-    "ju3": (24, U16), "j3": (8, U16), "jb": (32, FP), "m0": (24, FP), "m1": (24, FP), "evu": (32, U16),
-    "er0": (128, FP), "er1": (256, FP), "er2": (384, FP), "xr0": (128, BF), "xr1": (256, BF), "xr2": (384, BF),
-    "idr": (384, FP), "bk": (384, FP), "jv": (384, FP), "xt": (512, BF), "nt": (384, FP),
-    "qf0": (LX, FP), "qf1": (LX, FP), "of0": (LX, FP), "of1": (LX, FP), "ocx": (L, FP), "nl0": (LX, FP), "nl1": (LX, FP), "lid": (LX, FP),
+    "sx": (V, BF), "lx": (V, BF), "r1": (4 * 168, F16), "r0": (4 * 2 * L, F16), "ra": (1472, F16), "rk": (8 * L, F16),
+    "la": (512, FP), "ln": (512, FP), "vid": (512, FP), "idt": (512, FP),
+    "jf0": (8, FP), "jf1": (16, FP), "jf2": (24, FP), "ju0": (8, U16), "ju1": (16, U16), "ju2": (24, U16), "ju3": (24, U16),
+    "jb": (8, FP), "jb0": (8, FP), "jm": (96, FP), "sm": (96, BF), "evu": (24, U16), "evo": (32, U16),
+    "er": (384, FP), "xr": (384, BF), "idr": (384, FP), "bk": (384, FP), "jv": (384, FP), "xt": (512, BF), "nt": (512, FP),
+    "qs": (L, U16), "os": (LX, FP), "ns": (LX, FP), "nlb": (L, FP),
+    "qf0": (LX, FP), "qf1": (LX, FP), "of0": (LX, FP), "of1": (LX, FP), "nl0": (LX, FP), "nl1": (LX, FP), "lid": (LX, FP),
     "qu0": (L, U16), "qu1": (L, U16), "qn": (L, U16), "qm": (L, U16), "qr0": (16 * L, FP), "qr1": (16 * L, FP),
     "dead0": (L, BF), "dead1": (L, BF), "piv": (L, BF), "pih": (L, BF),
     "eq": (16 * L, BF), "xv": (16 * L, BF), "msc": (16 * L, BF), "deg": (LX, I32), "si": (L, I32),
@@ -41,29 +40,36 @@ _S = {
     "qp": (32, U16), "vp": (32, U16), "zp": (32, FP), "xn": (544, FP), "vr": (544, FP), "cc": (544, FP), "nsc": (512, FP),
     "key": (512, FP), "ksc": (512, FP), "mi": (32, I32), "mj": (32, I32), "rho": (768, FP), "ne": (768, BF), "fc": (768, FP),
     "c1": (768, FP), "rev": (48, U16), "rep": (48, U16), "revf": (48, FP), "repi": (48, I32),
-    "a1": (1, BF), "ai": (1, I32), "aj": (1, I32), "limi": (1, I32), "limf": (1, FP), "lima": (1, FP),
-    "one": (128, BF), "idn": (128, BF), "idead": (128, BF), "ipen": (128, BF), "imx": (128, BF), "bdh": (128, BF), "bd": (128, BF),
-    "bd8": (128, BF), "dk": (2048, BF), "o16": (128, BF), "pii": (2, I32), "pij": (2, I32), "c16": (2, I32), "sc": (2, FP),
+    "ai": (1, I32), "aj": (1, I32), "limi": (1, I32), "lims": (1, FP), "limf": (1, FP), "lima": (1, FP),
+    "one": (128, BF), "zero": (128, BF), "idn": (128, BF), "idead": (128, BF), "ipen": (128, BF), "imx": (128, BF), "bdh": (128, BF),
+    "bd": (128, BF), "bd8": (128, BF), "dk": (2048, BF), "wide": (512, BF), "to": (4 * 224, BF), "o16": (224, BF), "cq": (128, BF),
+    "cqh": (128, BF), "c16th": (128, BF),
+    "pii": (2, I32), "pij": (2, I32), "pq": (2, I32), "c16": (2, I32), "c232": (2, I32), "sc": (2, FP), "kq": (2, FP), "cv0": (2, FP),
+    "cv": (2, FP), "ncv": (2, FP), "cb0": (4, FP), "cb": (4, FP),
     "ck": (16, FP), "qsc": (16, FP), "qbi": (16, FP), "wsc": (16, FP), "seg": (1024, BF), "kb": (512, FP),
 }
 PSUM = {"b0": 1024, "b1": 1024, "b2": 512, "d0": 512, "bhit": 512, "bkey": 512}
-SCRATCH = {n: ("sbuf", [128, c], d) for n, (c, d) in _S.items()}
+SMALL = [n for n, (c, d) in _S.items() if c <= 16 and n != "limi"]
+SCRATCH = {n: ("sbuf", [128, c], d) for n, (c, d) in _S.items() if n not in SMALL}
+SCRATCH.update({"small_" + d: ("sbuf", [128, 16 * len(SMALL)], d) for d in (FP, I32, U16)})
 SCRATCH.update({n: ("psum", [128, c], FP) for n, c in PSUM.items()})
-SEMAPHORES = (["qv", "qs", "qt", "qg", "dn", "dx", "do", "dl", "on", "ox", "oj", "loc"]
-              + [x + str(b) for x in ("a", "n", "la", "ln") for b in range(16)])
+SEMAPHORES = (["qv", "qs", "qt", "qg", "dn", "do", "dl", "on", "ox", "oj", "loc"]
+              + [x + "_" + str(q) for x in SENDS + ["ds", "dx"] for q in range(N)])
 
 
-def block(t, q, part=0, n=None):
-    lo = START[t] + WIDE[t] * q + part
-    return ("la", lo, lo + (WIDE[t] if n is None else n))
+def slot(t, q, part, n):
+    lo = SLOTS[t] + WIDE[t] * q + part
+    return ("ra", lo, lo + n)
 
 
-def names_of(t, q):
-    return ("l3", 32 * q, 32 * q + 32) if t == ROUNDS - 1 else ("ln",) + block(t, q, SIZES[t], 32)[1:]
-
-
-def messages(t, q):
-    return [(block(t, q), "a%d" % (4 * t + q)), (names_of(t, q), "n%d" % (4 * t + q))]
+def message(name, q, d):
+    if name == "x":
+        return ("sx", 320 * d, 320 * d + 320), ("lx", 320 * q, 320 * q + 320)
+    t = int(name[1])
+    cols = {"r": ("r1", 168 * q, 168 * q + L + 1) if t else ("r0", 2 * L * q, 2 * L * (q + 1)),
+            "k": ("rk", L * (4 * (t % 2) + q), L * (4 * (t % 2) + q + 1)),
+            "a": slot(t, q, 0, NAMES[t] + 32 if t < 3 else FREE + 32), "n": slot(t, q, NAMES[t], 32)}[name[0]]
+    return cols, cols
 
 
 def plan(core, T, topo):
@@ -77,38 +83,32 @@ def plan(core, T, topo):
     return direct, list(zip(relays, rest))
 
 
-def bits(engines):
-    return sum(1 << e for e in engines)
-
-
 def legs(core, T, topo):
     direct, via = plan(core, T, topo)
     out = []
-    for ds in ([x for x, d in via], direct):
-        k = [len(topo.engines(core, d)) // len(ds) for d in ds]
-        out.append([(d, topo.engines(core, d)[i * k[i]:(i + 1) * k[i]]) for i, d in enumerate(ds)])
+    for ds in (via, [(d, d) for d in direct]):
+        k = [len(topo.engines(core, x)) // len(ds) for x, d in ds]
+        out.append([(x, d, topo.engines(core, x)[i * k[i]:(i + 1) * k[i]]) for i, (x, d) in enumerate(ds)])
     return out
 
 
-def transfer(T, topo, src, dst, engines, cols, sem):
+def transfer(T, topo, src, dst, engines, a, b, sem):
     rid, pid = topo.addr(dst, src)
-    piece = T[cols[0]][:, cols[1]:cols[2]]
-    return RemoteDMATransfer(dst_ids=[DstId(rid=rid, pnc=pid)], dma_engine_mask=bits(engines), remote_sem=T.sem[sem],
-                             srcs=[piece], dsts=[piece])
+    return RemoteDMATransfer(dst_ids=[DstId(rid=rid, pnc=pid)], dma_engine_mask=sum(1 << e for e in engines), remote_sem=T.sem[sem],
+                             srcs=[T[a[0]][:, a[1]:a[2]]], dsts=[T[b[0]][:, b[1]:b[2]]])
 
 
 def relay_program(g, core, T, topo):
     for r, src in enumerate(T.cores):
-        for x, dst in plan(src, T, topo)[1]:
+        for x, dst, into in legs(src, T, topo)[0]:
             if x != core:
                 continue
-            into = [eng for call in legs(src, T, topo) for d, eng in call if d == core][0]
             out = topo.engines(core, dst)
-            for t in range(ROUNDS):
-                for cols, sem in messages(t, r):
-                    g.wait_ge(T.sem[sem], len(into))
-                    g.remote_dma_fused([transfer(T, topo, core, dst, out, cols, sem)], local_sem=T.sem.loc)
-            g.wait_ge(T.sem.loc, 2 * ROUNDS * len(out))
+            for name in SENDS:
+                cols, sem = message(name, r, T.rank_of(dst))[1], "%s_%d" % (name, r)
+                g.wait_ge(T.sem[sem], len(into))
+                g.remote_dma_fused([transfer(T, topo, core, dst, out, cols, cols, sem)], local_sem=T.sem.loc)
+            g.wait_ge(T.sem.loc, len(SENDS) * len(out))
 
 
 def rank_program(g, core, T, topo):
@@ -144,8 +144,6 @@ def rank_program(g, core, T, topo):
                     if kind == "r" and e[2] == "r" and n not in PSUM:
                         continue
                     if n in PSUM and e[3] == q and (q == "t" or kind == "r" and e[2] == "r"):
-                        continue
-                    if not SAME and kind == "w" and e[3] == q and q in "vs":
                         continue
                     toks.append((e[4], e[5], e[6]))
         return toks
@@ -186,6 +184,9 @@ def rank_program(g, core, T, topo):
             return x
         if x[0] == "I":
             return ap(x[1]).indirect(ap(x[2]))
+        if x[0] in SMALL:
+            at = 16 * SMALL.index(x[0])
+            x = ("small_" + _S[x[0]][1], at + x[1], at + x[2]) + x[3:]
         if len(x) > 3:
             return T[x[0]][:, x[1]:x[2]:x[3]]
         return T[x[0]][:, x[1]:x[2]]
@@ -199,7 +200,7 @@ def rank_program(g, core, T, topo):
         if any(x[0] == "I" for x in full):
             return 0.06 + CYCLE * n * (SCATTER if outs[0][0] == "I" else GATHER)
         if pace is None:
-            narrow = all(x[0] not in PSUM and _S[x[0]][1] in (BF, U16) for x in full if width(x) == n)
+            narrow = all(x[0] not in PSUM and _S[x[0]][1] in (BF, F16, U16) for x in full if width(x) == n)
             pace = {"v": 0.5 if narrow else 1, "s": 1, "g": 2, "t": PE}[q]
         return FIXED[q] + CYCLE * (max(64, n * pace) if q == "v" else max(64, n) * pace if q == "t" else n * pace)
 
@@ -316,7 +317,7 @@ def rank_program(g, core, T, topo):
         f = func or (Fn.Identity if isinstance(bias, tuple) else Fn.Copy)
         emit("s", lambda: g.scalar.activation(out=ap(out), in_=ap(in_), func=f, bias=ap(bias), scale=ap(scale)), [out], [in_, bias, scale])
 
-    def mm(out, w, x, start, stop):
+    def mm(out, w, x, start=True, stop=True):
         emit("t", lambda: g.tensor.matmul(out=ap(out), lhsT=ap(w), rhs=ap(x), start=start, stop=stop), [out], [w, x])
 
     def iota(out, pattern, base, mul=0):
@@ -325,8 +326,9 @@ def rank_program(g, core, T, topo):
         else:
             emit("g", lambda: g.iota(ap(out), pattern, base, mul, allow_small_or_imprecise_dtypes=True), [out], [])
 
-    def const(out, c):
-        iota(out, [[0, width(out)]], c)
+    def count_up(n, lo, hi, step, base):
+        for a in range(lo, hi, 256):
+            iota((n, a, min(a + 256, hi)), [[step, min(a + 256, hi) - a]], base + step * a)
 
     def select(out, in_, pattern, op, base, mul):
         emit("g", lambda: g.affine_select(ap(out), ap(in_), pattern, op, 0.0, base, mul), [out], [in_])
@@ -344,35 +346,38 @@ def rank_program(g, core, T, topo):
 
     near = [T.rank_of(d) for d in plan(core, T, topo)[0]]
     far = [q for q in range(N) if q != r and q not in near]
+    coming = [r] + near + far
 
-    def send(t, j):
-        cols, sem = messages(t, r)[j]
+    def send(name, slow=1.0):
+        mine = [message(name, r, d)[0] for d in near + far]
 
         def issue():
-            wait_for("g", deps("g", [cols], []))
-            left = "l" + sem
+            wait_for("g", deps("g", mine, []))
             for call in legs(core, T, topo):
-                g.remote_dma_fused([transfer(T, topo, core, d, eng, cols, sem) for d, eng in call], local_sem=T.sem[left])
-                totals[left] = totals.get(left, 0) + sum(len(eng) for d, eng in call)
-            note("net", [cols], [], left, totals[left], {})
+                g.remote_dma_fused([transfer(T, topo, core, x, eng, *message(name, r, T.rank_of(d)), "%s_%d" % (name, r))
+                                    for x, d, eng in call], local_sem=T.sem.loc)
+                totals["loc"] = totals.get("loc", 0) + sum(len(eng) for x, d, eng in call)
         sent = [("sent", len(calls), len(calls) + 1)]
-        calls.append(("g", issue, [cols], [("sends", 0, 1)] + sent, 0.5, 0.5))
+        calls.append(("g", issue, mine, [("sends", 0, 1)] + sent, 0.5, 0.5))
         for q in near + far:
-            src = T.cores[q]
-            got = [len(eng) for call in legs(src, T, topo) for d, eng in call if d == core]
-            got += [len(topo.engines(x, core)) for x, d in plan(src, T, topo)[1] if d == core]
-            land, s = messages(t, q)[j]
+            got = [len(eng) if x == d else len(topo.engines(x, d)) for call in legs(T.cores[q], T, topo) for x, d, eng in call if d == core]
+            land, s = message(name, q, r)[1], "%s_%d" % (name, q)
             totals[s] = got[0]
             calls.append(("net", lambda a=([land], s, got[0]): note("net", [], a[0], a[1], a[2], {}), sent, [land],
-                          0.0, HOP * (1 if q in near else 2) * (1.8 if t == 0 else 1)))
-
-    c0s = [(8 * t + 2 * r) % 16 for t in range(2)]
+                          0.0, HOP * (1 if q in near else 2) * slow))
 
     def classes(st):
-        return [((m * H, (m + 1) * H), ("nm", c0s[st] + m, 16 * (H - 1) + c0s[st] + m + 1, 16)) for m in range(2)]
+        c = 8 * st + 2 * r
+        return [((m * H, (m + 1) * H), ("nm", c + m, 16 * (H - 1) + c + m + 1, 16)) for m in range(2)]
 
     def lx(t):
         return L + CAP * (1 + t // 2)
+
+    def to_all(q):
+        return ("wide", 128 * q, 128 * q + 128)
+
+    def to_one(q, d):
+        return ("to", 224 * q + 96 - 32 * d, 224 * q + 224 - 32 * d)
 
     P15 = ("sc", 0, 1)
     PLW = ("plw", 0, 2)
@@ -382,34 +387,49 @@ def rank_program(g, core, T, topo):
         iota(("c16", 0, 2), [[16, 2]], 0)
         ts(("pij", 0, 2), ("pii", 0, 2), 15, Op.bitwise_and)
         tt(("sc", 0, 2), ("pij", 0, 2), ("c16", 0, 2), Op.add)
+        iota(("c232", 0, 2), [[30, 2]], 2)
+        ts(("pq", 0, 2), ("pii", 0, 2), 5, Op.arith_shift_right)
+        tt(("kq", 0, 2), ("pq", 0, 2), ("c232", 0, 2), Op.mult)
+        iota(("cv0", 0, 2), [[8, 2]], -1024)
+        ts(("cv", 0, 2), ("cv0", 0, 2), ("kq", 0, 1), Op.add)
+        ts(("ncv", 0, 2), ("cv", 0, 2), -1.0, Op.mult, -1024.0, Op.add)
+        iota(("cb0", 0, 4), [[-128, 4]], VAL + START[0])
+        ts(("cb", 0, 4), ("cb0", 0, 4), ("kq", 1, 2), Op.add)
         fill(("one", 0, 128), 1.0)
         select(("idn", 0, 128), ("one", 0, 128), [[-1, 128]], Op.is_equal, 0, 1)
         select(("bdh", 0, 128), ("one", 0, 128), [[-16, 8], [0, 16]], Op.is_ge, 0, 1)
         select(("bd", 0, 128), ("bdh", 0, 128), [[16, 8], [0, 16]], Op.is_ge, 15, -1)
+        fill(("to", 0, 4 * 224), 0.0)
+        for q in range(N):
+            select(to_all(q), ("one", 0, 128), [[0, 4], [-1, 32]], Op.is_equal, -32 * q, 1)
+            act(("to", 224 * q + 96, 224 * q + 128), ("idn", 32 * q, 32 * q + 32))
+        fill(("o16", 0, 224), 0.0)
+        fill(("o16", 96, 128), 0.0625)
+        act(("c16th", 0, 128), ("one", 0, 128), 0.0625)
+        select(("cqh", 0, 128), ("c16th", 0, 128), [[-32, 4], [0, 32]], Op.is_ge, 0, 1)
+        select(("cq", 0, 128), ("cqh", 0, 128), [[32, 4], [0, 32]], Op.is_ge, 31, -1)
+        iota(("zero", 0, 128), [[0, 128]], 0)
+        iota(("nlb", 0, L), [[-1, 2], [-16, H]], V)
+        act(("ns", 0, L), ("nlb", 0, L), 1.0, -2.0 * r)
+        for n in ("ns", "os", "z"):
+            fill((n, L, LX), 0.0)
         for st in range(2):
-            iota(("nl%d" % st, 0, L), [[-1, 2], [-16, H]], V - c0s[st])
-            for n, c in (("nl", 0.0), ("of", 0.0), ("qf", float(V))):
-                fill((n + str(st), L, LX), c)
+            act(("nl%d" % st, 0, L), ("nlb", 0, L), 1.0, ("ncv", st, st + 1))
+            for n, c in (("nl", 0), ("of", 0), ("qf", V)):
+                iota((n + str(st), L, LX), [[0, LX - L]], c)
         iota(("lid", 0, LX), [[1, LX]], 0)
-        fill(("xm", V, V + 16), 0.0)
+        for n in ("xo", "xm"):
+            fill((n, V, V + 16), 0.0)
         fill(("hit", L, L + CAP), 1.0)
         fill(("c255", 0, LX), 255.0)
         fill(("deg", L, LX), 0)
-        fill(("z", L, LX), 0.0)
         fill(("sgl", 0, 2 * LX), 1.0)
         fill(("sgl", lx(0), lx(0) + 1), 0.0)
-        for t in range(ROUNDS):
-            const(block(t, r, VARS[t] + 2 + 8 * t, 2), 0)
-        for t in range(ROUNDS - 1):
-            for q in range(N):
-                lo = block(t, q, 0 if SIZES[t] else 32)[1]
-                const(("ln", lo, lo + WIDE[t] - 32), 0)
-        tc(("limf", 0, 1), ("limi", 0, 1))
-        tc(("lima", 0, 1), ("limi", 0, 1))
-        const(("en", 0, G0), -1)
-        const(("rs", 0, G0), -SHIFT - 16384)
-        iota(("idt", 0, CW), [[1, CW]], -ID0 - SHIFT)
-        iota(("jt", 0, VT), [[1, VT]], 0)
+        tc(("lims", 0, 1), ("limi", 0, 1))
+        count_up("en", 0, G0, 0, -1)
+        count_up("rs", 0, G0, 0, -SHIFT - 16384)
+        count_up("idt", 0, 512, 1, -ID0 - SHIFT)
+        count_up("jt", 0, VT, 1, 0)
         iota(("ck", 0, 16), [[1, 16]], 0)
         ts(("qsc", 0, 16), ("ck", 0, 16), P15, Op.not_equal, -1.0, Op.mult)
         ts(("qbi", 0, 16), ("qsc", 0, 16), -1281.0, Op.mult, -1.0, Op.add)
@@ -423,36 +443,41 @@ def rank_program(g, core, T, topo):
         for n, c in (("idead", -20480.0), ("imx", -1.0 / 4096), ("ipen", -32.0)):
             act((n, 0, 128), ("idn", 0, 128), c)
         act(("bd8", 0, 128), ("bd", 0, 128), -2.0)
-        act(("o16", 0, 128), ("one", 0, 128), -0.0625)
-        const(("dead1", 0, L), 1)
+        iota(("dead1", 0, L), [[0, L]], 1)
         fill(("seg", 0, 1024), 1.0)
         fill(("seg", 0, 1024, 16), 0.0)
-        const(("kb", 0, 512), 512)
+        count_up("kb", 0, 512, 0, 512)
         fill(("kb", 0, 512, 16), -6.0e7)
-        const(("c1", 0, 768), 1)
+        count_up("c1", 0, 768, 0, 1)
+        iota(("sm", 0, 96), [[0, 96]], 0)
+        fill(("sm", 0, 96, 4), 4096.0)
         iota(("revf", 0, 48), [[0, 24], [-16, 2]], 31)
         ts(("rev", 0, 48), ("revf", 0, 48), P15, Op.subtract)
         iota(("repi", 0, 48), [[1, 24], [0, 2]], 0)
         tc(("rep", 0, 48), ("repi", 0, 48))
-        for t in range(ROUNDS):
-            iota(("jb", 8 * t, 8 * t + 8), [[WIDE[t], 4], [16, 2]], START[t] + SIZES[t] + (VAL if t < 3 else 0))
-            ts(("jf%d" % t, 8 * t, 8 * t + 8) if t < 3 else ("j3", 0, 8), ("jb", 8 * t, 8 * t + 8), P15, Op.add)
+        iota(("jb0", 0, 8), [[16, 8]], 0)
+        ts(("jb", 0, 8), ("jb0", 0, 8), P15, Op.add)
+        for t in range(ROUNDS - 1):
+            tc(("ju%d" % t, 8 * t, 8 * t + 8), ("jb", 0, 8))
+            act(("jf%d" % t, 8 * t, 8 * t + 8), ("jb", 0, 8), 1.0, float(VAL + START[t]))
 
-    def lanes_of(st):
-        for (lo, hi), x in classes(st):
-            tc(("qu%d" % st, lo, hi), x)
-        n = len(calls)
-        for (lo, hi), x in classes(st):
-            act(("of%d" % st, lo, hi), x, -1.0, float(V))
-        for (lo, hi), x in classes(st):
-            act(("qf%d" % st, lo, hi), x)
+    def lanes_of(st, bank):
+        n = width(message("r%d" % st, r, r)[0])
+        for q in coming:
+            mm((bank, 0, n), to_one(r, q), message("r%d" % st, q, r)[1], q == r, q == coming[-1])
+        act(("qf%d" % st, 0, L), (bank, 0, L))
+        tc(("qu%d" % st, 0, L), (bank, 0, L))
+        if st:
+            act(("limf", 0, 1), (bank, L, L + 1), 1.0, 2048.0)
+        else:
+            act(("dead0", 0, L), (bank, L, 2 * L), 1.0, 1.0)
+        act(("of%d" % st, 0, L), ("qf%d" % st, 0, L), -1.0, float(V))
         for k in range(16):
             o, i = ("qr%d" % st, k, 16 * (L - 1) + k + 1, 16), ("qf%d" % st, 0, L)
-            if k % 3 < st:
+            if k % 2 < st:
                 ts(o, i, ("qsc", k, k + 1), Op.mult, ("qbi", k, k + 1), Op.add)
             else:
                 act(o, i, ("qsc", k, k + 1), ("qbi", k, k + 1))
-        aside.update(range(n, len(calls)))
 
     def sums(lo, hi, stop):
         for k in range(16):
@@ -461,7 +486,7 @@ def rank_program(g, core, T, topo):
     def hits(t):
         st, n = t % 2, lx(t)
         if t == 0:
-            ts(("ok", 0, L), ("d0", 0, L), ("lima", 0, 1), Op.is_le)
+            ts(("ok", 0, L), ("d0", 0, L), ("lims", 0, 1), Op.is_le)
             later(tc, ("deg", 0, L), ("d0", 0, L))
         else:
             tc(("si", 0, L), ("d0", 0, L))
@@ -480,29 +505,28 @@ def rank_program(g, core, T, topo):
     def variables(t):
         n = lx(t)
         ts(("vy", 0, 2), ("sn", n - 1, 2 * n, n), float(H), Op.is_ge, 1.0 - V, Op.mult)
-        ts(("vx", 0, 2), ("sn", n - 1, 2 * n, n), 16.0, Op.mult, float(c0s[t % 2]), Op.add)
-        ts(block(t, r, SIZES[t], 32), pick(("deg", 0, LX), PLW), -1.0, Op.mult, -255.0, Op.max)
-        tt(block(t, r, VARS[t], 2), ("vx", 0, 2), ("vy", 0, 2), Op.add)
+        ts(("vx", 0, 2), ("sn", n - 1, 2 * n, n), 16.0, Op.mult, ("cv", t % 2, t % 2 + 1) if t else 2.0 * r - 1024, Op.add)
+        ts(slot(t, r, 0, 32), pick(("deg", 0, LX), PLW), -1.0, Op.mult, -255.0, Op.max)
+        tt(slot(t, r, VARS, 2), ("vx", 0, 2), ("vy", 0, 2), Op.add)
+        later(ts, slot(t, r, COUNT, 2), ("cum", L - 2, L), float(CAP), Op.min)
 
-    def after(t):
-        if t < ROUNDS - 1:
-            act(("a1", 0, 1), ("cum", L - 1, L), -1.0, float(CAP), Fn.Relu)
-            mm(("bhit", 0, 1), ("o16", 0, 128), ("a1", 0, 1), True, True)
-            tc(("ai", 0, 1), ("bhit", 0, 1))
-            ts(("aj", 0, 1), ("ai", 0, 1), 7, Op.bitwise_and)
-            tt(("lima", 0, 1), ("limf", 0, 1), ("aj", 0, 1), Op.add)
-        if t < 2:
-            ts(("piv", 0, L), ("cum", 0, L), float(CAP), Op.is_le, 2.0, Op.mult)
-            tt(("pih", 0, L), ("piv", 0, L), ("hit", 0, L), Op.mult)
-            act(("dead%d" % t, 0, L), ("pih", 0, L), 1.0, 1.0)
-        if t == 1:
-            const(("hit", L, L + CAP), 0)
-            const(("hit", L + CAP, LX), 1)
-            const(("sgl", lx(0), lx(0) + 1), 1)
-            const(("sgl", LX, LX + 1), 0)
+    def limits(t):
+        for d in coming:
+            w = ("cq", 0, 128) if t else ("o16", 96 - 32 * d, 224 - 32 * d)
+            mm(("bkey", 0, 1), w, slot(t, d, COUNT + 1, 1), d == r, d == coming[-1])
+        tc(("ai", 0, 1), ("bkey", 0, 1))
+        ts(("aj", 0, 1), ("ai", 0, 1), 7, Op.bitwise_and)
+        tt(("lima", 0, 1), ("limf", 0, 1), ("aj", 0, 1), Op.add)
 
-    def put(table, n, src, lo=0):
-        tc(pick((table, 0, VT), ("evu", lo // 16, (lo + n) // 16)), src)
+    def pivot_lanes(out):
+        ts(("piv", 0, L), ("cum", 0, L), float(CAP), Op.is_le, 2.0, Op.mult)
+        tt(out, ("piv", 0, L), ("hit", 0, L), Op.mult)
+
+    def put(table, lists, lo, hi, src):
+        tc(pick((table, 0, VT), (lists, lo // 16, hi // 16)), src)
+
+    def own(table, t):
+        put(table, "evo", 128 * t, 128 * t + 128, ("nt" if table == "nm" else "xt", 128 * t, 128 * t + 128))
 
     def main(t):
         st = t % 2
@@ -510,7 +534,7 @@ def rank_program(g, core, T, topo):
 
         def cover(c):
             lo, hi = CH[c]
-            bank = ("b%d" % (c % 3), 0, hi - lo)
+            bank = ("b%d" % c, 0, hi - lo)
             next_of("covers")
             tt(("eq", 16 * lo, 16 * hi), pick(("en", 0, G0), (qu, lo, hi)), ("qr%d" % st, 16 * lo, 16 * hi), Op.is_equal)
             mm(bank, ("idead", 0, 128), ("dead%d" % st, lo, hi), True, False)
@@ -521,7 +545,7 @@ def rank_program(g, core, T, topo):
 
         def uncovered(c):
             lo, hi = CH[c]
-            bank = ("b%d" % (c % 3), 0, hi - lo)
+            bank = ("b%d" % c, 0, hi - lo)
             tt(("q2", lo, hi), ("qf%d" % st, lo, hi), bank, Op.max)
             ts((qn, lo, hi), ("q2", lo, hi), float(V), Op.min)
             later(act, ("z", lo, hi), bank, 1.0, 0.0, Fn.Abs)
@@ -542,15 +566,11 @@ def rank_program(g, core, T, topo):
         for c in range(len(CH)):
             if c + 1 < len(CH):
                 cover(c + 1)
-            elif KEYS == 0:
-                keys(t)
+            else:
+                tt(pick(("rs", 0, VT), ("evu", 0, 8 * t)), ("idr", 0, 128 * t), ("bk", 0, 128 * t), Op.add)
             uncovered(c)
         for c in range(len(CH)):
             degrees(c)
-        if KEYS == 1:
-            keys(t)
-        if KEYS == 2:
-            later(keys, t)
 
     def pivots(t):
         st, n = t % 2, 256 * t
@@ -559,120 +579,194 @@ def rank_program(g, core, T, topo):
         act(("key", 0, 512), pick(("rs", 0, G0), ("qp", 0, 32)))
         tc(("vp", 0, 32), pick(("lid", 0, LX), PLW))
         variables(t)
+        if t == ROUNDS - 1:
+            own("nm", 0)
         act(("vr", 0, 512), pick(nl, ("vp", 0, 32)))
         act(("vr", 512, 544), pick(nl, PLW))
         act(("b1", 0, 544), ("vr", 0, 544))
         act(("xn", 0, 512), pick(("en", 0, G0), ("qp", 0, 32)))
         act(("zp", 0, 32), pick(("z", 0, LX), PLW), -1.0)
         if t == ROUNDS - 1:
-            later(act, block(t, r, FREE, 32), ("vr", 512, 544), -1.0, float(V))
+            ts(slot(t, r, FREE, 32), pick(nl, PLW), -1.0, Op.mult, float(V), Op.add)
         scan(("ksc", 0, 512), ("kb", 0, 512), ("key", 0, 512), Op.add, Op.max)
         tc(("mi", 0, 32), ("ksc", 15, 512, 16))
         ts(("mj", 0, 32), ("mi", 0, 32), 511, Op.bitwise_and)
         later(act, ("rho", 0, n), pick(("jf%d" % (t - 1), 0, 8 * t), ("rep", 0, 16 * t)), 1.0, float(-VAL - ID0))
-        later(fill, ("c1", 31, n, 32), float(VAL + block(t, r, FREE if t == ROUNDS - 1 else SIZES[t])[1]))
+        later(ts, ("c1", 31, n, 32), ("c1", 0, 8 * t), ("cb", t, t + 1), Op.mult)
         tt(("ne", 0, n), pick(("mj", 0, 32), ("rev", 0, 16 * t)), ("rho", 0, n), Op.not_equal)
         scan(("fc", 0, n), ("ne", 0, n), ("c1", 0, n), Op.mult, Op.add, float(VAL))
-        tt(block(t, r, CLAIMS[t], 8 * t), ("fc", 31, n, 32), ("jf%d" % (t - 1), 0, 8 * t), Op.min)
-        send(t, 0)
+        tt(slot(t, r, CLAIMS, 8 * t), ("fc", 31, n, 32), ("jf%d" % (t - 1), 0, 8 * t), Op.min)
+        if t == ROUNDS - 1:
+            send("a3")
         tt(("xn", 512, 544), pick(("of%d" % st, 0, LX), PLW), ("zp", 0, 32), Op.add)
         tt(("b0", 0, 544), ("xn", 0, 544), ("b1", 0, 544), Op.not_equal)
         tt(("cc", 0, 544), ("xn", 0, 544), ("b0", 0, 544), Op.mult)
         scan(("nsc", 0, 512), ("seg", 0, 512), ("cc", 0, 512), Op.mult, Op.max)
-        tt(names_of(t, r), ("cc", 512, 544), ("nsc", 15, 512, 16), Op.max)
-        send(t, 1)
+        tt(slot(t, r, NAMES[t], 32), ("cc", 512, 544), ("nsc", 15, 512, 16), Op.max)
 
-    def kept_rows(t):
-        o = ("of1" if t == 1 else "ocx", 0, L)
-        act(o, ("q2", 0, L), -1.0, float(V), Fn.Relu)
-        if t == 1:
-            act(("qf1", 0, L), o, -1.0, float(V))
-        else:
-            for (lo, hi), x in classes(t % 2):
-                act(x, ("ocx", lo, hi), -1.0, float(V))
-
-    def roots(t):
-        if t > 0:
-            lists = [block(t, q, CLAIMS[t], 8 * t) for q in [r] + near + far]
-            tt(("m0", 0, 8 * t), lists[0], lists[1], Op.min)
-            tt(("m1", 0, 8 * t), lists[2], lists[3], Op.min)
-            tt(("jf%d" % t, 0, 8 * t), ("m0", 0, 8 * t), ("m1", 0, 8 * t), Op.min)
-        k = min(8 * t + 8, 24)
-        ts(("ju%d" % t, 0, k), ("jf%d" % t, 0, k), float(-VAL - START[t]), Op.add)
-        for c in range(2):
-            lo = START[t] + VARS[t] + c
-            tc(("evu", 8 * t + c, 8 * t + 7 + c, 2), ("la", lo, lo + 3 * WIDE[t] + 1, WIDE[t]))
+    def least(t, bank):
+        scan(("jm", 0, 32 * t), ("sm", 0, 32 * t), (bank, 16, 16 + 32 * t), Op.add, Op.min)
+        ts(("ju%d" % t, 0, 8 * t), ("jm", 3, 32 * t, 4), float(-VAL - START[t]), Op.add)
 
     def update(t):
         n = 128 * (t + 1)
         ju = ("ju%d" % t, 0, n // 16)
-        xr, er = ("xr%d" % t, 0, n), ("er%d" % t, 0, n)
-        roots(t)
-        act(xr, pick(("la", START[t], CW), ju), 4096.0)
-        next_of("roots")
-        act(er, pick(("ln", START[t], CW), ju))
-        put("xm", n, xr)
-        put("en", n, er)
-        mm(("bkey", 0, n), ("bd8", 0, 128), xr, True, True)
+        xr, er = ("xr", 0, n), ("er", 0, n)
+
+        def spread(part, k, out):
+            for q in coming if t == 0 else range(N):
+                mm(out(q), to_all(q if t else r), slot(t, r if t else q, part, k))
+        if t:
+            spread(CLAIMS, 8 * t, lambda q: ("bhit", 16 + q, 16 + 32 * t, 4))
+        spread(VARS, 2, lambda q: ("bhit", 2 * q, 2 * q + 2))
+        spread(0, 32, lambda q: ("d0", 32 * q, 32 * q + 32))
+        spread(NAMES[t], 32, lambda q: ("b2", 32 * q, 32 * q + 32))
+        if t:
+            least(t, "bhit")
+        ts(("evu", 8 * t, 8 * t + 8), ("bhit", 0, 8), 1024.0, Op.add)
+        new = (START[t], START[t] + 128)
+        if t:
+            act(("la",) + new, ("d0", 0, 128))
+            act(xr, pick(("la", START[t], 512), ju), 4096.0)
+            act(("ln",) + new, ("b2", 0, 128))
+            next_of("roots")
+            act(er, pick(("ln", START[t], 512), ju))
+            put("xm", "evu", 0, n, xr)
+            put("en", "evu", 0, n, er)
+            later(act, ("jf%d" % t, 0, 8 * t), ("jm", 3, 32 * t, 4))
+        else:
+            act(er, ("b2", 0, 128))
+            next_of("roots")
+            act(xr, ("d0", 0, 128), 4096.0)
+            put("en", "evu", 0, n, er)
+            put("xm", "evu", 0, n, xr)
+            later(act, ("la",) + new, xr, 1.0 / 4096)
+            later(act, ("ln",) + new, er)
+        mm(("bkey", 0, n), ("bd8", 0, 128), xr)
         next_of("roots")
         act(("bk", 0, n), ("bkey", 0, n))
         next_of("roots")
-        act(("idr", 0, n), pick(("idt", START[t], CW), ju))
-        later(act, ("xt", n - 128, n), (xr[0], n - 128, n), -1.0 / 4096)
-        later(act, ("nt", n - 128, n), (er[0], n - 128, n), -1.0, float(V))
+        act(("idr", 0, n), pick(("idt", START[t], 512), ju))
 
-    def keys(t):
-        n = 128 * t
-        tt(pick(("rs", 0, VT), ("evu", 0, n // 16)), ("idr", 0, n), ("bk", 0, n), Op.add)
+    def collect(t, bank, n, pieces):
+        if t == ROUNDS - 1:
+            mm((bank, 0, n), ("idn", 0, 128), ("zero", 0, n), True, False)
+        for d in coming if t == ROUNDS - 1 else [None]:
+            for part, k, out in pieces:
+                for q in range(N):
+                    if t == 0:
+                        mm((bank,) + out(q), ("idn", 0, 128), slot(t, q, part, k))
+                    elif d is None:
+                        for e in range(N):
+                            mm((bank,) + out(q), to_one(q, e), slot(t, e, part, k), e == 0, e == N - 1)
+                    else:
+                        mm((bank,) + out(q), to_one(q, d), slot(t, d, part, k), False, (d, part, q) == (coming[-1], pieces[-1][0], N - 1))
 
-    dma("y", T["nm"][:, 0:V], T.nb[:, :], "dn", [], [("nm", 0, V)], 3.8)
-    dma("s", T["xm"][:, 0:V], T.xs[:, :], "dx", [], [("xm", 0, V)], 3.8)
-    dma("s", T["limi"][:, 0:1], T.lim[:, 0:1], "dl", [], [("limi", 0, 1)], 3.8)
-    dma("y", T["xo"][:, 0:V], T.xs[:, :], "do", [("limi", 0, 1)], [("xo", 0, V)], 3.0)
+    def by32(q):
+        return (32 * q, 32 * q + 32)
+
+    def outputs(t):
+        collect(t, "bhit", 8, [(VARS, 2, lambda q: (2 * q, 2 * q + 2))])
+        ts(("evo", 8 * t, 8 * t + 8), ("bhit", 0, 8), 1024.0, Op.add)
+        collect(t, "d0", 128, [(0, 32, by32)])
+        act(("xt", 128 * t, 128 * t + 128), ("d0", 0, 128), -1.0)
+        collect(t, "b2", 128, [(NAMES[t], 32, by32)])
+        act(("nt", 128 * t, 128 * t + 128), ("b2", 0, 128), -1.0, float(V))
+        act(("vid", START[t], START[t] + 128), pick(("jt", 0, VT), ("evo", 8 * t, 8 * t + 8)))
+
+    def kept_rows(t):
+        for d in range(N):
+            mm(("bkey", 0, L), to_one(r, d), message("k%d" % t, d, r)[1], d == 0, d == N - 1)
+        for (lo, hi), x in classes(t % 2):
+            act(x, ("bkey", lo, hi))
+
+    for d in far + near:
+        dma("y", T["sx"][:, 320 * d:320 * d + 320], T.xs[32 * d:32 * d + 32, :], "ds_%d" % d, [], [message("x", r, d)[0]], 2.5)
+    dma("y", T["nm"][:, 0:V], T.nb[:, :], "dn", [], [("nm", 0, V)], 4.2)
+    dma("s", T["xo"][:, 0:V], T.xs[:, :], "do", [], [("xo", 0, V)], 4.2)
+    dma("s", T["limi"][:, 0:1], T.lim[:, 0:1], "dl", [], [("limi", 0, 1)], 4.2)
+    dma("y", T["xm"][32 * r:32 * r + 32, 0:V], T.xs[32 * r:32 * r + 32, :], "dx_%d" % r, [("nm", 0, V)], [("xm", r, V, N)], 1.5)
+    send("x", 2.4)
+    for q in near + far:
+        dma("y", T["xm"][32 * q:32 * q + 32, 0:V], T["lx"][:, 320 * q:320 * q + 320], "dx_%d" % q, [message("x", q, r)[1]], [("xm", q, V, N)], 1.5)
     later(constants)
 
-    lanes_of(0)
-    for lo, hi in CH0:
-        mid = (lo + hi) // 2
-        for f, a, z in ((tc, lo, mid), (act, mid, hi)):
-            f(("xv", 16 * a, 16 * z), pick(("xm", 0, G0), ("qu0", a, z)))
+    for (lo, hi), x in classes(0):
+        tc(("qs", lo, hi), x)
+    for (lo, hi), x in classes(1):
+        tc(("r1", 168 * r + lo, 168 * r + hi), x)
+    ts(("r1", 168 * r + L, 168 * r + L + 1), ("limi", 0, 1), -2048.0, Op.add)
+    send("r1")
+    for lo, mid, hi in CH0:
+        for f, a, z in ((act, lo, mid), (tc, mid, hi)):
+            f(("xv", 16 * a, 16 * z), pick(("xo", 0, G0), ("qs", a, z)))
         sums(lo, hi, True)
+    for (lo, hi), x in classes(0):
+        later(act, ("os", lo, hi), x, -1.0, float(V))
     hits(0)
     variables(0)
-    send(0, 0)
-    act(("zp", 0, 32), pick(("nl0", 0, LX), PLW))
-    tt(("vr", 0, 32), pick(("of0", 0, LX), PLW), ("zp", 0, 32), Op.not_equal)
-    tt(names_of(0, r), pick(("of0", 0, LX), PLW), ("vr", 0, 32), Op.mult)
-    send(0, 1)
-    later(after, 0)
-    later(lanes_of, 1)
+    act(("zp", 0, 32), pick(("ns", 0, LX), PLW))
+    tt(("vr", 0, 32), pick(("os", 0, LX), PLW), ("zp", 0, 32), Op.not_equal)
+    tt(slot(0, r, NAMES[0], 32), pick(("os", 0, LX), PLW), ("vr", 0, 32), Op.mult)
+    send("a0")
+    lanes_of(1, "b0")
+
+    def lanes_again():
+        for (lo, hi), x in classes(0):
+            tc(("r0", 2 * L * r + lo, 2 * L * r + hi), x)
+        pivot_lanes(("r0", 2 * L * r + L, 2 * L * (r + 1)))
+        send("r0")
+    later(lanes_again)
     update(0)
+    later(limits, 0)
 
     for t in range(1, ROUNDS):
+        if t == 3:
+            later(kept_rows, 2)
         main(t)
+        if t >= 2:
+            own("xo", t - 2)
+            later(ts, message("k%d" % t, r, r)[0], ("q2", 0, L), float(V), Op.min)
+            later(send, "k%d" % t)
         hits(t)
+        if t == 1:
+            later(lanes_of, 0, "bkey")
+        later(outputs, t - 1)
+        if t == 3:
+            later(kept_rows, 3)
         pivots(t)
-        later(after, t)
-        later(kept_rows, t)
+        if t == 1:
+            later(act, ("of1", 0, L), ("q2", 0, L), -1.0, float(V), Fn.Relu)
+            later(act, ("qf1", 0, L), ("of1", 0, L), -1.0, float(V))
+            later(pivot_lanes, ("pih", 0, L))
+            later(act, ("dead1", 0, L), ("pih", 0, L), 1.0, 1.0)
+            for x, c in ((("hit", L, L + CAP), 0), (("hit", L + CAP, LX), 1), (("sgl", lx(0), lx(0) + 1), 1), (("sgl", LX, LX + 1), 0)):
+                later(iota, x, [[0, width(x)]], c)
         if t < ROUNDS - 1:
+            later(send, "a%d" % t)
             update(t)
+            later(limits, t)
 
-    def older():
-        put("nm", 384, ("nt", 0, 384))
-        put("xo", 384, ("xt", 0, 384))
-        for t in range(ROUNDS - 1):
-            for q in range(N):
-                act(block(t, q, SIZES[t], 32), pick(("jt", 0, VT), ("evu", 8 * t + 2 * q, 8 * t + 2 * q + 2)))
-    later(older)
-    roots(3)
-    act(("jv", 0, 384), pick(("la", 0, CW), ("ju3", 0, 24)))
-    act(("xt", 384, 512), pick(("la", 0, START[2]), ("j3", 0, 8)), -1.0)
-    put("jt", 384, ("jv", 0, 384))
-    dma("s", T.yj[:, :], T["jt"][0:128:16, 0:V], "oj", [("jt", 0, V)], [], 2.0)
-    ts(pick(("nm", 0, VT), ("evu", 24, 32)), ("l3", 0, 128), -1.0, Op.mult, float(V), Op.add)
+    send("n3")
+    own("xo", 2)
+    own("nm", 2)
+    own("nm", 1)
+    collect(3, "bhit", 112, [(CLAIMS, 24, lambda q: (16 + q, 112, 4)), (VARS, 2, lambda q: (2 * q, 2 * q + 2))])
+    collect(3, "d0", 128, [(FREE, 32, by32)])
+    collect(3, "bkey", 128, [(0, 32, by32)])
+    collect(3, "b2", 128, [(NAMES[3], 32, by32)])
+    least(3, "bhit")
+    ts(("evo", 24, 32), ("bhit", 0, 8), 1024.0, Op.add)
+    act(("vid", 0, 128), ("d0", 0, 128))
+    act(("jv", 0, 384), pick(("vid", 0, 512), ("ju3", 0, 24)))
+    act(("xt", 384, 512), ("bkey", 0, 128), -1.0)
+    act(("nt", 384, 512), ("b2", 0, 128), -1.0, float(V))
+    own("xo", 3)
+    dma("y", T.yx[:, :], T["xo"][:, 0:V], "ox", [("xo", 0, V)], [], 2.5)
+    own("nm", 3)
     dma("y", T.yn[:, :], T["nm"][:, 0:V], "on", [("nm", 0, V)], [], 3.2)
-    put("xo", 128, ("xt", 384, 512), 384)
-    dma("s", T.yx[:, :], T["xo"][:, 0:V], "ox", [("xo", 0, V)], [], 2.5)
+    put("jt", "evo", 0, 384, ("jv", 0, 384))
+    dma("s", T.yj[:, :], T["jt"][0:128:16, 0:V], "oj", [("jt", 0, V)], [], 2.0)
     in_order()
     for s, v in totals.items():
         if known["g"].get(s, 0) < v:

@@ -10,17 +10,18 @@ G0 = 1288
 START = [384, 256, 128, 0]
 ID0, VAL = 124, 1024
 SHIFT = 512 * 32618
+ROUND = 1.5 * 2 ** 23
 WIDE, SLOTS = [72, 80, 88, 128], [0, 288, 608, 960]
 VARS, COUNT, CLAIMS, FREE, NAMES = 32, 34, 36, 60, [36, 44, 52, 96]
 FP, BF, F16, I32, U16 = "float32", "bfloat16", "float16", "int32", "uint16"
-CH0 = [(0, 54, 96), (96, 128, 160)]
+CH0 = [(0, 48, 96), (96, 128, 160)]
 CH = [(0, 48), (48, 112), (112, 160)]
-PART = [0, 0, 0]
+PART = [0, 0, 16]
 LISTS = {1: ("qu1", "qn"), 2: ("qu0", "qm"), 3: ("qn", "qu1")}
-CYCLE, GATHER, SCATTER, PE, WAKE, ACROSS, HOP = 0.001, 1.4, 3.0, 0.5, 0.08, 0.13, 1.7
-FIXED = {"v": 0.06, "s": 0.12, "t": 0.0, "g": 0.15}
+CYCLE, GATHER, SCATTER, PE, WAKE, ACROSS, HOP = 0.001, 1.36, 3.0, 0.5, 0.08, 0.13, 1.5
+FIXED = {"v": 0.06, "s": 0.13, "t": 0.0, "g": 0.13}
 SENDS = ["x", "r1", "a0", "r0", "a1", "k2", "a2", "k3", "a3", "n3"]
-PASSES = 1
+PASSES = 200
 DBG = []
 
 _S = {
@@ -31,17 +32,17 @@ _S = {
     "jb": (8, FP), "jb0": (8, FP), "jm": (96, FP), "sm": (96, BF), "evu": (24, U16), "evo": (32, U16),
     "er": (384, FP), "xr": (384, BF), "idr": (384, FP), "bk": (384, FP), "jv": (384, FP), "xt": (512, BF), "nt": (512, FP),
     "qs": (L, U16), "os": (LX, FP), "ns": (LX, FP), "nlb": (L, FP),
-    "qf0": (LX, FP), "qf1": (LX, FP), "of0": (LX, FP), "of1": (LX, FP), "nl0": (LX, FP), "nl1": (LX, FP), "lid": (LX, FP),
+    "qf0": (LX, FP), "qf1": (LX, FP), "of0": (LX, FP), "of1": (LX, FP), "nl0": (LX, FP), "nl1": (LX, FP),
     "qu0": (L, U16), "qu1": (L, U16), "qn": (L, U16), "qm": (L, U16), "qr0": (16 * L, FP), "qr1": (16 * L, FP),
-    "dead0": (L, BF), "dead1": (L, BF), "piv": (L, BF), "pih": (L, BF),
-    "eq": (16 * L, BF), "xv": (16 * L, BF), "msc": (16 * L, BF), "deg": (LX, I32), "si": (L, I32),
+    "dead0": (L, BF), "dead1": (L, BF), "piv": (L, BF), "neg": (128, FP),
+    "eq": (16 * L, BF), "xv": (16 * L, BF), "msc": (16 * L, BF), "deg": (LX, I32),
     "z": (LX, FP), "q2": (L, FP), "ok": (L, BF), "hit": (LX, BF), "cum": (LX, BF), "c255": (LX, BF),
     "sg": (2 * LX, BF), "sn": (2 * LX, BF), "sgl": (2 * LX, BF), "plw": (2, U16), "vx": (2, FP), "vy": (2, FP),
-    "qp": (32, U16), "vp": (32, U16), "zp": (32, FP), "xn": (544, FP), "vr": (544, FP), "cc": (544, FP), "nsc": (512, FP),
+    "qp": (32, U16), "vh": (32, F16), "zp": (32, FP), "xn": (544, FP), "vr": (32, FP), "cc": (544, FP), "nsc": (512, FP),
     "key": (512, FP), "ksc": (512, FP), "mi": (32, I32), "mj": (32, I32), "rho": (768, FP), "ne": (768, BF), "fc": (768, FP),
     "c1": (768, FP), "rev": (48, U16), "rep": (48, U16), "revf": (48, FP), "repi": (48, I32),
-    "ai": (1, I32), "aj": (1, I32), "limi": (1, I32), "lims": (1, FP), "limf": (1, FP), "lima": (1, FP),
-    "one": (128, BF), "zero": (128, BF), "idn": (128, BF), "idead": (128, BF), "ipen": (128, BF), "imx": (128, BF), "bdh": (128, BF),
+    "am": (5, FP), "limi": (1, I32), "lims": (1, FP), "limf": (1, FP), "lima": (1, FP),
+    "one": (128, BF), "zero": (512, BF), "idn": (128, BF), "idead": (128, BF), "ipen": (128, BF), "imx": (128, BF), "bdh": (128, BF),
     "bd": (128, BF), "bd8": (128, BF), "dk": (2048, BF), "wide": (512, BF), "to": (4 * 224, BF), "o16": (224, BF), "cq": (128, BF),
     "cqh": (128, BF), "c16th": (128, BF),
     "pii": (2, I32), "pij": (2, I32), "pq": (2, I32), "c16": (2, I32), "c232": (2, I32), "sc": (2, FP), "kq": (2, FP), "cv0": (2, FP),
@@ -240,36 +241,46 @@ def rank_program(g, core, T, topo):
             p = set()
             for kind, regs in (("r", reads), ("w", writes)):
                 for n, c in parts(regs):
-                    p.update(e[2] for e in seen.get(n, ()) if n in PSUM or (meet(c, e[0]) and "w" in (kind, e[1])))
+                    p.update(e[2] for e in seen.get(n, ()) if (n in PSUM or meet(c, e[0])) and
+                             ("w" in (kind, e[1]) or n in PSUM and calls[e[2]][0] != q))
             for n, c in parts(writes):
                 seen[n] = [e for e in seen.get(n, ()) if not holds(c, e[0])] + [(c, "w", i)]
             for n, c in parts(reads):
                 seen.setdefault(n, []).append((c, "r", i))
             pre.append(p - {i})
-        post = [[] for _ in calls]
-        for i, p in enumerate(pre):
-            for j in p:
-                post[j].append(i)
 
         def gap(j, i):
+            if calls[j][0] == calls[i][0] == "y":
+                return calls[j][4]
             return calls[j][5] + (ACROSS if calls[j][0] != calls[i][0] else 0.0 if calls[j][0] == "t" else WAKE)
+        needs = [[(j, gap(j, i)) for j in p] for i, p in enumerate(pre)]
 
-        def lay(order, back):
-            at, used = {}, {}
+        def lay(order):
+            at, held, used = {}, {}, {}
             for i in order:
                 d = calls[i][4]
-                if back:
-                    t0 = max([calls[i][5] - d] + [at[k] + calls[k][4] + gap(i, k) - d for k in post[i]])
-                else:
-                    t0 = max([0.0] + [at[j] + gap(j, i) for j in pre[i]])
+                t0, held[i] = max([(0.0, -1)] + [(at[j] + x, j) for j, x in needs[i]])
                 u = used.setdefault(calls[i][0], [])
-                n = 0
+                n = len(u)
+                while n and u[n - 1][1] > t0:
+                    n -= 1
                 while n < len(u) and u[n][0] < t0 + d:
-                    t0 = max(t0, u[n][1])
+                    t0, held[i] = u[n][1:]
                     n += 1
-                u.insert(n, (t0, t0 + d))
+                u.insert(n, (t0, t0 + d, i))
                 at[i] = t0
-            return at
+            last = max(at, key=lambda i: at[i] + calls[i][5])
+            return at[last] + calls[last][5], at, held, last
+
+        def first(order, i, j):
+            n = order.index(j)
+            late, need, stack = set(order[n:]), set(), [i]
+            while stack:
+                k = stack.pop()
+                if k in late and k not in need:
+                    need.add(k)
+                    stack += pre[k]
+            return order[:n] + [k for k in order[n:] if k in need] + [k for k in order[n:] if k not in need]
         order, done = [], set()
         for i in [i for i in range(len(calls)) if i not in aside] + sorted(aside):
             stack, need = [i], set()
@@ -280,16 +291,23 @@ def rank_program(g, core, T, topo):
                     stack += pre[j]
             order += sorted(need)
             done |= need
-        best = None
+        best, tried = lay(order), set()
         for _ in range(PASSES):
-            at = lay(order, False)
-            end = max(at[i] + calls[i][5] for i in at)
-            if best is None or end < best[0]:
-                best = (end, at)
-            late = lay(sorted(at, key=lambda i: (-at[i] - calls[i][5], -i)), True)
-            order = sorted(late, key=lambda i: (-late[i] - calls[i][4], i))
-            DBG.append(end)
-        for i in sorted(best[1], key=lambda i: (best[1][i], i)):
+            i, swaps = best[3], []
+            while best[2][i] >= 0:
+                if best[2][i] not in pre[i] and (i, best[2][i]) not in tried:
+                    swaps.append((i, best[2][i]))
+                i = best[2][i]
+            if not swaps:
+                break
+            tried.add(swaps[-1])
+            other = first(order, *swaps[-1])
+            new = lay(other)
+            if new[0] < best[0] - 0.01:
+                best, order = new, other
+            DBG.append(best[0])
+        DBG.append([(calls[i][0], best[1][i], calls[i][3]) for i in sorted(best[1], key=lambda i: (best[1][i], order.index(i)))])
+        for i in sorted(best[1], key=lambda i: (best[1][i], order.index(i))):
             calls[i][1]()
 
     def tc(out, in_):
@@ -317,8 +335,8 @@ def rank_program(g, core, T, topo):
         f = func or (Fn.Identity if isinstance(bias, tuple) else Fn.Copy)
         emit("s", lambda: g.scalar.activation(out=ap(out), in_=ap(in_), func=f, bias=ap(bias), scale=ap(scale)), [out], [in_, bias, scale])
 
-    def mm(out, w, x, start=True, stop=True):
-        emit("t", lambda: g.tensor.matmul(out=ap(out), lhsT=ap(w), rhs=ap(x), start=start, stop=stop), [out], [w, x])
+    def mm(out, w, x, start=True, stop=True, pace=None):
+        emit("t", lambda: g.tensor.matmul(out=ap(out), lhsT=ap(w), rhs=ap(x), start=start, stop=stop), [out], [w, x], pace)
 
     def iota(out, pattern, base, mul=0):
         if _S[out[0]][1] == I32:
@@ -339,7 +357,7 @@ def rank_program(g, core, T, topo):
             Q[q].dma_start(out=out, in_=in_).then_inc(T.sem[sem], 16)
             totals[sem] = totals.get(sem, 0) + 16
             note("dma", reads, writes, sem, totals[sem], dict(known[q]))
-        calls.append((q, issue, reads, writes, 0.05, lat))
+        calls.append((q, issue, reads, writes + [("dma" + q, 0, 1)] * (q == "y"), 0.05, lat))
 
     def pick(win, offs):
         return ("I", win, offs)
@@ -363,8 +381,10 @@ def rank_program(g, core, T, topo):
             got = [len(eng) if x == d else len(topo.engines(x, d)) for call in legs(T.cores[q], T, topo) for x, d, eng in call if d == core]
             land, s = message(name, q, r)[1], "%s_%d" % (name, q)
             totals[s] = got[0]
-            calls.append(("net", lambda a=([land], s, got[0]): note("net", [], a[0], a[1], a[2], {}), sent, [land],
-                          0.0, HOP * (1 if q in near else 2) * slow))
+            way = [("way", len(calls), len(calls) + 1)]
+            calls.append(("net", lambda: None, sent, way, 0.0, HOP * (1 if q in near else 2) * slow - 0.6))
+            calls.append(("net", lambda a=([land], s, got[0]): note("net", [], a[0], a[1], a[2], {}), way, [land, ("from", q, q + 1)],
+                          0.0, 0.5))
 
     def classes(st):
         c = 8 * st + 2 * r
@@ -408,7 +428,7 @@ def rank_program(g, core, T, topo):
         act(("c16th", 0, 128), ("one", 0, 128), 0.0625)
         select(("cqh", 0, 128), ("c16th", 0, 128), [[-32, 4], [0, 32]], Op.is_ge, 0, 1)
         select(("cq", 0, 128), ("cqh", 0, 128), [[32, 4], [0, 32]], Op.is_ge, 31, -1)
-        iota(("zero", 0, 128), [[0, 128]], 0)
+        count_up("zero", 0, 512, 0, 0)
         iota(("nlb", 0, L), [[-1, 2], [-16, H]], V)
         act(("ns", 0, L), ("nlb", 0, L), 1.0, -2.0 * r)
         for n in ("ns", "os", "z"):
@@ -417,7 +437,6 @@ def rank_program(g, core, T, topo):
             act(("nl%d" % st, 0, L), ("nlb", 0, L), 1.0, ("ncv", st, st + 1))
             for n, c in (("nl", 0), ("of", 0), ("qf", V)):
                 iota((n + str(st), L, LX), [[0, LX - L]], c)
-        iota(("lid", 0, LX), [[1, LX]], 0)
         for n in ("xo", "xm"):
             fill((n, V, V + 16), 0.0)
         fill(("hit", L, L + CAP), 1.0)
@@ -440,10 +459,10 @@ def rank_program(g, core, T, topo):
                 ts(o, ("idn", 0, 128), ("wsc", k, k + 1), Op.mult)
             else:
                 act(o, ("idn", 0, 128), ("wsc", k, k + 1))
-        for n, c in (("idead", -20480.0), ("imx", -1.0 / 4096), ("ipen", -32.0)):
+        for n, c in (("idead", -20480.0), ("imx", -4096.0), ("ipen", -32.0)):
             act((n, 0, 128), ("idn", 0, 128), c)
-        act(("bd8", 0, 128), ("bd", 0, 128), -2.0)
-        iota(("dead1", 0, L), [[0, L]], 1)
+        act(("bd8", 0, 128), ("bd", 0, 128), -4096.0 * 8192)
+        act(("neg", 0, 128), ("idn", 0, 128), -1.0)
         fill(("seg", 0, 1024), 1.0)
         fill(("seg", 0, 1024, 16), 0.0)
         count_up("kb", 0, 512, 0, 512)
@@ -461,23 +480,25 @@ def rank_program(g, core, T, topo):
             tc(("ju%d" % t, 8 * t, 8 * t + 8), ("jb", 0, 8))
             act(("jf%d" % t, 8 * t, 8 * t + 8), ("jb", 0, 8), 1.0, float(VAL + START[t]))
 
-    def lanes_of(st, bank):
+    def lanes_of(st, *banks):
         n = width(message("r%d" % st, r, r)[0])
-        for q in coming:
-            mm((bank, 0, n), to_one(r, q), message("r%d" % st, q, r)[1], q == r, q == coming[-1])
-        act(("qf%d" % st, 0, L), (bank, 0, L))
-        tc(("qu%d" % st, 0, L), (bank, 0, L))
+        for b in banks:
+            for q in coming:
+                mm((b, 0, n), to_one(r, q), message("r%d" % st, q, r)[1], q == r, q == coming[-1])
+        qf = ("qf%d" % st, 0, L)
+        later(act, qf, (banks[0], 0, L))
         if st:
-            act(("limf", 0, 1), (bank, L, L + 1), 1.0, 2048.0)
+            later(act, ("limf", 0, 1), (banks[0], L, L + 1), 1.0, 2048.0)
         else:
-            act(("dead0", 0, L), (bank, L, 2 * L), 1.0, 1.0)
-        act(("of%d" % st, 0, L), ("qf%d" % st, 0, L), -1.0, float(V))
+            act(("dead0", 0, L), (banks[0], L, 2 * L))
+        tc(("qu%d" % st, 0, L), (banks[1], 0, L) if st else qf)
         for k in range(16):
-            o, i = ("qr%d" % st, k, 16 * (L - 1) + k + 1, 16), ("qf%d" % st, 0, L)
-            if k % 2 < st:
-                ts(o, i, ("qsc", k, k + 1), Op.mult, ("qbi", k, k + 1), Op.add)
+            o = ("qr%d" % st, k, 16 * (L - 1) + k + 1, 16)
+            if k < 9 * st:
+                ts(o, (banks[1], 0, L), ("qsc", k, k + 1), Op.mult, ("qbi", k, k + 1), Op.add)
             else:
-                act(o, i, ("qsc", k, k + 1), ("qbi", k, k + 1))
+                act(o, (banks[0], 0, L) if st else qf, ("qsc", k, k + 1), ("qbi", k, k + 1))
+        later(act, ("of%d" % st, 0, L), qf, -1.0, float(V))
 
     def sums(lo, hi, stop):
         for k in range(16):
@@ -485,17 +506,12 @@ def rank_program(g, core, T, topo):
 
     def hits(t):
         st, n = t % 2, lx(t)
-        if t == 0:
-            ts(("ok", 0, L), ("d0", 0, L), ("lims", 0, 1), Op.is_le)
-            later(tc, ("deg", 0, L), ("d0", 0, L))
-        else:
-            tc(("si", 0, L), ("d0", 0, L))
-            ts(("deg", 0, L), ("si", 0, L), 4095, Op.bitwise_and)
-            ts(("ok", 0, L), ("deg", 0, L), ("lima", 0, 1), Op.is_le)
+        ts(("ok", 0, L), ("d0", 0, L), ("lima" if t else "lims", 0, 1), Op.is_le)
+        ts(("deg", 0, L), ("d0", 0, L), 255.0 / 512, Op.add)
         if t >= 2:
             mm(("bhit", 0, L), ("ipen", 0, 128), ("dead%d" % st, 0, L), True, False)
         mm(("bhit", 0, L), ("bd", 0, 128), ("ok", 0, L), t < 2, True)
-        ts(("hit", 0, L), ("bhit", 0, L), 9.0 if t < 2 else -23.0, Op.is_ge)
+        ts(("hit", 0, L), ("bhit", 0, L), 9.0, Op.is_ge)
         scan(("cum", 0, n), ("hit", 0, n), ("c255", 0, n), Op.add, Op.min)
         for c in range(2):
             ts(("sg", c * n, (c + 1) * n), ("cum", 0, n), ("sc", c, c + 1), Op.is_le)
@@ -508,19 +524,28 @@ def rank_program(g, core, T, topo):
         ts(("vx", 0, 2), ("sn", n - 1, 2 * n, n), 16.0, Op.mult, ("cv", t % 2, t % 2 + 1) if t else 2.0 * r - 1024, Op.add)
         ts(slot(t, r, 0, 32), pick(("deg", 0, LX), PLW), -1.0, Op.mult, -255.0, Op.max)
         tt(slot(t, r, VARS, 2), ("vx", 0, 2), ("vy", 0, 2), Op.add)
-        later(ts, slot(t, r, COUNT, 2), ("cum", L - 2, L), float(CAP), Op.min)
+        ts(slot(t, r, COUNT, 2), ("cum", L - 2, L), float(CAP), Op.min)
 
     def limits(t):
         for d in coming:
             w = ("cq", 0, 128) if t else ("o16", 96 - 32 * d, 224 - 32 * d)
             mm(("bkey", 0, 1), w, slot(t, d, COUNT + 1, 1), d == r, d == coming[-1])
-        tc(("ai", 0, 1), ("bkey", 0, 1))
-        ts(("aj", 0, 1), ("ai", 0, 1), 7, Op.bitwise_and)
-        tt(("lima", 0, 1), ("limf", 0, 1), ("aj", 0, 1), Op.add)
+        act(("am", 0, 1), ("bkey", 0, 1))
+        act(("am", 1, 2), ("am", 0, 1), 0.125, -0.4375)
+        act(("am", 2, 3), ("am", 1, 2), 1.0, ROUND)
+        act(("am", 3, 4), ("am", 2, 3), -8.0, 8 * ROUND)
+        act(("am", 4, 5), ("am", 3, 4), 1.0, ("am", 0, 1))
+        act(("lima", 0, 1), ("am", 4, 5), 1.0, ("limf", 0, 1))
 
-    def pivot_lanes(out):
-        ts(("piv", 0, L), ("cum", 0, L), float(CAP), Op.is_le, 2.0, Op.mult)
-        tt(out, ("piv", 0, L), ("hit", 0, L), Op.mult)
+    def pivot_lanes(t):
+        if t == 0:
+            ts(("piv", 0, L), ("cum", 0, L), float(CAP), Op.is_le, 2.0, Op.mult)
+            tt(("r0", 2 * L * r + L, 2 * L * (r + 1)), ("piv", 0, L), ("hit", 0, L), Op.mult)
+        else:
+            mm(("bkey", 0, L), ("idn", 0, 128), ("cum", 0, L), True, False)
+            for k in range(2):
+                mm(("bkey", 0, L), ("ipen", 0, 128), ("hit", 0, L), False, k == 1)
+            act(("dead1", 0, L), ("bkey", 0, L), -2.0, -62.0, Fn.Relu)
 
     def put(table, lists, lo, hi, src):
         tc(pick((table, 0, VT), (lists, lo // 16, hi // 16)), src)
@@ -537,7 +562,9 @@ def rank_program(g, core, T, topo):
             bank = ("b%d" % c, 0, hi - lo)
             next_of("covers")
             tt(("eq", 16 * lo, 16 * hi), pick(("en", 0, G0), (qu, lo, hi)), ("qr%d" % st, 16 * lo, 16 * hi), Op.is_equal)
-            mm(bank, ("idead", 0, 128), ("dead%d" % st, lo, hi), True, False)
+            mm(bank, ("idead", 0, 128), ("one", 0, hi - lo), True, False)
+            if t >= 2:
+                mm(bank, ("idead", 0, 128), ("dead%d" % st, lo, hi), False, False)
             for k in range(16):
                 if k == 15 and hi == L:
                     next_of("sums")
@@ -577,30 +604,33 @@ def rank_program(g, core, T, topo):
         nl = ("nl%d" % st, 0, LX)
         tc(("qp", 0, 32), pick(("qf%d" % st, 0, LX), PLW))
         act(("key", 0, 512), pick(("rs", 0, G0), ("qp", 0, 32)))
-        tc(("vp", 0, 32), pick(("lid", 0, LX), PLW))
-        variables(t)
-        if t == ROUNDS - 1:
-            own("nm", 0)
-        act(("vr", 0, 512), pick(nl, ("vp", 0, 32)))
-        act(("vr", 512, 544), pick(nl, PLW))
-        act(("b1", 0, 544), ("vr", 0, 544))
         act(("xn", 0, 512), pick(("en", 0, G0), ("qp", 0, 32)))
         act(("zp", 0, 32), pick(("z", 0, LX), PLW), -1.0)
+        tc(("vh", 0, 32), pick(nl, PLW))
+        tt(("xn", 512, 544), pick(("of%d" % st, 0, LX), PLW), ("zp", 0, 32), Op.add)
+        mm(("b1", 0, 512), ("idn", 0, 128), ("zero", 0, 512), True, False)
+        for k in range(16):
+            mm(("b1", k, 512, 16), ("idn", 0, 128), ("vh", 0, 32), False, False)
+        mm(("b1", 512, 544), ("idn", 0, 128), ("vh", 0, 32), True, False)
+        mm(("b1", 512, 544), ("neg", 0, 128), ("xn", 512, 544), False, True, 4 * PE)
+        mm(("b1", 0, 512), ("neg", 0, 128), ("xn", 0, 512), False, True, 4 * PE)
+        act(("b0", 0, 544), ("b1", 0, 544), 2048.0, 0.0, Fn.Abs)
         if t == ROUNDS - 1:
-            ts(slot(t, r, FREE, 32), pick(nl, PLW), -1.0, Op.mult, float(V), Op.add)
+            ts(slot(t, r, FREE, 32), ("vh", 0, 32), -1.0, Op.mult, float(V), Op.add)
+        variables(t)
         scan(("ksc", 0, 512), ("kb", 0, 512), ("key", 0, 512), Op.add, Op.max)
         tc(("mi", 0, 32), ("ksc", 15, 512, 16))
         ts(("mj", 0, 32), ("mi", 0, 32), 511, Op.bitwise_and)
         later(act, ("rho", 0, n), pick(("jf%d" % (t - 1), 0, 8 * t), ("rep", 0, 16 * t)), 1.0, float(-VAL - ID0))
-        later(ts, ("c1", 31, n, 32), ("c1", 0, 8 * t), ("cb", t, t + 1), Op.mult)
+        later(act, ("c1", 31, n, 32), ("c1", 0, 8 * t), ("cb", t, t + 1))
         tt(("ne", 0, n), pick(("mj", 0, 32), ("rev", 0, 16 * t)), ("rho", 0, n), Op.not_equal)
         scan(("fc", 0, n), ("ne", 0, n), ("c1", 0, n), Op.mult, Op.add, float(VAL))
         tt(slot(t, r, CLAIMS, 8 * t), ("fc", 31, n, 32), ("jf%d" % (t - 1), 0, 8 * t), Op.min)
         if t == ROUNDS - 1:
             send("a3")
-        tt(("xn", 512, 544), pick(("of%d" % st, 0, LX), PLW), ("zp", 0, 32), Op.add)
-        tt(("b0", 0, 544), ("xn", 0, 544), ("b1", 0, 544), Op.not_equal)
-        tt(("cc", 0, 544), ("xn", 0, 544), ("b0", 0, 544), Op.mult)
+        tt(("cc", 0, 544), ("xn", 0, 544), ("b0", 0, 544), Op.min)
+        if t < ROUNDS - 1:
+            roots(t)
         scan(("nsc", 0, 512), ("seg", 0, 512), ("cc", 0, 512), Op.mult, Op.max)
         tt(slot(t, r, NAMES[t], 32), ("cc", 512, 544), ("nsc", 15, 512, 16), Op.max)
 
@@ -608,40 +638,42 @@ def rank_program(g, core, T, topo):
         scan(("jm", 0, 32 * t), ("sm", 0, 32 * t), (bank, 16, 16 + 32 * t), Op.add, Op.min)
         ts(("ju%d" % t, 0, 8 * t), ("jm", 3, 32 * t, 4), float(-VAL - START[t]), Op.add)
 
+    def spread(t, part, k, out):
+        for q in coming if t == 0 else range(N):
+            mm(out(q), to_all(q if t else r), slot(t, r if t else q, part, k))
+
+    def roots(t):
+        n, new = 128 * (t + 1), ("la", START[t], START[t] + 128)
+        spread(t, 0, 32, lambda q: ("d0", 32 * q, 32 * q + 32))
+        spread(t, VARS, 2, lambda q: ("bhit", 2 * q, 2 * q + 2))
+        if t:
+            spread(t, CLAIMS, 8 * t, lambda q: ("bhit", 16 + q, 16 + 32 * t, 4))
+            act(new, ("d0", 0, 128))
+            least(t, "bhit")
+            act(("xr", 0, n), pick(("la", START[t], 512), ("ju%d" % t, 0, n // 16)), 1.0 / 4096)
+            later(act, ("jf%d" % t, 0, 8 * t), ("jm", 3, 32 * t, 4))
+        else:
+            act(("xr", 0, n), ("d0", 0, 128), 1.0 / 4096)
+            later(act, new, ("xr", 0, n), 4096.0)
+        ts(("evu", 8 * t, 8 * t + 8), ("bhit", 0, 8), 1024.0, Op.add)
+
     def update(t):
-        n = 128 * (t + 1)
+        n, new = 128 * (t + 1), ("ln", START[t], START[t] + 128)
         ju = ("ju%d" % t, 0, n // 16)
         xr, er = ("xr", 0, n), ("er", 0, n)
-
-        def spread(part, k, out):
-            for q in coming if t == 0 else range(N):
-                mm(out(q), to_all(q if t else r), slot(t, r if t else q, part, k))
+        spread(t, NAMES[t], 32, lambda q: ("b2", 32 * q, 32 * q + 32))
         if t:
-            spread(CLAIMS, 8 * t, lambda q: ("bhit", 16 + q, 16 + 32 * t, 4))
-        spread(VARS, 2, lambda q: ("bhit", 2 * q, 2 * q + 2))
-        spread(0, 32, lambda q: ("d0", 32 * q, 32 * q + 32))
-        spread(NAMES[t], 32, lambda q: ("b2", 32 * q, 32 * q + 32))
-        if t:
-            least(t, "bhit")
-        ts(("evu", 8 * t, 8 * t + 8), ("bhit", 0, 8), 1024.0, Op.add)
-        new = (START[t], START[t] + 128)
-        if t:
-            act(("la",) + new, ("d0", 0, 128))
-            act(xr, pick(("la", START[t], 512), ju), 4096.0)
-            act(("ln",) + new, ("b2", 0, 128))
+            act(new, ("b2", 0, 128))
             next_of("roots")
             act(er, pick(("ln", START[t], 512), ju))
             put("xm", "evu", 0, n, xr)
             put("en", "evu", 0, n, er)
-            later(act, ("jf%d" % t, 0, 8 * t), ("jm", 3, 32 * t, 4))
         else:
             act(er, ("b2", 0, 128))
-            next_of("roots")
-            act(xr, ("d0", 0, 128), 4096.0)
+            roots(0)
             put("en", "evu", 0, n, er)
             put("xm", "evu", 0, n, xr)
-            later(act, ("la",) + new, xr, 1.0 / 4096)
-            later(act, ("ln",) + new, er)
+            later(act, new, er)
         mm(("bkey", 0, n), ("bd8", 0, 128), xr)
         next_of("roots")
         act(("bk", 0, n), ("bkey", 0, n))
@@ -685,22 +717,22 @@ def rank_program(g, core, T, topo):
     dma("y", T["nm"][:, 0:V], T.nb[:, :], "dn", [], [("nm", 0, V)], 4.2)
     dma("s", T["xo"][:, 0:V], T.xs[:, :], "do", [], [("xo", 0, V)], 4.2)
     dma("s", T["limi"][:, 0:1], T.lim[:, 0:1], "dl", [], [("limi", 0, 1)], 4.2)
-    dma("y", T["xm"][32 * r:32 * r + 32, 0:V], T.xs[32 * r:32 * r + 32, :], "dx_%d" % r, [("nm", 0, V)], [("xm", r, V, N)], 1.5)
-    send("x", 2.4)
+    dma("y", T["xm"][32 * r:32 * r + 32, 0:V], T.xs[32 * r:32 * r + 32, :], "dx_%d" % r, [("nm", 0, V)], [("xm", r, V, N)], 6.0)
+    send("x", 2.6)
     for q in near + far:
         dma("y", T["xm"][32 * q:32 * q + 32, 0:V], T["lx"][:, 320 * q:320 * q + 320], "dx_%d" % q, [message("x", q, r)[1]], [("xm", q, V, N)], 1.5)
     later(constants)
 
     for (lo, hi), x in classes(0):
         tc(("qs", lo, hi), x)
-    for (lo, hi), x in classes(1):
-        tc(("r1", 168 * r + lo, 168 * r + hi), x)
-    ts(("r1", 168 * r + L, 168 * r + L + 1), ("limi", 0, 1), -2048.0, Op.add)
-    send("r1")
     for lo, mid, hi in CH0:
         for f, a, z in ((act, lo, mid), (tc, mid, hi)):
             f(("xv", 16 * a, 16 * z), pick(("xo", 0, G0), ("qs", a, z)))
         sums(lo, hi, True)
+    for (lo, hi), x in classes(1):
+        tc(("r1", 168 * r + lo, 168 * r + hi), x)
+    ts(("r1", 168 * r + L, 168 * r + L + 1), ("limi", 0, 1), -2048.0, Op.add)
+    send("r1")
     for (lo, hi), x in classes(0):
         later(act, ("os", lo, hi), x, -1.0, float(V))
     hits(0)
@@ -709,28 +741,24 @@ def rank_program(g, core, T, topo):
     tt(("vr", 0, 32), pick(("os", 0, LX), PLW), ("zp", 0, 32), Op.not_equal)
     tt(slot(0, r, NAMES[0], 32), pick(("os", 0, LX), PLW), ("vr", 0, 32), Op.mult)
     send("a0")
-    lanes_of(1, "b0")
-
-    def lanes_again():
-        for (lo, hi), x in classes(0):
-            tc(("r0", 2 * L * r + lo, 2 * L * r + hi), x)
-        pivot_lanes(("r0", 2 * L * r + L, 2 * L * (r + 1)))
-        send("r0")
-    later(lanes_again)
+    for (lo, hi), x in classes(0):
+        tc(("r0", 2 * L * r + lo, 2 * L * r + hi), x)
+    pivot_lanes(0)
+    send("r0")
+    lanes_of(1, "bkey", "b1")
     update(0)
     later(limits, 0)
+    later(lanes_of, 0, "bkey")
 
     for t in range(1, ROUNDS):
         if t == 3:
             later(kept_rows, 2)
         main(t)
         if t >= 2:
-            own("xo", t - 2)
-            later(ts, message("k%d" % t, r, r)[0], ("q2", 0, L), float(V), Op.min)
-            later(send, "k%d" % t)
+            ts(message("k%d" % t, r, r)[0], ("q2", 0, L), float(V), Op.min)
+            send("k%d" % t)
+            later(own, "xo", t - 2)
         hits(t)
-        if t == 1:
-            later(lanes_of, 0, "bkey")
         later(outputs, t - 1)
         if t == 3:
             later(kept_rows, 3)
@@ -738,8 +766,7 @@ def rank_program(g, core, T, topo):
         if t == 1:
             later(act, ("of1", 0, L), ("q2", 0, L), -1.0, float(V), Fn.Relu)
             later(act, ("qf1", 0, L), ("of1", 0, L), -1.0, float(V))
-            later(pivot_lanes, ("pih", 0, L))
-            later(act, ("dead1", 0, L), ("pih", 0, L), 1.0, 1.0)
+            later(pivot_lanes, 1)
             for x, c in ((("hit", L, L + CAP), 0), (("hit", L + CAP, LX), 1), (("sgl", lx(0), lx(0) + 1), 1), (("sgl", LX, LX + 1), 0)):
                 later(iota, x, [[0, width(x)]], c)
         if t < ROUNDS - 1:
@@ -748,9 +775,8 @@ def rank_program(g, core, T, topo):
             later(limits, t)
 
     send("n3")
+    put("nm", "evo", 0, 384, ("nt", 0, 384))
     own("xo", 2)
-    own("nm", 2)
-    own("nm", 1)
     collect(3, "bhit", 112, [(CLAIMS, 24, lambda q: (16 + q, 112, 4)), (VARS, 2, lambda q: (2 * q, 2 * q + 2))])
     collect(3, "d0", 128, [(FREE, 32, by32)])
     collect(3, "bkey", 128, [(0, 32, by32)])
@@ -758,14 +784,14 @@ def rank_program(g, core, T, topo):
     least(3, "bhit")
     ts(("evo", 24, 32), ("bhit", 0, 8), 1024.0, Op.add)
     act(("vid", 0, 128), ("d0", 0, 128))
-    act(("jv", 0, 384), pick(("vid", 0, 512), ("ju3", 0, 24)))
     act(("xt", 384, 512), ("bkey", 0, 128), -1.0)
+    act(("jv", 0, 384), pick(("vid", 0, 512), ("ju3", 0, 24)))
     act(("nt", 384, 512), ("b2", 0, 128), -1.0, float(V))
     own("xo", 3)
     dma("y", T.yx[:, :], T["xo"][:, 0:V], "ox", [("xo", 0, V)], [], 2.5)
+    put("jt", "evo", 0, 384, ("jv", 0, 384))
     own("nm", 3)
     dma("y", T.yn[:, :], T["nm"][:, 0:V], "on", [("nm", 0, V)], [], 3.2)
-    put("jt", "evo", 0, 384, ("jv", 0, 384))
     dma("s", T.yj[:, :], T["jt"][0:128:16, 0:V], "oj", [("jt", 0, V)], [], 2.0)
     in_order()
     for s, v in totals.items():

@@ -10,42 +10,48 @@ G0 = 1288
 START = [384, 256, 128, 0]
 ID0, VAL = 124, 1024
 SHIFT = 512 * 32618
-ROUND = 1.5 * 2 ** 23
+ROUND, HALF = 1.5 * 2 ** 23, 255.0 / 512
 WIDE, SLOTS = [72, 80, 88, 128], [0, 288, 608, 960]
-VARS, COUNT, CLAIMS, FREE, NAMES = 32, 34, 36, 60, [36, 44, 52, 96]
+VARS, COUNT, FREE, CLAIMS, NAMES = 32, 34, 34, [None, 36, 36, 72], [36, 44, 52, 96]
 FP, BF, F16, I32, U16 = "float32", "bfloat16", "float16", "int32", "uint16"
-CH0 = [(0, 48, 96), (96, 128, 160)]
-CH = [(0, 48), (48, 112), (112, 160)]
-PART = [0, 0, 16]
+CH = [(0, 52), (52, 116), (116, 160)]
+PART = [0, 0, 20]
 LISTS = {1: ("qu1", "qn"), 2: ("qu0", "qm"), 3: ("qn", "qu1")}
-CYCLE, GATHER, SCATTER, PE, WAKE, ACROSS, HOP = 0.001, 1.36, 3.0, 0.5, 0.08, 0.13, 1.5
+CYCLE, GATHER, SCATTER, PE, WAKE, ACROSS, HOP = 0.001, 1.36, 3.0, 0.6, 0.06, 0.19, 1.5
 FIXED = {"v": 0.06, "s": 0.13, "t": 0.0, "g": 0.13}
-SENDS = ["x", "r1", "a0", "r0", "a1", "k2", "a2", "k3", "a3", "n3"]
+SENDS = ["x", "r1", "a0", "r0", "a1", "k2", "a2", "k3", "s3", "c3", "n3"]
+SLOW, BACK = {"x": 2.5, "r1": 1.0, "a0": 1.0, "s3": 1.0, "c3": 1.0, "n3": 1.0}, 1.4
+RS, DKV = "g", 8
+ROOM, SEND = 1.0, 0.7
+KEYS = {1: [(0, 128)], 2: [(0, 128), (128, 192), (192, 256)], 3: [(0, 192), (192, 256), (256, 320), (320, 384)]}
+KEYV = [0, 16, 20, 24]
+EVEN = 0.01
 PASSES = 200
+SHARE = [8, 9]
 DBG = []
 
 _S = {
     "nm": (VT, FP), "en": (VT, FP), "rs": (VT, FP), "jt": (VT, FP), "xm": (VT, BF), "xo": (VT, BF),
     "sx": (V, BF), "lx": (V, BF), "r1": (4 * 168, F16), "r0": (4 * 2 * L, F16), "ra": (1472, F16), "rk": (8 * L, F16),
-    "la": (512, FP), "ln": (512, FP), "vid": (512, FP), "idt": (512, FP),
-    "jf0": (8, FP), "jf1": (16, FP), "jf2": (24, FP), "ju0": (8, U16), "ju1": (16, U16), "ju2": (24, U16), "ju3": (24, U16),
+    "la": (512, FP), "ln": (512, FP), "vid": (512, FP),
+    "jf0": (8, FP), "jf1": (16, FP), "jf2": (24, FP), "ju": (24, U16), "ju3": (24, U16),
     "jb": (8, FP), "jb0": (8, FP), "jm": (96, FP), "sm": (96, BF), "evu": (24, U16), "evo": (32, U16),
     "er": (384, FP), "xr": (384, BF), "idr": (384, FP), "bk": (384, FP), "jv": (384, FP), "xt": (512, BF), "nt": (512, FP),
     "qs": (L, U16), "os": (LX, FP), "ns": (LX, FP), "nlb": (L, FP),
     "qf0": (LX, FP), "qf1": (LX, FP), "of0": (LX, FP), "of1": (LX, FP), "nl0": (LX, FP), "nl1": (LX, FP),
     "qu0": (L, U16), "qu1": (L, U16), "qn": (L, U16), "qm": (L, U16), "qr0": (16 * L, FP), "qr1": (16 * L, FP),
     "dead0": (L, BF), "dead1": (L, BF), "piv": (L, BF), "neg": (128, FP),
-    "eq": (16 * L, BF), "xv": (16 * L, BF), "msc": (16 * L, BF), "deg": (LX, I32),
+    "eq": (16 * L, BF), "xv": (16 * L, BF), "msc": (16 * L, BF), "deg": (LX, FP), "half": (128, BF),
     "z": (LX, FP), "q2": (L, FP), "ok": (L, BF), "hit": (LX, BF), "cum": (LX, BF), "c255": (LX, BF),
-    "sg": (2 * LX, BF), "sn": (2 * LX, BF), "sgl": (2 * LX, BF), "plw": (2, U16), "vx": (2, FP), "vy": (2, FP),
-    "qp": (32, U16), "vh": (32, F16), "zp": (32, FP), "xn": (544, FP), "vr": (32, FP), "cc": (544, FP), "nsc": (512, FP),
-    "key": (512, FP), "ksc": (512, FP), "mi": (32, I32), "mj": (32, I32), "rho": (768, FP), "ne": (768, BF), "fc": (768, FP),
-    "c1": (768, FP), "rev": (48, U16), "rep": (48, U16), "revf": (48, FP), "repi": (48, I32),
+    "sg": (2 * LX, BF), "sn": (2 * LX, BF), "sgl": (2 * LX, BF), "plw": (2, U16), "vx": (2, FP), "vy": (4, FP),
+    "qp": (32, U16), "vh": (32, F16), "zp": (32, FP), "xn": (544, FP), "vr": (32, FP), "cc": (544, F16), "nsc": (512, F16),
+    "key": (512, FP), "ksc": (512, FP), "mi": (32, I32), "mj": (32, I32), "rho": (768, FP), "ne": (768, BF), "fc": (768, F16),
+    "c1": (768, BF), "rev": (48, U16), "rep": (48, U16), "revf": (48, FP), "repi": (48, I32),
     "am": (5, FP), "limi": (1, I32), "lims": (1, FP), "limf": (1, FP), "lima": (1, FP),
     "one": (128, BF), "zero": (512, BF), "idn": (128, BF), "idead": (128, BF), "ipen": (128, BF), "imx": (128, BF), "bdh": (128, BF),
     "bd": (128, BF), "bd8": (128, BF), "dk": (2048, BF), "wide": (512, BF), "to": (4 * 224, BF), "o16": (224, BF), "cq": (128, BF),
     "cqh": (128, BF), "c16th": (128, BF),
-    "pii": (2, I32), "pij": (2, I32), "pq": (2, I32), "c16": (2, I32), "c232": (2, I32), "sc": (2, FP), "kq": (2, FP), "cv0": (2, FP),
+    "pii": (2, I32), "pij": (2, I32), "pq": (3, FP), "c16": (2, I32), "sc": (2, FP), "kq": (2, FP), "cv0": (2, FP),
     "cv": (2, FP), "ncv": (2, FP), "cb0": (4, FP), "cb": (4, FP),
     "ck": (16, FP), "qsc": (16, FP), "qbi": (16, FP), "wsc": (16, FP), "seg": (1024, BF), "kb": (512, FP),
 }
@@ -54,7 +60,7 @@ SMALL = [n for n, (c, d) in _S.items() if c <= 16 and n != "limi"]
 SCRATCH = {n: ("sbuf", [128, c], d) for n, (c, d) in _S.items() if n not in SMALL}
 SCRATCH.update({"small_" + d: ("sbuf", [128, 16 * len(SMALL)], d) for d in (FP, I32, U16)})
 SCRATCH.update({n: ("psum", [128, c], FP) for n, c in PSUM.items()})
-SEMAPHORES = (["qv", "qs", "qt", "qg", "dn", "do", "dl", "on", "ox", "oj", "loc"]
+SEMAPHORES = (["qv", "qs", "qt", "qg", "dn", "dm", "do", "dl", "on", "ox", "oj", "loc"]
               + [x + "_" + str(q) for x in SENDS + ["ds", "dx"] for q in range(N)])
 
 
@@ -69,7 +75,8 @@ def message(name, q, d):
     t = int(name[1])
     cols = {"r": ("r1", 168 * q, 168 * q + L + 1) if t else ("r0", 2 * L * q, 2 * L * (q + 1)),
             "k": ("rk", L * (4 * (t % 2) + q), L * (4 * (t % 2) + q + 1)),
-            "a": slot(t, q, 0, NAMES[t] + 32 if t < 3 else FREE + 32), "n": slot(t, q, NAMES[t], 32)}[name[0]]
+            "a": slot(t, q, 0, NAMES[t] + 32), "s": slot(t, q, 0, FREE + 32), "c": slot(t, q, CLAIMS[3], 24),
+            "n": slot(t, q, NAMES[t], 32)}[name[0]]
     return cols, cols
 
 
@@ -235,6 +242,9 @@ def rank_program(g, core, T, topo):
         f(*args)
         aside.update(range(n, len(calls)))
 
+    def call(f, *args):
+        f(*args)
+
     def in_order():
         seen, pre = {}, []
         for i, (q, issue, reads, writes, c, lat) in enumerate(calls):
@@ -250,7 +260,7 @@ def rank_program(g, core, T, topo):
             pre.append(p - {i})
 
         def gap(j, i):
-            if calls[j][0] == calls[i][0] == "y":
+            if calls[i][3][-1:] == calls[j][3][-1:] == [("dma", 0, 1)]:
                 return calls[j][4]
             return calls[j][5] + (ACROSS if calls[j][0] != calls[i][0] else 0.0 if calls[j][0] == "t" else WAKE)
         needs = [[(j, gap(j, i)) for j in p] for i, p in enumerate(pre)]
@@ -258,7 +268,7 @@ def rank_program(g, core, T, topo):
         def lay(order):
             at, held, used = {}, {}, {}
             for i in order:
-                d = calls[i][4]
+                d = calls[i][4] * (ROOM if i in aside else 1.0)
                 t0, held[i] = max([(0.0, -1)] + [(at[j] + x, j) for j, x in needs[i]])
                 u = used.setdefault(calls[i][0], [])
                 n = len(u)
@@ -291,7 +301,7 @@ def rank_program(g, core, T, topo):
                     stack += pre[j]
             order += sorted(need)
             done |= need
-        best, tried = lay(order), set()
+        best, tried, chain = lay(order), set(), [i for i in order if i not in aside]
         for _ in range(PASSES):
             i, swaps = best[3], []
             while best[2][i] >= 0:
@@ -303,7 +313,7 @@ def rank_program(g, core, T, topo):
             tried.add(swaps[-1])
             other = first(order, *swaps[-1])
             new = lay(other)
-            if new[0] < best[0] - 0.01:
+            if new[0] < best[0] - 0.01 or new[0] < best[0] + EVEN and sum(new[1][k] - best[1][k] for k in chain) < -1.0:
                 best, order = new, other
             DBG.append(best[0])
         DBG.append([(calls[i][0], best[1][i], calls[i][3]) for i in sorted(best[1], key=lambda i: (best[1][i], order.index(i)))])
@@ -348,16 +358,16 @@ def rank_program(g, core, T, topo):
         for a in range(lo, hi, 256):
             iota((n, a, min(a + 256, hi)), [[step, min(a + 256, hi) - a]], base + step * a)
 
-    def select(out, in_, pattern, op, base, mul):
-        emit("g", lambda: g.affine_select(ap(out), ap(in_), pattern, op, 0.0, base, mul), [out], [in_])
+    def select(out, in_, pattern, op, base, mul, other=0.0):
+        emit("g", lambda: g.affine_select(ap(out), ap(in_), pattern, op, other, base, mul), [out], [in_])
 
     def dma(q, out, in_, sem, reads, writes, lat):
         def issue():
             wait_for(q, deps("dma", reads, writes))
             Q[q].dma_start(out=out, in_=in_).then_inc(T.sem[sem], 16)
-            totals[sem] = totals.get(sem, 0) + 16
-            note("dma", reads, writes, sem, totals[sem], dict(known[q]))
-        calls.append((q, issue, reads, writes + [("dma" + q, 0, 1)] * (q == "y"), 0.05, lat))
+            totals[sem] = 16
+            note("dma", reads, writes, sem, 16, dict(known[q]))
+        calls.append((q, issue, reads, writes + [("dma", 0, 1)], 0.05, lat))
 
     def pick(win, offs):
         return ("I", win, offs)
@@ -366,23 +376,23 @@ def rank_program(g, core, T, topo):
     far = [q for q in range(N) if q != r and q not in near]
     coming = [r] + near + far
 
-    def send(name, slow=1.0):
+    def send(name):
         mine = [message(name, r, d)[0] for d in near + far]
 
         def issue():
-            wait_for("g", deps("g", mine, []))
             for call in legs(core, T, topo):
+                wait_for("g", deps("g", [message(name, r, T.rank_of(d))[0] for x, d, eng in call], []))
                 g.remote_dma_fused([transfer(T, topo, core, x, eng, *message(name, r, T.rank_of(d)), "%s_%d" % (name, r))
                                     for x, d, eng in call], local_sem=T.sem.loc)
                 totals["loc"] = totals.get("loc", 0) + sum(len(eng) for x, d, eng in call)
         sent = [("sent", len(calls), len(calls) + 1)]
-        calls.append(("g", issue, mine, [("sends", 0, 1)] + sent, 0.5, 0.5))
+        calls.append(("g", issue, mine, [("sends", 0, 1)] + sent, SEND, 0.5))
         for q in near + far:
             got = [len(eng) if x == d else len(topo.engines(x, d)) for call in legs(T.cores[q], T, topo) for x, d, eng in call if d == core]
             land, s = message(name, q, r)[1], "%s_%d" % (name, q)
             totals[s] = got[0]
             way = [("way", len(calls), len(calls) + 1)]
-            calls.append(("net", lambda: None, sent, way, 0.0, HOP * (1 if q in near else 2) * slow - 0.6))
+            calls.append(("net", lambda: None, sent, way, 0.0, HOP * (1 if q in near else 2) * SLOW.get(name, BACK) - 0.6))
             calls.append(("net", lambda a=([land], s, got[0]): note("net", [], a[0], a[1], a[2], {}), way, [land, ("from", q, q + 1)],
                           0.0, 0.5))
 
@@ -407,14 +417,16 @@ def rank_program(g, core, T, topo):
         iota(("c16", 0, 2), [[16, 2]], 0)
         ts(("pij", 0, 2), ("pii", 0, 2), 15, Op.bitwise_and)
         tt(("sc", 0, 2), ("pij", 0, 2), ("c16", 0, 2), Op.add)
-        iota(("c232", 0, 2), [[30, 2]], 2)
-        ts(("pq", 0, 2), ("pii", 0, 2), 5, Op.arith_shift_right)
-        tt(("kq", 0, 2), ("pq", 0, 2), ("c232", 0, 2), Op.mult)
+        iota(("pq", 0, 1), [[0, 1]], 0, 1)
+        act(("pq", 1, 2), ("pq", 0, 1), 1.0 / 32, -31.0 / 64)
+        act(("pq", 2, 3), ("pq", 1, 2), 1.0, ROUND)
+        for i, c in enumerate((2, 32)):
+            act(("kq", i, i + 1), ("pq", 2, 3), float(c), -c * ROUND)
         iota(("cv0", 0, 2), [[8, 2]], -1024)
-        ts(("cv", 0, 2), ("cv0", 0, 2), ("kq", 0, 1), Op.add)
-        ts(("ncv", 0, 2), ("cv", 0, 2), -1.0, Op.mult, -1024.0, Op.add)
+        act(("cv", 0, 2), ("cv0", 0, 2), 1.0, ("kq", 0, 1))
+        act(("ncv", 0, 2), ("cv", 0, 2), -1.0, -1024.0)
         iota(("cb0", 0, 4), [[-128, 4]], VAL + START[0])
-        ts(("cb", 0, 4), ("cb0", 0, 4), ("kq", 1, 2), Op.add)
+        act(("cb", 0, 4), ("cb0", 0, 4), 1.0, ("kq", 1, 2))
         fill(("one", 0, 128), 1.0)
         select(("idn", 0, 128), ("one", 0, 128), [[-1, 128]], Op.is_equal, 0, 1)
         select(("bdh", 0, 128), ("one", 0, 128), [[-16, 8], [0, 16]], Op.is_ge, 0, 1)
@@ -422,17 +434,16 @@ def rank_program(g, core, T, topo):
         fill(("to", 0, 4 * 224), 0.0)
         for q in range(N):
             select(to_all(q), ("one", 0, 128), [[0, 4], [-1, 32]], Op.is_equal, -32 * q, 1)
-            act(("to", 224 * q + 96, 224 * q + 128), ("idn", 32 * q, 32 * q + 32))
-        fill(("o16", 0, 224), 0.0)
-        fill(("o16", 96, 128), 0.0625)
-        act(("c16th", 0, 128), ("one", 0, 128), 0.0625)
+            select(("to", 224 * q + 96, 224 * q + 128), ("one", 0, 32), [[-1, 32]], Op.is_equal, -32 * q, 1)
+        count_up("zero", 0, 512, 0, 0)
+        select(("o16", 0, 224), ("zero", 0, 224), [[1, 7], [0, 32]], Op.not_equal, -3, 0, 0.0625)
+        select(("c16th", 0, 128), ("zero", 0, 128), [[0, 128]], Op.is_gt, 0, 0, 0.0625)
         select(("cqh", 0, 128), ("c16th", 0, 128), [[-32, 4], [0, 32]], Op.is_ge, 0, 1)
         select(("cq", 0, 128), ("cqh", 0, 128), [[32, 4], [0, 32]], Op.is_ge, 31, -1)
-        count_up("zero", 0, 512, 0, 0)
         iota(("nlb", 0, L), [[-1, 2], [-16, H]], V)
-        act(("ns", 0, L), ("nlb", 0, L), 1.0, -2.0 * r)
+        iota(("ns", 0, L), [[-1, 2], [-16, H]], V - 2 * r)
         for n in ("ns", "os", "z"):
-            fill((n, L, LX), 0.0)
+            iota((n, L, LX), [[0, LX - L]], 0)
         for st in range(2):
             act(("nl%d" % st, 0, L), ("nlb", 0, L), 1.0, ("ncv", st, st + 1))
             for n, c in (("nl", 0), ("of", 0), ("qf", V)):
@@ -441,76 +452,85 @@ def rank_program(g, core, T, topo):
             fill((n, V, V + 16), 0.0)
         fill(("hit", L, L + CAP), 1.0)
         fill(("c255", 0, LX), 255.0)
-        fill(("deg", L, LX), 0)
+        fill(("deg", L, LX), ROUND)
         fill(("sgl", 0, 2 * LX), 1.0)
         fill(("sgl", lx(0), lx(0) + 1), 0.0)
         tc(("lims", 0, 1), ("limi", 0, 1))
-        count_up("en", 0, G0, 0, -1)
-        count_up("rs", 0, G0, 0, -SHIFT - 16384)
-        count_up("idt", 0, 512, 1, -ID0 - SHIFT)
+        for lo in range(0, G0, 322):
+            fill(("en", lo, lo + 322), -1.0)
+            if RS == "g":
+                iota(("rs", lo, lo + 322), [[0, 322]], -SHIFT - 16384)
+            elif RS == "v":
+                fill(("rs", lo, lo + 322), -SHIFT - 16384.0)
+            else:
+                act(("rs", lo, lo + 322), ("xo", 0, 322), 0.0, -SHIFT - 16384.0)
         count_up("jt", 0, VT, 1, 0)
+        count_up("c1", 0, 768, 0, 1)
         iota(("ck", 0, 16), [[1, 16]], 0)
         ts(("qsc", 0, 16), ("ck", 0, 16), P15, Op.not_equal, -1.0, Op.mult)
         ts(("qbi", 0, 16), ("qsc", 0, 16), -1281.0, Op.mult, -1.0, Op.add)
         ts(("wsc", 0, 16), ("qsc", 0, 16), 19200.0, Op.mult, 20480.0, Op.add)
         for k in range(16):
             o = ("dk", 128 * k, 128 * k + 128)
-            if k % 2:
+            if k < DKV:
                 ts(o, ("idn", 0, 128), ("wsc", k, k + 1), Op.mult)
             else:
                 act(o, ("idn", 0, 128), ("wsc", k, k + 1))
-        for n, c in (("idead", -20480.0), ("imx", -4096.0), ("ipen", -32.0)):
-            act((n, 0, 128), ("idn", 0, 128), c)
+        for n, c in (("idead", -20480.0), ("imx", -4096.0), ("ipen", -32.0), ("half", HALF / 255)):
+            select((n, 0, 128), ("zero", 0, 128), [[-1, 128]], Op.not_equal, 0, 1, c)
         act(("bd8", 0, 128), ("bd", 0, 128), -4096.0 * 8192)
         act(("neg", 0, 128), ("idn", 0, 128), -1.0)
-        fill(("seg", 0, 1024), 1.0)
-        fill(("seg", 0, 1024, 16), 0.0)
+        for lo in range(0, 1024, 256):
+            select(("seg", lo, lo + 256), ("zero", 0, 256), [[0, 16], [1, 16]], Op.is_equal, 0, 0, 1.0)
         count_up("kb", 0, 512, 0, 512)
-        fill(("kb", 0, 512, 16), -6.0e7)
-        count_up("c1", 0, 768, 0, 1)
-        iota(("sm", 0, 96), [[0, 96]], 0)
-        fill(("sm", 0, 96, 4), 4096.0)
+        for lo in (0, 256):
+            select(("kb", lo, lo + 256), ("kb", lo, lo + 256), [[0, 16], [1, 16]], Op.is_gt, 0, 0, -6.0e7)
+        select(("sm", 0, 96), ("zero", 0, 96), [[0, 24], [1, 4]], Op.is_gt, 0, 0, 4096.0)
         iota(("revf", 0, 48), [[0, 24], [-16, 2]], 31)
         ts(("rev", 0, 48), ("revf", 0, 48), P15, Op.subtract)
         iota(("repi", 0, 48), [[1, 24], [0, 2]], 0)
         tc(("rep", 0, 48), ("repi", 0, 48))
         iota(("jb0", 0, 8), [[16, 8]], 0)
-        ts(("jb", 0, 8), ("jb0", 0, 8), P15, Op.add)
+        ts(("ju", 16, 24), ("jb0", 0, 8), P15, Op.add)
+        act(("jb", 0, 8), ("jb0", 0, 8), 1.0, P15)
         for t in range(ROUNDS - 1):
-            tc(("ju%d" % t, 8 * t, 8 * t + 8), ("jb", 0, 8))
             act(("jf%d" % t, 8 * t, 8 * t + 8), ("jb", 0, 8), 1.0, float(VAL + START[t]))
 
     def lanes_of(st, *banks):
         n = width(message("r%d" % st, r, r)[0])
         for b in banks:
             for q in coming:
+                if st:
+                    next_of("hits")
                 mm((b, 0, n), to_one(r, q), message("r%d" % st, q, r)[1], q == r, q == coming[-1])
         qf = ("qf%d" % st, 0, L)
         later(act, qf, (banks[0], 0, L))
         if st:
-            later(act, ("limf", 0, 1), (banks[0], L, L + 1), 1.0, 2048.0)
+            later(act, ("limf", 0, 1), (banks[0], L, L + 1), 1.0, 2048.0 + HALF)
         else:
             act(("dead0", 0, L), (banks[0], L, 2 * L))
         tc(("qu%d" % st, 0, L), (banks[1], 0, L) if st else qf)
         for k in range(16):
             o = ("qr%d" % st, k, 16 * (L - 1) + k + 1, 16)
-            if k < 9 * st:
-                ts(o, (banks[1], 0, L), ("qsc", k, k + 1), Op.mult, ("qbi", k, k + 1), Op.add)
+            if k < SHARE[st]:
+                ts(o, (banks[1], 0, L) if st else qf, ("qsc", k, k + 1), Op.mult, ("qbi", k, k + 1), Op.add)
             else:
                 act(o, (banks[0], 0, L) if st else qf, ("qsc", k, k + 1), ("qbi", k, k + 1))
         later(act, ("of%d" % st, 0, L), qf, -1.0, float(V))
 
     def sums(lo, hi, stop):
         for k in range(16):
-            mm(("d0", lo, hi), ("idn", 0, 128), ("xv", 16 * lo + k, 16 * (hi - 1) + k + 1, 16), k == 0, stop and k == 15)
+            mm(("d0", lo, hi), ("idn", 0, 128), ("xv", 16 * lo + k, 16 * (hi - 1) + k + 1, 16), stop and k == 0, stop and k == 15)
 
     def hits(t):
         st, n = t % 2, lx(t)
         ts(("ok", 0, L), ("d0", 0, L), ("lima" if t else "lims", 0, 1), Op.is_le)
-        ts(("deg", 0, L), ("d0", 0, L), 255.0 / 512, Op.add)
         if t >= 2:
             mm(("bhit", 0, L), ("ipen", 0, 128), ("dead%d" % st, 0, L), True, False)
-        mm(("bhit", 0, L), ("bd", 0, 128), ("ok", 0, L), t < 2, True)
+        for lo, at, k in [(0, 0, L)] if t else [(0, 0, 40), (40, 80, 40), (80, 40, 40), (120, 120, 40)]:
+            next_of("hits")
+            mm(("bhit", lo, lo + k), ("bd", 0, 128), ("ok", at, at + k), t < 2, True)
+            act(("deg", lo, lo + k), ("d0", at, at + k), 1.0, ROUND)
         ts(("hit", 0, L), ("bhit", 0, L), 9.0, Op.is_ge)
         scan(("cum", 0, n), ("hit", 0, n), ("c255", 0, n), Op.add, Op.min)
         for c in range(2):
@@ -520,11 +540,18 @@ def rank_program(g, core, T, topo):
 
     def variables(t):
         n = lx(t)
-        ts(("vy", 0, 2), ("sn", n - 1, 2 * n, n), float(H), Op.is_ge, 1.0 - V, Op.mult)
-        ts(("vx", 0, 2), ("sn", n - 1, 2 * n, n), 16.0, Op.mult, ("cv", t % 2, t % 2 + 1) if t else 2.0 * r - 1024, Op.add)
-        ts(slot(t, r, 0, 32), pick(("deg", 0, LX), PLW), -1.0, Op.mult, -255.0, Op.max)
-        tt(slot(t, r, VARS, 2), ("vx", 0, 2), ("vy", 0, 2), Op.add)
-        ts(slot(t, r, COUNT, 2), ("cum", L - 2, L), float(CAP), Op.min)
+        lanes = ("sn", n - 1, 2 * n, n)
+        if t:
+            act(("vx", 0, 2), lanes, 16.0, ("cv", t % 2, t % 2 + 1))
+            act(("vy", 2, 4), lanes, 1.0, 0.5 - H, Fn.Sign)
+            act(("vy", 0, 2), ("vy", 2, 4), (1.0 - V) / 2, (1.0 - V) / 2)
+        else:
+            ts(("vy", 0, 2), lanes, float(H), Op.is_ge, 1.0 - V, Op.mult)
+            ts(("vx", 0, 2), lanes, 16.0, Op.mult, 2.0 * r - 1024, Op.add)
+        ts(slot(t, r, 0, 32), pick(("deg", 0, LX), PLW), -ROUND, Op.add, 255.0, Op.min)
+        (later if t else call)(tt, slot(t, r, VARS, 2), ("vx", 0, 2), ("vy", 0, 2), Op.add)
+        if t < ROUNDS - 1:
+            ts(slot(t, r, COUNT, 2), ("cum", L - 2, L), float(CAP), Op.min)
 
     def limits(t):
         for d in coming:
@@ -550,8 +577,8 @@ def rank_program(g, core, T, topo):
     def put(table, lists, lo, hi, src):
         tc(pick((table, 0, VT), (lists, lo // 16, hi // 16)), src)
 
-    def own(table, t):
-        put(table, "evo", 128 * t, 128 * t + 128, ("nt" if table == "nm" else "xt", 128 * t, 128 * t + 128))
+    def own(table, lo, hi):
+        put(table, "evo", lo, hi, ("nt" if table == "nm" else "xt", lo, hi))
 
     def main(t):
         st = t % 2
@@ -587,47 +614,53 @@ def rank_program(g, core, T, topo):
             scan(("msc", 16 * lo, 16 * hi), ("seg", 0, 16 * (hi - lo)), ("xv", 16 * lo, 16 * hi), Op.mult, Op.min)
             next_of("sums")
             sums(lo, hi, False)
-            mm(("d0", lo, hi), ("imx", 0, 128), ("msc", 16 * lo + 15, 16 * hi, 16), False, True)
 
         cover(0)
         for c in range(len(CH)):
             if c + 1 < len(CH):
                 cover(c + 1)
             else:
-                tt(pick(("rs", 0, VT), ("evu", 0, 8 * t)), ("idr", 0, 128 * t), ("bk", 0, 128 * t), Op.add)
+                for a, z in KEYS[t]:
+                    (later if a else call)(tt, pick(("rs", 0, VT), ("evu", a // 16, z // 16)), ("idr", a, z), ("bk", a, z), Op.add)
             uncovered(c)
+        mm(("d0", 0, L), ("half", 0, 128), ("c255", 0, L), True, False)
         for c in range(len(CH)):
             degrees(c)
+        mm(("d0", 0, L), ("imx", 0, 128), ("msc", 15, 16 * L, 16), False, True)
 
     def pivots(t):
         st, n = t % 2, 256 * t
         nl = ("nl%d" % st, 0, LX)
         tc(("qp", 0, 32), pick(("qf%d" % st, 0, LX), PLW))
-        act(("key", 0, 512), pick(("rs", 0, G0), ("qp", 0, 32)))
-        act(("xn", 0, 512), pick(("en", 0, G0), ("qp", 0, 32)))
+        for f, a, z in ((act, 0, KEYV[t]), (tc, KEYV[t], 32)):
+            if a < z:
+                f(("key", 16 * a, 16 * z), pick(("rs", 0, G0), ("qp", a, z)))
         act(("zp", 0, 32), pick(("z", 0, LX), PLW), -1.0)
-        tc(("vh", 0, 32), pick(nl, PLW))
+        buf, v0, v1 = slot(t, r, FREE, 32) if t == ROUNDS - 1 else ("vh", 0, 32)
+        tc((buf, v0, v1), pick(nl, PLW))
         tt(("xn", 512, 544), pick(("of%d" % st, 0, LX), PLW), ("zp", 0, 32), Op.add)
-        mm(("b1", 0, 512), ("idn", 0, 128), ("zero", 0, 512), True, False)
-        for k in range(16):
-            mm(("b1", k, 512, 16), ("idn", 0, 128), ("vh", 0, 32), False, False)
-        mm(("b1", 512, 544), ("idn", 0, 128), ("vh", 0, 32), True, False)
-        mm(("b1", 512, 544), ("neg", 0, 128), ("xn", 512, 544), False, True, 4 * PE)
-        mm(("b1", 0, 512), ("neg", 0, 128), ("xn", 0, 512), False, True, 4 * PE)
-        act(("b0", 0, 544), ("b1", 0, 544), 2048.0, 0.0, Fn.Abs)
-        if t == ROUNDS - 1:
-            ts(slot(t, r, FREE, 32), ("vh", 0, 32), -1.0, Op.mult, float(V), Op.add)
+        for bank, a in (("b1", 0), ("b2", 16)):
+            act(("xn", 16 * a, 16 * a + 256), pick(("en", 0, G0), ("qp", a, a + 16)))
+            mm((bank, 0, 288), ("idn", 0, 128), ("zero", 0, 288), True, False)
+            for k in range(16):
+                mm((bank, k, 256, 16), ("idn", 0, 128), (buf, v0 + a, v0 + a + 16), False, False)
+            if a:
+                mm((bank, 256, 288), ("idn", 0, 128), (buf, v0, v1), False, False)
+            mm((bank, 0, 256 + 2 * a), ("neg", 0, 128), ("xn", 16 * a, 18 * a + 256), False, True, 4 * PE)
+            act(("b0", 16 * a, 18 * a + 256), (bank, 0, 256 + 2 * a), 2048.0, 0.0, Fn.Abs)
         variables(t)
         scan(("ksc", 0, 512), ("kb", 0, 512), ("key", 0, 512), Op.add, Op.max)
         tc(("mi", 0, 32), ("ksc", 15, 512, 16))
+        if t == ROUNDS - 1:
+            send("s3")
         ts(("mj", 0, 32), ("mi", 0, 32), 511, Op.bitwise_and)
         later(act, ("rho", 0, n), pick(("jf%d" % (t - 1), 0, 8 * t), ("rep", 0, 16 * t)), 1.0, float(-VAL - ID0))
         later(act, ("c1", 31, n, 32), ("c1", 0, 8 * t), ("cb", t, t + 1))
         tt(("ne", 0, n), pick(("mj", 0, 32), ("rev", 0, 16 * t)), ("rho", 0, n), Op.not_equal)
         scan(("fc", 0, n), ("ne", 0, n), ("c1", 0, n), Op.mult, Op.add, float(VAL))
-        tt(slot(t, r, CLAIMS, 8 * t), ("fc", 31, n, 32), ("jf%d" % (t - 1), 0, 8 * t), Op.min)
+        tt(slot(t, r, CLAIMS[t], 8 * t), ("fc", 31, n, 32), ("jf%d" % (t - 1), 0, 8 * t), Op.min)
         if t == ROUNDS - 1:
-            send("a3")
+            send("c3")
         tt(("cc", 0, 544), ("xn", 0, 544), ("b0", 0, 544), Op.min)
         if t < ROUNDS - 1:
             roots(t)
@@ -636,7 +669,7 @@ def rank_program(g, core, T, topo):
 
     def least(t, bank):
         scan(("jm", 0, 32 * t), ("sm", 0, 32 * t), (bank, 16, 16 + 32 * t), Op.add, Op.min)
-        ts(("ju%d" % t, 0, 8 * t), ("jm", 3, 32 * t, 4), float(-VAL - START[t]), Op.add)
+        ts(("ju", 16 - 8 * t, 16) if t < 3 else ("ju3", 0, 24), ("jm", 3, 32 * t, 4), float(-VAL - START[t]), Op.add)
 
     def spread(t, part, k, out):
         for q in coming if t == 0 else range(N):
@@ -645,40 +678,40 @@ def rank_program(g, core, T, topo):
     def roots(t):
         n, new = 128 * (t + 1), ("la", START[t], START[t] + 128)
         spread(t, 0, 32, lambda q: ("d0", 32 * q, 32 * q + 32))
-        spread(t, VARS, 2, lambda q: ("bhit", 2 * q, 2 * q + 2))
+        bank = "bkey" if t else "bhit"
+        later(spread, t, VARS, 2, lambda q: (bank, 2 * q, 2 * q + 2))
+        later(ts, ("evu", 8 * t, 8 * t + 8), (bank, 0, 8), 1024.0, Op.add)
+        later(act, ("xr", n - 128, n), ("d0", 0, 128), -1.0 / 4096)
+        later(act, new, ("d0", 0, 128))
+        for lo in (n - 128, n - 64):
+            later(put, "xm", "evu", lo, lo + 64, ("xr", lo, lo + 64))
         if t:
-            spread(t, CLAIMS, 8 * t, lambda q: ("bhit", 16 + q, 16 + 32 * t, 4))
-            act(new, ("d0", 0, 128))
+            spread(t, CLAIMS[t], 8 * t, lambda q: ("bhit", 16 + q, 16 + 32 * t, 4))
             least(t, "bhit")
-            act(("xr", 0, n), pick(("la", START[t], 512), ("ju%d" % t, 0, n // 16)), 1.0 / 4096)
+            act(("xr", 0, n - 128), pick(("la", START[t], 512), ("ju", 16 - 8 * t, 16)), -1.0 / 4096)
             later(act, ("jf%d" % t, 0, 8 * t), ("jm", 3, 32 * t, 4))
-        else:
-            act(("xr", 0, n), ("d0", 0, 128), 1.0 / 4096)
-            later(act, new, ("xr", 0, n), 4096.0)
-        ts(("evu", 8 * t, 8 * t + 8), ("bhit", 0, 8), 1024.0, Op.add)
 
     def update(t):
         n, new = 128 * (t + 1), ("ln", START[t], START[t] + 128)
-        ju = ("ju%d" % t, 0, n // 16)
-        xr, er = ("xr", 0, n), ("er", 0, n)
+        ju = ("ju", 16 - 8 * t, 24)
+        xr = ("xr", 0, n)
         spread(t, NAMES[t], 32, lambda q: ("b2", 32 * q, 32 * q + 32))
         if t:
             act(new, ("b2", 0, 128))
             next_of("roots")
-            act(er, pick(("ln", START[t], 512), ju))
-            put("xm", "evu", 0, n, xr)
-            put("en", "evu", 0, n, er)
+            act(("er", 0, n - 128), pick(("ln", START[t], 512), ("ju", 16 - 8 * t, 16)))
+            put("xm", "evu", 0, n - 128, ("xr", 0, n - 128))
+            put("en", "evu", n - 128, n, new)
+            put("en", "evu", 0, n - 128, ("er", 0, n - 128))
         else:
-            act(er, ("b2", 0, 128))
+            act(new, ("b2", 0, 128))
             roots(0)
-            put("en", "evu", 0, n, er)
-            put("xm", "evu", 0, n, xr)
-            later(act, new, er)
+            put("en", "evu", 0, n, new)
         mm(("bkey", 0, n), ("bd8", 0, 128), xr)
         next_of("roots")
         act(("bk", 0, n), ("bkey", 0, n))
         next_of("roots")
-        act(("idr", 0, n), pick(("idt", START[t], 512), ju))
+        act(("idr", 0, n), pick(("jt", START[t], 512), ju), 1.0, float(-ID0 - SHIFT))
 
     def collect(t, bank, n, pieces):
         if t == ROUNDS - 1:
@@ -692,6 +725,8 @@ def rank_program(g, core, T, topo):
                         for e in range(N):
                             mm((bank,) + out(q), to_one(q, e), slot(t, e, part, k), e == 0, e == N - 1)
                     else:
+                        if (d, q) == ((r, 0) if part == NAMES[t] else (coming[-1], N - 1)):
+                            next_of("last")
                         mm((bank,) + out(q), to_one(q, d), slot(t, d, part, k), False, (d, part, q) == (coming[-1], pieces[-1][0], N - 1))
 
     def by32(q):
@@ -701,7 +736,7 @@ def rank_program(g, core, T, topo):
         collect(t, "bhit", 8, [(VARS, 2, lambda q: (2 * q, 2 * q + 2))])
         ts(("evo", 8 * t, 8 * t + 8), ("bhit", 0, 8), 1024.0, Op.add)
         collect(t, "d0", 128, [(0, 32, by32)])
-        act(("xt", 128 * t, 128 * t + 128), ("d0", 0, 128), -1.0)
+        act(("xt", 128 * t, 128 * t + 128), ("d0", 0, 128))
         collect(t, "b2", 128, [(NAMES[t], 32, by32)])
         act(("nt", 128 * t, 128 * t + 128), ("b2", 0, 128), -1.0, float(V))
         act(("vid", START[t], START[t] + 128), pick(("jt", 0, VT), ("evo", 8 * t, 8 * t + 8)))
@@ -712,23 +747,24 @@ def rank_program(g, core, T, topo):
         for (lo, hi), x in classes(t % 2):
             act(x, ("bkey", lo, hi))
 
-    for d in far + near:
-        dma("y", T["sx"][:, 320 * d:320 * d + 320], T.xs[32 * d:32 * d + 32, :], "ds_%d" % d, [], [message("x", r, d)[0]], 2.5)
-    dma("y", T["nm"][:, 0:V], T.nb[:, :], "dn", [], [("nm", 0, V)], 4.2)
-    dma("s", T["xo"][:, 0:V], T.xs[:, :], "do", [], [("xo", 0, V)], 4.2)
-    dma("s", T["limi"][:, 0:1], T.lim[:, 0:1], "dl", [], [("limi", 0, 1)], 4.2)
+    for q, d in zip("yss", far + near):
+        dma(q, T["sx"][:, 320 * d:320 * d + 320], T.xs[32 * d:32 * d + 32, :], "ds_%d" % d, [], [message("x", r, d)[0]], 1.8)
+    dma("y", T["limi"][:, 0:1], T.lim[:, 0:1], "dl", [], [("limi", 0, 1)], 2.0)
+    dma("y", T["nm"][:, 0:V // 2], T.nb[:, 0:V // 2], "dn", [], [("nm", 0, V // 2)], 2.7)
+    dma("y", T["xo"][:, 0:V], T.xs[:, :], "do", [], [("xo", 0, V)], 3.5)
+    dma("y", T["nm"][:, V // 2:V], T.nb[:, V // 2:V], "dm", [], [("nm", V // 2, V)], 4.3)
     dma("y", T["xm"][32 * r:32 * r + 32, 0:V], T.xs[32 * r:32 * r + 32, :], "dx_%d" % r, [("nm", 0, V)], [("xm", r, V, N)], 6.0)
-    send("x", 2.6)
+    send("x")
+    later(constants)
     for q in near + far:
         dma("y", T["xm"][32 * q:32 * q + 32, 0:V], T["lx"][:, 320 * q:320 * q + 320], "dx_%d" % q, [message("x", q, r)[1]], [("xm", q, V, N)], 1.5)
-    later(constants)
 
-    for (lo, hi), x in classes(0):
-        tc(("qs", lo, hi), x)
-    for lo, mid, hi in CH0:
-        for f, a, z in ((act, lo, mid), (tc, mid, hi)):
-            f(("xv", 16 * a, 16 * z), pick(("xo", 0, G0), ("qs", a, z)))
-        sums(lo, hi, True)
+    for half in range(2):
+        for m, f in enumerate((act, tc)):
+            at, c = H * half + H // 2 * m, V // 2 * half + 2 * r + m
+            tc(("qs", at, at + H // 2), ("nm", c, c + V // 2 - 15, 16))
+            f(("xv", 16 * at, 16 * at + V // 2), pick(("xo", 0, G0), ("qs", at, at + H // 2)))
+        sums(H * half, H * half + H, True)
     for (lo, hi), x in classes(1):
         tc(("r1", 168 * r + lo, 168 * r + hi), x)
     ts(("r1", 168 * r + L, 168 * r + L + 1), ("limi", 0, 1), -2048.0, Op.add)
@@ -757,7 +793,6 @@ def rank_program(g, core, T, topo):
         if t >= 2:
             ts(message("k%d" % t, r, r)[0], ("q2", 0, L), float(V), Op.min)
             send("k%d" % t)
-            later(own, "xo", t - 2)
         hits(t)
         later(outputs, t - 1)
         if t == 3:
@@ -775,23 +810,26 @@ def rank_program(g, core, T, topo):
             later(limits, t)
 
     send("n3")
-    put("nm", "evo", 0, 384, ("nt", 0, 384))
-    own("xo", 2)
-    collect(3, "bhit", 112, [(CLAIMS, 24, lambda q: (16 + q, 112, 4)), (VARS, 2, lambda q: (2 * q, 2 * q + 2))])
-    collect(3, "d0", 128, [(FREE, 32, by32)])
-    collect(3, "bkey", 128, [(0, 32, by32)])
+    collect(3, "d0", 128, [(0, 32, by32)])
+    collect(3, "bkey", 8, [(VARS, 2, lambda q: (2 * q, 2 * q + 2))])
+    collect(3, "b1", 128, [(FREE, 32, by32)])
+    act(("xt", 384, 512), ("d0", 0, 128))
+    act(("vid", 0, 128), ("b1", 0, 128), -1.0, float(V))
+    ts(("evo", 24, 32), ("bkey", 0, 8), 1024.0, Op.add)
+    own("nm", 0, 384)
+    own("xo", 0, 256)
+    collect(3, "bhit", 112, [(CLAIMS[3], 24, lambda q: (16 + q, 112, 4))])
     collect(3, "b2", 128, [(NAMES[3], 32, by32)])
     least(3, "bhit")
-    ts(("evo", 24, 32), ("bhit", 0, 8), 1024.0, Op.add)
-    act(("vid", 0, 128), ("d0", 0, 128))
-    act(("xt", 384, 512), ("bkey", 0, 128), -1.0)
-    act(("jv", 0, 384), pick(("vid", 0, 512), ("ju3", 0, 24)))
+    own("xo", 256, 512)
+    dma("y", T.yx[:, :], T["xo"][:, 0:V], "ox", [("xo", 0, V)], [], 2.2)
+    act(("jv", 0, 256), pick(("vid", 0, 512), ("ju3", 0, 16)))
     act(("nt", 384, 512), ("b2", 0, 128), -1.0, float(V))
-    own("xo", 3)
-    dma("y", T.yx[:, :], T["xo"][:, 0:V], "ox", [("xo", 0, V)], [], 2.5)
-    put("jt", "evo", 0, 384, ("jv", 0, 384))
-    own("nm", 3)
-    dma("y", T.yn[:, :], T["nm"][:, 0:V], "on", [("nm", 0, V)], [], 3.2)
+    act(("jv", 256, 384), pick(("vid", 0, 512), ("ju3", 16, 24)))
+    put("jt", "evo", 0, 256, ("jv", 0, 256))
+    own("nm", 384, 512)
+    dma("y", T.yn[:, :], T["nm"][:, 0:V], "on", [("nm", 0, V)], [], 2.8)
+    put("jt", "evo", 256, 384, ("jv", 256, 384))
     dma("s", T.yj[:, :], T["jt"][0:128:16, 0:V], "oj", [("jt", 0, V)], [], 2.0)
     in_order()
     for s, v in totals.items():

from concourse.bass import DstId, RemoteDMATransfer
from concourse.mybir import AluOpType as Op, ActivationFunctionType as Fn

V, H, CAP, ROUNDS = 1280, 80, 32, 4
N = 4
L = 2 * H
LX = L + 2 * CAP
VT = 2304
G0 = 1288
START = [384, 256, 128, 0]
ID0, VAL = 124, 1024
SHIFT = 512 * 32618
ROUND, HALF = 1.5 * 2 ** 23, 255.0 / 512
WIDE, SLOTS = [72, 80, 88, 128], [0, 288, 608, 960]
VARS, COUNT, FREE, CLAIMS, NAMES = 32, 34, 34, [None, 36, 36, 72], [36, 44, 52, 96]
FP, BF, F16, I32, U16 = "float32", "bfloat16", "float16", "int32", "uint16"
CH = [(0, 52), (52, 116), (116, 160)]
PART = [0, 0, 20]
LISTS = {1: ("qu1", "qn"), 2: ("qu0", "qm"), 3: ("qn", "qu1")}
CYCLE, GATHER, SCATTER, PE, WAKE, ACROSS, HOP = 0.001, 1.36, 3.0, 0.6, 0.06, 0.19, 1.5
FIXED = {"v": 0.06, "s": 0.13, "t": 0.0, "g": 0.13}
SENDS = ["x", "r1", "a0", "r0", "a1", "k2", "a2", "k3", "s3", "c3", "n3"]
SLOW, BACK = {"x": 2.5, "r1": 1.0, "a0": 1.0, "s3": 1.0, "c3": 1.0, "n3": 1.0}, 1.4
RS, DKV = "g", 8
ROOM, SEND = 1.0, 0.7
KEYS = {1: [(0, 128)], 2: [(0, 128), (128, 192), (192, 256)], 3: [(0, 192), (192, 256), (256, 320), (320, 384)]}
KEYV = [0, 16, 20, 24]
EVEN = 0.01
PASSES = 200
SHARE = [8, 9]
DBG = []

_S = {
    "nm": (VT, FP), "en": (VT, FP), "rs": (VT, FP), "jt": (VT, FP), "xm": (VT, BF), "xo": (VT, BF),
    "sx": (V, BF), "lx": (V, BF), "r1": (4 * 168, F16), "r0": (4 * 2 * L, F16), "ra": (1472, F16), "rk": (8 * L, F16),
    "la": (512, FP), "ln": (512, FP), "vid": (512, FP),
    "jf0": (8, FP), "jf1": (16, FP), "jf2": (24, FP), "ju": (24, U16), "ju3": (24, U16),
    "jb": (8, FP), "jb0": (8, FP), "jm": (96, FP), "sm": (96, BF), "evu": (24, U16), "evo": (32, U16),
    "er": (384, FP), "xr": (384, BF), "idr": (384, FP), "bk": (384, FP), "jv": (384, FP), "xt": (512, BF), "nt": (512, FP),
    "qs": (L, U16), "os": (LX, FP), "ns": (LX, FP), "nlb": (L, FP),
    "qf0": (LX, FP), "qf1": (LX, FP), "of0": (LX, FP), "of1": (LX, FP), "nl0": (LX, FP), "nl1": (LX, FP),
    "qu0": (L, U16), "qu1": (L, U16), "qn": (L, U16), "qm": (L, U16), "qr0": (16 * L, FP), "qr1": (16 * L, FP),
    "dead0": (L, BF), "dead1": (L, BF), "piv": (L, BF), "neg": (128, FP),
    "eq": (16 * L, BF), "xv": (16 * L, BF), "msc": (16 * L, BF), "deg": (LX, FP), "half": (128, BF),
    "z": (LX, FP), "q2": (L, FP), "ok": (L, BF), "hit": (LX, BF), "cum": (LX, BF), "c255": (LX, BF),
    "sg": (2 * LX, BF), "sn": (2 * LX, BF), "sgl": (2 * LX, BF), "plw": (2, U16), "vx": (2, FP), "vy": (4, FP),
    "qp": (32, U16), "vh": (32, F16), "zp": (32, FP), "xn": (544, FP), "vr": (32, FP), "cc": (544, F16), "nsc": (512, F16),
    "key": (512, FP), "ksc": (512, FP), "mi": (32, I32), "mj": (32, I32), "rho": (768, FP), "ne": (768, BF), "fc": (768, F16),
    "c1": (768, BF), "rev": (48, U16), "rep": (48, U16), "revf": (48, FP), "repi": (48, I32),
    "am": (5, FP), "limi": (1, I32), "lims": (1, FP), "limf": (1, FP), "lima": (1, FP),
    "one": (128, BF), "zero": (512, BF), "idn": (128, BF), "idead": (128, BF), "ipen": (128, BF), "imx": (128, BF), "bdh": (128, BF),
    "bd": (128, BF), "bd8": (128, BF), "dk": (2048, BF), "wide": (512, BF), "to": (4 * 224, BF), "o16": (224, BF), "cq": (128, BF),
    "cqh": (128, BF), "c16th": (128, BF),
    "pii": (2, I32), "pij": (2, I32), "pq": (3, FP), "c16": (2, I32), "sc": (2, FP), "kq": (2, FP), "cv0": (2, FP),
    "cv": (2, FP), "ncv": (2, FP), "cb0": (4, FP), "cb": (4, FP),
    "ck": (16, FP), "qsc": (16, FP), "qbi": (16, FP), "wsc": (16, FP), "seg": (1024, BF), "kb": (512, FP),
}
PSUM = {"b0": 1024, "b1": 1024, "b2": 512, "d0": 512, "bhit": 512, "bkey": 512}
SMALL = [n for n, (c, d) in _S.items() if c <= 16 and n != "limi"]
SCRATCH = {n: ("sbuf", [128, c], d) for n, (c, d) in _S.items() if n not in SMALL}
SCRATCH.update({"small_" + d: ("sbuf", [128, 16 * len(SMALL)], d) for d in (FP, I32, U16)})
SCRATCH.update({n: ("psum", [128, c], FP) for n, c in PSUM.items()})
SEMAPHORES = (["qv", "qs", "qt", "qg", "dn", "dm", "do", "dl", "on", "ox", "oj", "loc"]
              + [x + "_" + str(q) for x in SENDS + ["ds", "dx"] for q in range(N)])


def slot(t, q, part, n):
    lo = SLOTS[t] + WIDE[t] * q + part
    return ("ra", lo, lo + n)


def message(name, q, d):
    if name == "x":
        return ("sx", 320 * d, 320 * d + 320), ("lx", 320 * q, 320 * q + 320)
    t = int(name[1])
    cols = {"r": ("r1", 168 * q, 168 * q + L + 1) if t else ("r0", 2 * L * q, 2 * L * (q + 1)),
            "k": ("rk", L * (4 * (t % 2) + q), L * (4 * (t % 2) + q + 1)),
            "a": slot(t, q, 0, NAMES[t] + 32), "s": slot(t, q, 0, FREE + 32), "c": slot(t, q, CLAIMS[3], 24),
            "n": slot(t, q, NAMES[t], 32)}[name[0]]
    return cols, cols


def plan(core, T, topo):
    direct = [d for d in T.cores if d != core and topo.may_write(core, d)]
    rest = [d for d in T.cores if d != core and not topo.may_write(core, d)]
    relays = []
    for d in rest:
        ok = [x for x in topo.cores_of(core) if x not in T.cores and x not in relays and topo.may_write(x, d)]
        ok.sort(key=lambda x: (topo.die(x) != topo.die(core), x))
        relays.append(ok[0])
    return direct, list(zip(relays, rest))


def legs(core, T, topo):
    direct, via = plan(core, T, topo)
    out = []
    for ds in (via, [(d, d) for d in direct]):
        k = [len(topo.engines(core, x)) // len(ds) for x, d in ds]
        out.append([(x, d, topo.engines(core, x)[i * k[i]:(i + 1) * k[i]]) for i, (x, d) in enumerate(ds)])
    return out


def transfer(T, topo, src, dst, engines, a, b, sem):
    rid, pid = topo.addr(dst, src)
    return RemoteDMATransfer(dst_ids=[DstId(rid=rid, pnc=pid)], dma_engine_mask=sum(1 << e for e in engines), remote_sem=T.sem[sem],
                             srcs=[T[a[0]][:, a[1]:a[2]]], dsts=[T[b[0]][:, b[1]:b[2]]])


def relay_program(g, core, T, topo):
    for r, src in enumerate(T.cores):
        for x, dst, into in legs(src, T, topo)[0]:
            if x != core:
                continue
            out = topo.engines(core, dst)
            for name in SENDS:
                cols, sem = message(name, r, T.rank_of(dst))[1], "%s_%d" % (name, r)
                g.wait_ge(T.sem[sem], len(into))
                g.remote_dma_fused([transfer(T, topo, core, dst, out, cols, cols, sem)], local_sem=T.sem.loc)
            g.wait_ge(T.sem.loc, len(SENDS) * len(out))


def rank_program(g, core, T, topo):
    rank = T.rank_of(core)
    if rank is None:
        relay_program(g, core, T, topo)
        return
    r = rank
    Q = {"v": g.vector, "s": g.scalar, "t": g.tensor, "g": g, "y": g.sync}
    cnt = {q: 0 for q in "vstg"}
    known = {q: {} for q in "vstgy"}
    hist = {}
    totals = {}
    row, aside = [], set()
    calls = []

    def meet(a, b):
        return a[0] < b[1] and b[0] < a[1] and (a[2] != b[2] or (a[0] - b[0]) % a[2] == 0)

    def holds(a, b):
        return a[0] <= b[0] and b[1] <= a[1] and (a[2] == 1 or a[2] == b[2] and (a[0] - b[0]) % a[2] == 0)

    def parts(regs):
        return [(x[0], (x[1:] + (1,))[:3]) for x in regs]

    def deps(q, reads, writes):
        toks = []
        for kind, regs in (("r", reads), ("w", writes)):
            for n, c in parts(regs):
                for e in hist.get(n, ()):
                    if n not in PSUM and not meet(c, e[0]):
                        continue
                    if kind == "r" and e[2] == "r" and n not in PSUM:
                        continue
                    if n in PSUM and e[3] == q and (q == "t" or kind == "r" and e[2] == "r"):
                        continue
                    toks.append((e[4], e[5], e[6]))
        return toks

    def wait_for(q, toks):
        need = {}
        k = known[q]
        for s, v, snap in toks:
            if need.get(s, (0, None))[0] < v:
                need[s] = (v, snap)
        for s in list(need):
            v = need[s][0]
            if k.get(s, 0) >= v or any(o != s and sn.get(s, 0) >= v and k.get(o, 0) < ov for o, (ov, sn) in need.items()):
                continue
            Q[q].wait_ge(T.sem[s], v)
        for s, (v, snap) in need.items():
            k[s] = max(k.get(s, 0), v)
            for o, ov in snap.items():
                k[o] = max(k.get(o, 0), ov)

    def note(q, reads, writes, sem, val, snap):
        for n, c in parts(writes):
            h = hist.setdefault(n, [])
            h[:] = [e for e in h if not holds(c, e[0])]
            h.append((c, n, "w", q, sem, val, snap))
        for n, c in parts(reads):
            h = hist.setdefault(n, [])
            h[:] = [e for e in h if not (e[2] == "r" and e[3] == q and q in cnt and holds(c, e[0]))]
            h.append((c, n, "r", q, sem, val, snap))

    def flat(x):
        if not isinstance(x, tuple):
            return []
        return [x[1], x[2]] if x[0] == "I" else [x]

    def ap(x):
        if not isinstance(x, tuple):
            return x
        if x[0] == "I":
            return ap(x[1]).indirect(ap(x[2]))
        if x[0] in SMALL:
            at = 16 * SMALL.index(x[0])
            x = ("small_" + _S[x[0]][1], at + x[1], at + x[2]) + x[3:]
        if len(x) > 3:
            return T[x[0]][:, x[1]:x[2]:x[3]]
        return T[x[0]][:, x[1]:x[2]]

    def width(x):
        return 16 * width(x[2]) if x[0] == "I" else len(range(*x[1:]))

    def cost(q, outs, ins, pace):
        full = [x for x in ins + outs if isinstance(x, tuple)]
        n = max(width(x) for x in full) if q != "t" else width(outs[0])
        if any(x[0] == "I" for x in full):
            return 0.06 + CYCLE * n * (SCATTER if outs[0][0] == "I" else GATHER)
        if pace is None:
            narrow = all(x[0] not in PSUM and _S[x[0]][1] in (BF, F16, U16) for x in full if width(x) == n)
            pace = {"v": 0.5 if narrow else 1, "s": 1, "g": 2, "t": PE}[q]
        return FIXED[q] + CYCLE * (max(64, n * pace) if q == "v" else max(64, n) * pace if q == "t" else n * pace)

    def emit(q, fn, outs, ins, pace=None):
        reads, writes = [], []
        for x in ins:
            reads += flat(x)
        for x in outs:
            writes += flat(x)[:1]
            reads += flat(x)[1:]

        def issue():
            wait_for(q, deps(q, reads, writes))
            inst = fn()
            sem = "q" + q
            cnt[q] += 1
            inst.then_inc(T.sem[sem], 1)
            totals[sem] = cnt[q]
            snap = dict(known[q])
            snap[sem] = cnt[q]
            note(q, reads, writes, sem, cnt[q], snap)
        c = cost(q, outs, ins, pace)
        calls.append((q, issue, reads, writes + row, c, c))
        del row[:]

    def next_of(name):
        row.append((name, 0, 1))

    def later(f, *args):
        n = len(calls)
        f(*args)
        aside.update(range(n, len(calls)))

    def call(f, *args):
        f(*args)

    def in_order():
        seen, pre = {}, []
        for i, (q, issue, reads, writes, c, lat) in enumerate(calls):
            p = set()
            for kind, regs in (("r", reads), ("w", writes)):
                for n, c in parts(regs):
                    p.update(e[2] for e in seen.get(n, ()) if (n in PSUM or meet(c, e[0])) and
                             ("w" in (kind, e[1]) or n in PSUM and calls[e[2]][0] != q))
            for n, c in parts(writes):
                seen[n] = [e for e in seen.get(n, ()) if not holds(c, e[0])] + [(c, "w", i)]
            for n, c in parts(reads):
                seen.setdefault(n, []).append((c, "r", i))
            pre.append(p - {i})

        def gap(j, i):
            if calls[i][3][-1:] == calls[j][3][-1:] == [("dma", 0, 1)]:
                return calls[j][4]
            return calls[j][5] + (ACROSS if calls[j][0] != calls[i][0] else 0.0 if calls[j][0] == "t" else WAKE)
        needs = [[(j, gap(j, i)) for j in p] for i, p in enumerate(pre)]

        def lay(order):
            at, held, used = {}, {}, {}
            for i in order:
                d = calls[i][4] * (ROOM if i in aside else 1.0)
                t0, held[i] = max([(0.0, -1)] + [(at[j] + x, j) for j, x in needs[i]])
                u = used.setdefault(calls[i][0], [])
                n = len(u)
                while n and u[n - 1][1] > t0:
                    n -= 1
                while n < len(u) and u[n][0] < t0 + d:
                    t0, held[i] = u[n][1:]
                    n += 1
                u.insert(n, (t0, t0 + d, i))
                at[i] = t0
            last = max(at, key=lambda i: at[i] + calls[i][5])
            return at[last] + calls[last][5], at, held, last

        def first(order, i, j):
            n = order.index(j)
            late, need, stack = set(order[n:]), set(), [i]
            while stack:
                k = stack.pop()
                if k in late and k not in need:
                    need.add(k)
                    stack += pre[k]
            return order[:n] + [k for k in order[n:] if k in need] + [k for k in order[n:] if k not in need]
        order, done = [], set()
        for i in [i for i in range(len(calls)) if i not in aside] + sorted(aside):
            stack, need = [i], set()
            while stack:
                j = stack.pop()
                if j not in done and j not in need:
                    need.add(j)
                    stack += pre[j]
            order += sorted(need)
            done |= need
        best, tried, chain = lay(order), set(), [i for i in order if i not in aside]
        for _ in range(PASSES):
            i, swaps = best[3], []
            while best[2][i] >= 0:
                if best[2][i] not in pre[i] and (i, best[2][i]) not in tried:
                    swaps.append((i, best[2][i]))
                i = best[2][i]
            if not swaps:
                break
            tried.add(swaps[-1])
            other = first(order, *swaps[-1])
            new = lay(other)
            if new[0] < best[0] - 0.01 or new[0] < best[0] + EVEN and sum(new[1][k] - best[1][k] for k in chain) < -1.0:
                best, order = new, other
            DBG.append(best[0])
        DBG.append([(calls[i][0], best[1][i], calls[i][3]) for i in sorted(best[1], key=lambda i: (best[1][i], order.index(i)))])
        for i in sorted(best[1], key=lambda i: (best[1][i], order.index(i))):
            calls[i][1]()

    def tc(out, in_):
        emit("v", lambda: g.vector.tensor_copy(out=ap(out), in_=ap(in_)), [out], [in_])

    def tt(out, a, b, op):
        emit("v", lambda: g.vector.tensor_tensor(out=ap(out), in0=ap(a), in1=ap(b), op=op), [out], [a, b],
             1 if a[0] in PSUM or b[0] in PSUM else 2)

    def ts(out, a, s1, op0, s2=None, op1=None):
        if op1 is None:
            emit("v", lambda: g.vector.tensor_scalar(out=ap(out), in0=ap(a), scalar1=ap(s1), scalar2=None, op0=op0), [out], [a, s1])
        else:
            emit("v", lambda: g.vector.tensor_scalar(out=ap(out), in0=ap(a), scalar1=ap(s1), scalar2=ap(s2), op0=op0, op1=op1),
                 [out], [a, s1, s2])

    def scan(out, d0, d1, op0, op1, first=0.0):
        emit("v", lambda: g.vector.tensor_tensor_scan(out=ap(out), data0=ap(d0), data1=ap(d1), initial=first, op0=op0, op1=op1),
             [out], [d0, d1])

    def fill(out, c):
        emit("v", lambda: g.vector.memset(ap(out), c), [out], [])

    def act(out, in_, scale=1.0, bias=0.0, func=None):
        f = func or (Fn.Identity if isinstance(bias, tuple) else Fn.Copy)
        emit("s", lambda: g.scalar.activation(out=ap(out), in_=ap(in_), func=f, bias=ap(bias), scale=ap(scale)), [out], [in_, bias, scale])

    def mm(out, w, x, start=True, stop=True, pace=None):
        emit("t", lambda: g.tensor.matmul(out=ap(out), lhsT=ap(w), rhs=ap(x), start=start, stop=stop), [out], [w, x], pace)

    def iota(out, pattern, base, mul=0):
        if _S[out[0]][1] == I32:
            emit("g", lambda: g.iota(ap(out), pattern, base, mul), [out], [])
        else:
            emit("g", lambda: g.iota(ap(out), pattern, base, mul, allow_small_or_imprecise_dtypes=True), [out], [])

    def count_up(n, lo, hi, step, base):
        for a in range(lo, hi, 256):
            iota((n, a, min(a + 256, hi)), [[step, min(a + 256, hi) - a]], base + step * a)

    def select(out, in_, pattern, op, base, mul, other=0.0):
        emit("g", lambda: g.affine_select(ap(out), ap(in_), pattern, op, other, base, mul), [out], [in_])

    def dma(q, out, in_, sem, reads, writes, lat):
        def issue():
            wait_for(q, deps("dma", reads, writes))
            Q[q].dma_start(out=out, in_=in_).then_inc(T.sem[sem], 16)
            totals[sem] = 16
            note("dma", reads, writes, sem, 16, dict(known[q]))
        calls.append((q, issue, reads, writes + [("dma", 0, 1)], 0.05, lat))

    def pick(win, offs):
        return ("I", win, offs)

    near = [T.rank_of(d) for d in plan(core, T, topo)[0]]
    far = [q for q in range(N) if q != r and q not in near]
    coming = [r] + near + far

    def send(name):
        mine = [message(name, r, d)[0] for d in near + far]

        def issue():
            for call in legs(core, T, topo):
                wait_for("g", deps("g", [message(name, r, T.rank_of(d))[0] for x, d, eng in call], []))
                g.remote_dma_fused([transfer(T, topo, core, x, eng, *message(name, r, T.rank_of(d)), "%s_%d" % (name, r))
                                    for x, d, eng in call], local_sem=T.sem.loc)
                totals["loc"] = totals.get("loc", 0) + sum(len(eng) for x, d, eng in call)
        sent = [("sent", len(calls), len(calls) + 1)]
        calls.append(("g", issue, mine, [("sends", 0, 1)] + sent, SEND, 0.5))
        for q in near + far:
            got = [len(eng) if x == d else len(topo.engines(x, d)) for call in legs(T.cores[q], T, topo) for x, d, eng in call if d == core]
            land, s = message(name, q, r)[1], "%s_%d" % (name, q)
            totals[s] = got[0]
            way = [("way", len(calls), len(calls) + 1)]
            calls.append(("net", lambda: None, sent, way, 0.0, HOP * (1 if q in near else 2) * SLOW.get(name, BACK) - 0.6))
            calls.append(("net", lambda a=([land], s, got[0]): note("net", [], a[0], a[1], a[2], {}), way, [land, ("from", q, q + 1)],
                          0.0, 0.5))

    def classes(st):
        c = 8 * st + 2 * r
        return [((m * H, (m + 1) * H), ("nm", c + m, 16 * (H - 1) + c + m + 1, 16)) for m in range(2)]

    def lx(t):
        return L + CAP * (1 + t // 2)

    def to_all(q):
        return ("wide", 128 * q, 128 * q + 128)

    def to_one(q, d):
        return ("to", 224 * q + 96 - 32 * d, 224 * q + 224 - 32 * d)

    P15 = ("sc", 0, 1)
    PLW = ("plw", 0, 2)

    def constants():
        iota(("pii", 0, 2), [[0, 2]], 0, 1)
        iota(("c16", 0, 2), [[16, 2]], 0)
        ts(("pij", 0, 2), ("pii", 0, 2), 15, Op.bitwise_and)
        tt(("sc", 0, 2), ("pij", 0, 2), ("c16", 0, 2), Op.add)
        iota(("pq", 0, 1), [[0, 1]], 0, 1)
        act(("pq", 1, 2), ("pq", 0, 1), 1.0 / 32, -31.0 / 64)
        act(("pq", 2, 3), ("pq", 1, 2), 1.0, ROUND)
        for i, c in enumerate((2, 32)):
            act(("kq", i, i + 1), ("pq", 2, 3), float(c), -c * ROUND)
        iota(("cv0", 0, 2), [[8, 2]], -1024)
        act(("cv", 0, 2), ("cv0", 0, 2), 1.0, ("kq", 0, 1))
        act(("ncv", 0, 2), ("cv", 0, 2), -1.0, -1024.0)
        iota(("cb0", 0, 4), [[-128, 4]], VAL + START[0])
        act(("cb", 0, 4), ("cb0", 0, 4), 1.0, ("kq", 1, 2))
        fill(("one", 0, 128), 1.0)
        select(("idn", 0, 128), ("one", 0, 128), [[-1, 128]], Op.is_equal, 0, 1)
        select(("bdh", 0, 128), ("one", 0, 128), [[-16, 8], [0, 16]], Op.is_ge, 0, 1)
        select(("bd", 0, 128), ("bdh", 0, 128), [[16, 8], [0, 16]], Op.is_ge, 15, -1)
        fill(("to", 0, 4 * 224), 0.0)
        for q in range(N):
            select(to_all(q), ("one", 0, 128), [[0, 4], [-1, 32]], Op.is_equal, -32 * q, 1)
            select(("to", 224 * q + 96, 224 * q + 128), ("one", 0, 32), [[-1, 32]], Op.is_equal, -32 * q, 1)
        count_up("zero", 0, 512, 0, 0)
        select(("o16", 0, 224), ("zero", 0, 224), [[1, 7], [0, 32]], Op.not_equal, -3, 0, 0.0625)
        select(("c16th", 0, 128), ("zero", 0, 128), [[0, 128]], Op.is_gt, 0, 0, 0.0625)
        select(("cqh", 0, 128), ("c16th", 0, 128), [[-32, 4], [0, 32]], Op.is_ge, 0, 1)
        select(("cq", 0, 128), ("cqh", 0, 128), [[32, 4], [0, 32]], Op.is_ge, 31, -1)
        iota(("nlb", 0, L), [[-1, 2], [-16, H]], V)
        iota(("ns", 0, L), [[-1, 2], [-16, H]], V - 2 * r)
        for n in ("ns", "os", "z"):
            iota((n, L, LX), [[0, LX - L]], 0)
        for st in range(2):
            act(("nl%d" % st, 0, L), ("nlb", 0, L), 1.0, ("ncv", st, st + 1))
            for n, c in (("nl", 0), ("of", 0), ("qf", V)):
                iota((n + str(st), L, LX), [[0, LX - L]], c)
        for n in ("xo", "xm"):
            fill((n, V, V + 16), 0.0)
        fill(("hit", L, L + CAP), 1.0)
        fill(("c255", 0, LX), 255.0)
        fill(("deg", L, LX), ROUND)
        fill(("sgl", 0, 2 * LX), 1.0)
        fill(("sgl", lx(0), lx(0) + 1), 0.0)
        tc(("lims", 0, 1), ("limi", 0, 1))
        for lo in range(0, G0, 322):
            fill(("en", lo, lo + 322), -1.0)
            if RS == "g":
                iota(("rs", lo, lo + 322), [[0, 322]], -SHIFT - 16384)
            elif RS == "v":
                fill(("rs", lo, lo + 322), -SHIFT - 16384.0)
            else:
                act(("rs", lo, lo + 322), ("xo", 0, 322), 0.0, -SHIFT - 16384.0)
        count_up("jt", 0, VT, 1, 0)
        count_up("c1", 0, 768, 0, 1)
        iota(("ck", 0, 16), [[1, 16]], 0)
        ts(("qsc", 0, 16), ("ck", 0, 16), P15, Op.not_equal, -1.0, Op.mult)
        ts(("qbi", 0, 16), ("qsc", 0, 16), -1281.0, Op.mult, -1.0, Op.add)
        ts(("wsc", 0, 16), ("qsc", 0, 16), 19200.0, Op.mult, 20480.0, Op.add)
        for k in range(16):
            o = ("dk", 128 * k, 128 * k + 128)
            if k < DKV:
                ts(o, ("idn", 0, 128), ("wsc", k, k + 1), Op.mult)
            else:
                act(o, ("idn", 0, 128), ("wsc", k, k + 1))
        for n, c in (("idead", -20480.0), ("imx", -4096.0), ("ipen", -32.0), ("half", HALF / 255)):
            select((n, 0, 128), ("zero", 0, 128), [[-1, 128]], Op.not_equal, 0, 1, c)
        act(("bd8", 0, 128), ("bd", 0, 128), -4096.0 * 8192)
        act(("neg", 0, 128), ("idn", 0, 128), -1.0)
        for lo in range(0, 1024, 256):
            select(("seg", lo, lo + 256), ("zero", 0, 256), [[0, 16], [1, 16]], Op.is_equal, 0, 0, 1.0)
        count_up("kb", 0, 512, 0, 512)
        for lo in (0, 256):
            select(("kb", lo, lo + 256), ("kb", lo, lo + 256), [[0, 16], [1, 16]], Op.is_gt, 0, 0, -6.0e7)
        select(("sm", 0, 96), ("zero", 0, 96), [[0, 24], [1, 4]], Op.is_gt, 0, 0, 4096.0)
        iota(("revf", 0, 48), [[0, 24], [-16, 2]], 31)
        ts(("rev", 0, 48), ("revf", 0, 48), P15, Op.subtract)
        iota(("repi", 0, 48), [[1, 24], [0, 2]], 0)
        tc(("rep", 0, 48), ("repi", 0, 48))
        iota(("jb0", 0, 8), [[16, 8]], 0)
        ts(("ju", 16, 24), ("jb0", 0, 8), P15, Op.add)
        act(("jb", 0, 8), ("jb0", 0, 8), 1.0, P15)
        for t in range(ROUNDS - 1):
            act(("jf%d" % t, 8 * t, 8 * t + 8), ("jb", 0, 8), 1.0, float(VAL + START[t]))

    def lanes_of(st, *banks):
        n = width(message("r%d" % st, r, r)[0])
        for b in banks:
            for q in coming:
                if st:
                    next_of("hits")
                mm((b, 0, n), to_one(r, q), message("r%d" % st, q, r)[1], q == r, q == coming[-1])
        qf = ("qf%d" % st, 0, L)
        later(act, qf, (banks[0], 0, L))
        if st:
            later(act, ("limf", 0, 1), (banks[0], L, L + 1), 1.0, 2048.0 + HALF)
        else:
            act(("dead0", 0, L), (banks[0], L, 2 * L))
        tc(("qu%d" % st, 0, L), (banks[1], 0, L) if st else qf)
        for k in range(16):
            o = ("qr%d" % st, k, 16 * (L - 1) + k + 1, 16)
            if k < SHARE[st]:
                ts(o, (banks[1], 0, L) if st else qf, ("qsc", k, k + 1), Op.mult, ("qbi", k, k + 1), Op.add)
            else:
                act(o, (banks[0], 0, L) if st else qf, ("qsc", k, k + 1), ("qbi", k, k + 1))
        later(act, ("of%d" % st, 0, L), qf, -1.0, float(V))

    def sums(lo, hi, stop):
        for k in range(16):
            mm(("d0", lo, hi), ("idn", 0, 128), ("xv", 16 * lo + k, 16 * (hi - 1) + k + 1, 16), stop and k == 0, stop and k == 15)

    def hits(t):
        st, n = t % 2, lx(t)
        ts(("ok", 0, L), ("d0", 0, L), ("lima" if t else "lims", 0, 1), Op.is_le)
        if t >= 2:
            mm(("bhit", 0, L), ("ipen", 0, 128), ("dead%d" % st, 0, L), True, False)
        for lo, at, k in [(0, 0, L)] if t else [(0, 0, 40), (40, 80, 40), (80, 40, 40), (120, 120, 40)]:
            next_of("hits")
            mm(("bhit", lo, lo + k), ("bd", 0, 128), ("ok", at, at + k), t < 2, True)
            act(("deg", lo, lo + k), ("d0", at, at + k), 1.0, ROUND)
        ts(("hit", 0, L), ("bhit", 0, L), 9.0, Op.is_ge)
        scan(("cum", 0, n), ("hit", 0, n), ("c255", 0, n), Op.add, Op.min)
        for c in range(2):
            ts(("sg", c * n, (c + 1) * n), ("cum", 0, n), ("sc", c, c + 1), Op.is_le)
        scan(("sn", 0, 2 * n), ("sgl", 0, 2 * n), ("sg", 0, 2 * n), Op.mult, Op.add)
        tc(PLW, ("sn", n - 1, 2 * n, n))

    def variables(t):
        n = lx(t)
        lanes = ("sn", n - 1, 2 * n, n)
        if t:
            act(("vx", 0, 2), lanes, 16.0, ("cv", t % 2, t % 2 + 1))
            act(("vy", 2, 4), lanes, 1.0, 0.5 - H, Fn.Sign)
            act(("vy", 0, 2), ("vy", 2, 4), (1.0 - V) / 2, (1.0 - V) / 2)
        else:
            ts(("vy", 0, 2), lanes, float(H), Op.is_ge, 1.0 - V, Op.mult)
            ts(("vx", 0, 2), lanes, 16.0, Op.mult, 2.0 * r - 1024, Op.add)
        ts(slot(t, r, 0, 32), pick(("deg", 0, LX), PLW), -ROUND, Op.add, 255.0, Op.min)
        (later if t else call)(tt, slot(t, r, VARS, 2), ("vx", 0, 2), ("vy", 0, 2), Op.add)
        if t < ROUNDS - 1:
            ts(slot(t, r, COUNT, 2), ("cum", L - 2, L), float(CAP), Op.min)

    def limits(t):
        for d in coming:
            w = ("cq", 0, 128) if t else ("o16", 96 - 32 * d, 224 - 32 * d)
            mm(("bkey", 0, 1), w, slot(t, d, COUNT + 1, 1), d == r, d == coming[-1])
        act(("am", 0, 1), ("bkey", 0, 1))
        act(("am", 1, 2), ("am", 0, 1), 0.125, -0.4375)
        act(("am", 2, 3), ("am", 1, 2), 1.0, ROUND)
        act(("am", 3, 4), ("am", 2, 3), -8.0, 8 * ROUND)
        act(("am", 4, 5), ("am", 3, 4), 1.0, ("am", 0, 1))
        act(("lima", 0, 1), ("am", 4, 5), 1.0, ("limf", 0, 1))

    def pivot_lanes(t):
        if t == 0:
            ts(("piv", 0, L), ("cum", 0, L), float(CAP), Op.is_le, 2.0, Op.mult)
            tt(("r0", 2 * L * r + L, 2 * L * (r + 1)), ("piv", 0, L), ("hit", 0, L), Op.mult)
        else:
            mm(("bkey", 0, L), ("idn", 0, 128), ("cum", 0, L), True, False)
            for k in range(2):
                mm(("bkey", 0, L), ("ipen", 0, 128), ("hit", 0, L), False, k == 1)
            act(("dead1", 0, L), ("bkey", 0, L), -2.0, -62.0, Fn.Relu)

    def put(table, lists, lo, hi, src):
        tc(pick((table, 0, VT), (lists, lo // 16, hi // 16)), src)

    def own(table, lo, hi):
        put(table, "evo", lo, hi, ("nt" if table == "nm" else "xt", lo, hi))

    def main(t):
        st = t % 2
        qu, qn = LISTS[t]

        def cover(c):
            lo, hi = CH[c]
            bank = ("b%d" % c, 0, hi - lo)
            next_of("covers")
            tt(("eq", 16 * lo, 16 * hi), pick(("en", 0, G0), (qu, lo, hi)), ("qr%d" % st, 16 * lo, 16 * hi), Op.is_equal)
            mm(bank, ("idead", 0, 128), ("one", 0, hi - lo), True, False)
            if t >= 2:
                mm(bank, ("idead", 0, 128), ("dead%d" % st, lo, hi), False, False)
            for k in range(16):
                if k == 15 and hi == L:
                    next_of("sums")
                mm(bank, ("dk", 128 * k, 128 * k + 128), ("eq", 16 * lo + k, 16 * (hi - 1) + k + 1, 16), False, k == 15)

        def uncovered(c):
            lo, hi = CH[c]
            bank = ("b%d" % c, 0, hi - lo)
            tt(("q2", lo, hi), ("qf%d" % st, lo, hi), bank, Op.max)
            ts((qn, lo, hi), ("q2", lo, hi), float(V), Op.min)
            later(act, ("z", lo, hi), bank, 1.0, 0.0, Fn.Abs)
            for f, a, z in ((act, lo, hi - PART[c]), (tc, hi - PART[c], hi)):
                if a < z:
                    if f is act:
                        next_of("picks")
                    f(("xv", 16 * a, 16 * z), pick(("xm", 0, G0), (qn, a, z)))

        def degrees(c):
            lo, hi = CH[c]
            scan(("msc", 16 * lo, 16 * hi), ("seg", 0, 16 * (hi - lo)), ("xv", 16 * lo, 16 * hi), Op.mult, Op.min)
            next_of("sums")
            sums(lo, hi, False)

        cover(0)
        for c in range(len(CH)):
            if c + 1 < len(CH):
                cover(c + 1)
            else:
                for a, z in KEYS[t]:
                    (later if a else call)(tt, pick(("rs", 0, VT), ("evu", a // 16, z // 16)), ("idr", a, z), ("bk", a, z), Op.add)
            uncovered(c)
        mm(("d0", 0, L), ("half", 0, 128), ("c255", 0, L), True, False)
        for c in range(len(CH)):
            degrees(c)
        mm(("d0", 0, L), ("imx", 0, 128), ("msc", 15, 16 * L, 16), False, True)

    def pivots(t):
        st, n = t % 2, 256 * t
        nl = ("nl%d" % st, 0, LX)
        tc(("qp", 0, 32), pick(("qf%d" % st, 0, LX), PLW))
        for f, a, z in ((act, 0, KEYV[t]), (tc, KEYV[t], 32)):
            if a < z:
                f(("key", 16 * a, 16 * z), pick(("rs", 0, G0), ("qp", a, z)))
        act(("zp", 0, 32), pick(("z", 0, LX), PLW), -1.0)
        buf, v0, v1 = slot(t, r, FREE, 32) if t == ROUNDS - 1 else ("vh", 0, 32)
        tc((buf, v0, v1), pick(nl, PLW))
        tt(("xn", 512, 544), pick(("of%d" % st, 0, LX), PLW), ("zp", 0, 32), Op.add)
        for bank, a in (("b1", 0), ("b2", 16)):
            act(("xn", 16 * a, 16 * a + 256), pick(("en", 0, G0), ("qp", a, a + 16)))
            mm((bank, 0, 288), ("idn", 0, 128), ("zero", 0, 288), True, False)
            for k in range(16):
                mm((bank, k, 256, 16), ("idn", 0, 128), (buf, v0 + a, v0 + a + 16), False, False)
            if a:
                mm((bank, 256, 288), ("idn", 0, 128), (buf, v0, v1), False, False)
            mm((bank, 0, 256 + 2 * a), ("neg", 0, 128), ("xn", 16 * a, 18 * a + 256), False, True, 4 * PE)
            act(("b0", 16 * a, 18 * a + 256), (bank, 0, 256 + 2 * a), 2048.0, 0.0, Fn.Abs)
        variables(t)
        scan(("ksc", 0, 512), ("kb", 0, 512), ("key", 0, 512), Op.add, Op.max)
        tc(("mi", 0, 32), ("ksc", 15, 512, 16))
        if t == ROUNDS - 1:
            send("s3")
        ts(("mj", 0, 32), ("mi", 0, 32), 511, Op.bitwise_and)
        later(act, ("rho", 0, n), pick(("jf%d" % (t - 1), 0, 8 * t), ("rep", 0, 16 * t)), 1.0, float(-VAL - ID0))
        later(act, ("c1", 31, n, 32), ("c1", 0, 8 * t), ("cb", t, t + 1))
        tt(("ne", 0, n), pick(("mj", 0, 32), ("rev", 0, 16 * t)), ("rho", 0, n), Op.not_equal)
        scan(("fc", 0, n), ("ne", 0, n), ("c1", 0, n), Op.mult, Op.add, float(VAL))
        tt(slot(t, r, CLAIMS[t], 8 * t), ("fc", 31, n, 32), ("jf%d" % (t - 1), 0, 8 * t), Op.min)
        if t == ROUNDS - 1:
            send("c3")
        tt(("cc", 0, 544), ("xn", 0, 544), ("b0", 0, 544), Op.min)
        if t < ROUNDS - 1:
            roots(t)
        scan(("nsc", 0, 512), ("seg", 0, 512), ("cc", 0, 512), Op.mult, Op.max)
        tt(slot(t, r, NAMES[t], 32), ("cc", 512, 544), ("nsc", 15, 512, 16), Op.max)

    def least(t, bank):
        scan(("jm", 0, 32 * t), ("sm", 0, 32 * t), (bank, 16, 16 + 32 * t), Op.add, Op.min)
        ts(("ju", 16 - 8 * t, 16) if t < 3 else ("ju3", 0, 24), ("jm", 3, 32 * t, 4), float(-VAL - START[t]), Op.add)

    def spread(t, part, k, out):
        for q in coming if t == 0 else range(N):
            mm(out(q), to_all(q if t else r), slot(t, r if t else q, part, k))

    def roots(t):
        n, new = 128 * (t + 1), ("la", START[t], START[t] + 128)
        spread(t, 0, 32, lambda q: ("d0", 32 * q, 32 * q + 32))
        bank = "bkey" if t else "bhit"
        later(spread, t, VARS, 2, lambda q: (bank, 2 * q, 2 * q + 2))
        later(ts, ("evu", 8 * t, 8 * t + 8), (bank, 0, 8), 1024.0, Op.add)
        later(act, ("xr", n - 128, n), ("d0", 0, 128), -1.0 / 4096)
        later(act, new, ("d0", 0, 128))
        for lo in (n - 128, n - 64):
            later(put, "xm", "evu", lo, lo + 64, ("xr", lo, lo + 64))
        if t:
            spread(t, CLAIMS[t], 8 * t, lambda q: ("bhit", 16 + q, 16 + 32 * t, 4))
            least(t, "bhit")
            act(("xr", 0, n - 128), pick(("la", START[t], 512), ("ju", 16 - 8 * t, 16)), -1.0 / 4096)
            later(act, ("jf%d" % t, 0, 8 * t), ("jm", 3, 32 * t, 4))

    def update(t):
        n, new = 128 * (t + 1), ("ln", START[t], START[t] + 128)
        ju = ("ju", 16 - 8 * t, 24)
        xr = ("xr", 0, n)
        spread(t, NAMES[t], 32, lambda q: ("b2", 32 * q, 32 * q + 32))
        if t:
            act(new, ("b2", 0, 128))
            next_of("roots")
            act(("er", 0, n - 128), pick(("ln", START[t], 512), ("ju", 16 - 8 * t, 16)))
            put("xm", "evu", 0, n - 128, ("xr", 0, n - 128))
            put("en", "evu", n - 128, n, new)
            put("en", "evu", 0, n - 128, ("er", 0, n - 128))
        else:
            act(new, ("b2", 0, 128))
            roots(0)
            put("en", "evu", 0, n, new)
        mm(("bkey", 0, n), ("bd8", 0, 128), xr)
        next_of("roots")
        act(("bk", 0, n), ("bkey", 0, n))
        next_of("roots")
        act(("idr", 0, n), pick(("jt", START[t], 512), ju), 1.0, float(-ID0 - SHIFT))

    def collect(t, bank, n, pieces):
        if t == ROUNDS - 1:
            mm((bank, 0, n), ("idn", 0, 128), ("zero", 0, n), True, False)
        for d in coming if t == ROUNDS - 1 else [None]:
            for part, k, out in pieces:
                for q in range(N):
                    if t == 0:
                        mm((bank,) + out(q), ("idn", 0, 128), slot(t, q, part, k))
                    elif d is None:
                        for e in range(N):
                            mm((bank,) + out(q), to_one(q, e), slot(t, e, part, k), e == 0, e == N - 1)
                    else:
                        if (d, q) == ((r, 0) if part == NAMES[t] else (coming[-1], N - 1)):
                            next_of("last")
                        mm((bank,) + out(q), to_one(q, d), slot(t, d, part, k), False, (d, part, q) == (coming[-1], pieces[-1][0], N - 1))

    def by32(q):
        return (32 * q, 32 * q + 32)

    def outputs(t):
        collect(t, "bhit", 8, [(VARS, 2, lambda q: (2 * q, 2 * q + 2))])
        ts(("evo", 8 * t, 8 * t + 8), ("bhit", 0, 8), 1024.0, Op.add)
        collect(t, "d0", 128, [(0, 32, by32)])
        act(("xt", 128 * t, 128 * t + 128), ("d0", 0, 128))
        collect(t, "b2", 128, [(NAMES[t], 32, by32)])
        act(("nt", 128 * t, 128 * t + 128), ("b2", 0, 128), -1.0, float(V))
        act(("vid", START[t], START[t] + 128), pick(("jt", 0, VT), ("evo", 8 * t, 8 * t + 8)))

    def kept_rows(t):
        for d in range(N):
            mm(("bkey", 0, L), to_one(r, d), message("k%d" % t, d, r)[1], d == 0, d == N - 1)
        for (lo, hi), x in classes(t % 2):
            act(x, ("bkey", lo, hi))

    for q, d in zip("yss", far + near):
        dma(q, T["sx"][:, 320 * d:320 * d + 320], T.xs[32 * d:32 * d + 32, :], "ds_%d" % d, [], [message("x", r, d)[0]], 1.8)
    dma("y", T["limi"][:, 0:1], T.lim[:, 0:1], "dl", [], [("limi", 0, 1)], 2.0)
    dma("y", T["nm"][:, 0:V // 2], T.nb[:, 0:V // 2], "dn", [], [("nm", 0, V // 2)], 2.7)
    dma("y", T["xo"][:, 0:V], T.xs[:, :], "do", [], [("xo", 0, V)], 3.5)
    dma("y", T["nm"][:, V // 2:V], T.nb[:, V // 2:V], "dm", [], [("nm", V // 2, V)], 4.3)
    dma("y", T["xm"][32 * r:32 * r + 32, 0:V], T.xs[32 * r:32 * r + 32, :], "dx_%d" % r, [("nm", 0, V)], [("xm", r, V, N)], 6.0)
    send("x")
    later(constants)
    for q in near + far:
        dma("y", T["xm"][32 * q:32 * q + 32, 0:V], T["lx"][:, 320 * q:320 * q + 320], "dx_%d" % q, [message("x", q, r)[1]], [("xm", q, V, N)], 1.5)

    for half in range(2):
        for m, f in enumerate((act, tc)):
            at, c = H * half + H // 2 * m, V // 2 * half + 2 * r + m
            tc(("qs", at, at + H // 2), ("nm", c, c + V // 2 - 15, 16))
            f(("xv", 16 * at, 16 * at + V // 2), pick(("xo", 0, G0), ("qs", at, at + H // 2)))
        sums(H * half, H * half + H, True)
    for (lo, hi), x in classes(1):
        tc(("r1", 168 * r + lo, 168 * r + hi), x)
    ts(("r1", 168 * r + L, 168 * r + L + 1), ("limi", 0, 1), -2048.0, Op.add)
    send("r1")
    for (lo, hi), x in classes(0):
        later(act, ("os", lo, hi), x, -1.0, float(V))
    hits(0)
    variables(0)
    act(("zp", 0, 32), pick(("ns", 0, LX), PLW))
    tt(("vr", 0, 32), pick(("os", 0, LX), PLW), ("zp", 0, 32), Op.not_equal)
    tt(slot(0, r, NAMES[0], 32), pick(("os", 0, LX), PLW), ("vr", 0, 32), Op.mult)
    send("a0")
    for (lo, hi), x in classes(0):
        tc(("r0", 2 * L * r + lo, 2 * L * r + hi), x)
    pivot_lanes(0)
    send("r0")
    lanes_of(1, "bkey", "b1")
    update(0)
    later(limits, 0)
    later(lanes_of, 0, "bkey")

    for t in range(1, ROUNDS):
        if t == 3:
            later(kept_rows, 2)
        main(t)
        if t >= 2:
            ts(message("k%d" % t, r, r)[0], ("q2", 0, L), float(V), Op.min)
            send("k%d" % t)
        hits(t)
        later(outputs, t - 1)
        if t == 3:
            later(kept_rows, 3)
        pivots(t)
        if t == 1:
            later(act, ("of1", 0, L), ("q2", 0, L), -1.0, float(V), Fn.Relu)
            later(act, ("qf1", 0, L), ("of1", 0, L), -1.0, float(V))
            later(pivot_lanes, 1)
            for x, c in ((("hit", L, L + CAP), 0), (("hit", L + CAP, LX), 1), (("sgl", lx(0), lx(0) + 1), 1), (("sgl", LX, LX + 1), 0)):
                later(iota, x, [[0, width(x)]], c)
        if t < ROUNDS - 1:
            later(send, "a%d" % t)
            update(t)
            later(limits, t)

    send("n3")
    collect(3, "d0", 128, [(0, 32, by32)])
    collect(3, "bkey", 8, [(VARS, 2, lambda q: (2 * q, 2 * q + 2))])
    collect(3, "b1", 128, [(FREE, 32, by32)])
    act(("xt", 384, 512), ("d0", 0, 128))
    act(("vid", 0, 128), ("b1", 0, 128), -1.0, float(V))
    ts(("evo", 24, 32), ("bkey", 0, 8), 1024.0, Op.add)
    own("nm", 0, 384)
    own("xo", 0, 256)
    collect(3, "bhit", 112, [(CLAIMS[3], 24, lambda q: (16 + q, 112, 4))])
    collect(3, "b2", 128, [(NAMES[3], 32, by32)])
    least(3, "bhit")
    own("xo", 256, 512)
    dma("y", T.yx[:, :], T["xo"][:, 0:V], "ox", [("xo", 0, V)], [], 2.2)
    act(("jv", 0, 256), pick(("vid", 0, 512), ("ju3", 0, 16)))
    act(("nt", 384, 512), ("b2", 0, 128), -1.0, float(V))
    act(("jv", 256, 384), pick(("vid", 0, 512), ("ju3", 16, 24)))
    put("jt", "evo", 0, 256, ("jv", 0, 256))
    own("nm", 384, 512)
    dma("y", T.yn[:, :], T["nm"][:, 0:V], "on", [("nm", 0, V)], [], 2.8)
    put("jt", "evo", 256, 384, ("jv", 256, 384))
    dma("s", T.yj[:, :], T["jt"][0:128:16, 0:V], "oj", [("jt", 0, V)], [], 2.0)
    in_order()
    for s, v in totals.items():
        if known["g"].get(s, 0) < v:
            g.wait_ge(T.sem[s], v)
